import numpy as np, ml_dtypes
CORES = [5,29,101,125,133,157,229,253]
N = 8
import mx_ref
BF = ml_dtypes.bfloat16
def gentries(a):
    return np.ascontiguousarray(a.reshape(8, 16, -1).transpose(0, 2, 1)).reshape(8, -1)
def gtable(e):
    e = np.asarray(e); return np.ascontiguousarray(e.reshape(8, -1, 16).transpose(0, 2, 1)).reshape(128, -1).astype(np.int32)
def gcols(t, e):
    v = np.concatenate([t.reshape(8, 16, -1, 4), np.zeros((8, 16, 1, 4), BF)], axis=2)
    return np.ascontiguousarray(np.stack([v[g][:, e[g]] for g in range(8)])).reshape(128, -1)
def tile(rs):
    return np.stack(rs, axis=2).reshape(128, -1).astype(BF)
def pick(q, e):
    c = np.concatenate([q[0].reshape(128, -1, 4), np.zeros((128, 1, 4), np.uint8)], axis=1); s = np.concatenate([q[1], np.ones((16, 1), np.uint8)], axis=1)
    return (np.ascontiguousarray(c[:, e].reshape(128, -1)), np.ascontiguousarray(s[:, e]))
def join(*qs):
    return (np.concatenate([q[0] for q in qs], axis=1), np.concatenate([q[1] for q in qs], axis=1))
def put(q, e, v):
    c, s = q[0].reshape(128, -1, 4).copy(), q[1].copy(); c[:, e] = v[0].reshape(128, -1, 4); s[:, e] = v[1]
    return (c.reshape(128, -1), s)
def pk(c, s):
    return (np.ascontiguousarray(c), mx_ref.live(s))
def emit(q):
    return q[0], q[1]
def packed(v, rng):
    q = [mx_ref.quantize(np.ascontiguousarray(v[r])) for r in range(N)]
    return np.stack([a for a, b in q]), np.stack([mx_ref.plane(b, rng) for a, b in q])
def values_of_codes():
    e, c = np.zeros((128, 128, 4), np.float32), np.zeros((128, 2, 4), np.uint8)
    e[np.arange(128), np.arange(128), 0] = 1
    c[:127, :, 0] = np.arange(256).reshape(2, 128).T[:127]
    return mx_ref.matmul(mx_ref.quantize(e.reshape(128, 512).astype(BF)), (c.reshape(128, 8), np.full((16, 2), 127, np.uint8))).T.reshape(-1).astype(np.float64)
CODE_VALUE, SCALE_VALUE = values_of_codes(), 2.0 ** (np.arange(256) - 127.0)
def decode(q):
    return (CODE_VALUE[q[0]].reshape(16, 8, -1, 4) * SCALE_VALUE[q[1]][:, None, :, None] + 0.0).reshape(128, -1).astype(np.float32)
def f(rng, *shape):
    return mx_ref.flush((rng.standard_normal(shape, dtype=np.float32) * np.exp2(rng.integers(-2, 3, shape[:-1] + (1,)))).astype(BF))
def wide(rng, *shape, cols=0):
    v = rng.standard_normal(shape, dtype=np.float32) * np.exp2(rng.integers(-12, 13, shape)).astype(np.float32)
    if cols: v *= np.repeat(np.exp2(rng.integers(-cols, cols + 1, shape[:-2] + (1, shape[-1] // 4))) * (rng.random(shape[:-2] + (1, shape[-1] // 4)) > 0.0625), 4, axis=-1).astype(np.float32)
    return mx_ref.flush(v.astype(BF))
C, T = 384, 160
STEPS = [1, 2, 4]
def big(v):
    v = v.astype(np.float32)
    v[np.abs(v) < np.float32(2.0 ** -16)] = 0
    return v.astype(BF)
def numbers_of(rng):
    return {"x": big(f(rng, N, 128, 4 * C)), "u": np.array(f(rng, N, 128, 512)), "v": np.array(f(rng, N, 128, 512))}
def lists(rng, a=None):
    if a is None: a = np.argsort(rng.random((N, 8, C // 8, 8)), axis=3)
    a = (a + 8 * np.arange(C // 8)[:, None]).reshape(N, 8, C)
    c = np.argsort(rng.random((N, 8, C)), axis=2)
    return {"p": np.stack([gtable(a[r]) for r in range(N)]), "h": np.stack([gtable(c[r]) for r in range(N)])}
def weights(rng, w):
    c, s = packed(np.ascontiguousarray(w).reshape(N, 128, 2048), rng)
    return {"wc": c, "ws": s}
def layers(rng, still=[]):
    w = big(f(rng, N, 128, 2048)).reshape(N, 8, 16, 4, 8, 16, 4)
    for i in still:
        w[:, :, i] = 0
        w[:, :, :, :, :, i] = 0
    return weights(rng, w)
def setup_inputs(rng):
    return {**numbers_of(rng), **lists(rng), **layers(rng)}
def setup_inputs_ties(rng):
    d = numbers_of(rng)
    x = d["x"].astype(np.float32).reshape(N, 8, 16, C, 4)
    x[:, :, 0] = 0
    x[:, :, 0, :, 0] = rng.integers(-2, 3, (N, 8, C))
    z = np.exp2(rng.integers(-14, -7, (N, 8, C, 32))) * (1 + (2 * rng.integers(0, 64, (N, 8, C, 32)) + 1) / 128) * rng.choice([-1.0, 1.0], (N, 8, C, 32))
    np.put_along_axis(z, rng.integers(0, 32, (N, 8, C, 1)), 1.96875 * rng.choice([-1.0, 1.0], (N, 8, C, 1)), axis=3)
    z = z * np.exp2(rng.integers(-2, 3, (N, 8, C, 1)))
    x[:, :, 8:] = z.reshape(N, 8, C, 8, 4).transpose(0, 1, 3, 2, 4)
    u = d["u"].reshape(N, 128, 128, 4)
    u[:, :, ::16] = 0
    o = rng.permutation(N)
    for r in range(N):
        for i in range(0, 128, 16): u[r, i, i, 0] = 0.0 if r == o[0] else -1.0 if r == o[1] else 1.0
    return {"x": x.reshape(N, 128, 4 * C).astype(BF), "u": u.reshape(N, 128, 512), "v": d["v"], **lists(rng), **layers(rng, [0, 8, 9, 10, 11, 12, 13, 14, 15])}
def setup_inputs_near(rng):
    d = numbers_of(rng)
    x = d["x"].astype(np.float32).reshape(N, 8, 16, C, 4)
    u = d["u"].reshape(N, 128, 128, 4)
    x[:, :, 0] = 0
    x[:, :, 8:] = 0
    u[:, :, ::16] = 0
    s = rng.integers(0, 16, (N, 8, C))
    k = rng.permutation(8) % 4
    for g in range(8):
        i = 16 * g
        if k[g] < 2:
            x[:, g, 0, :, 0] = 1
            x[:, g, 8] = ((s[:, g, :, None] >> np.arange(4)) & 1) * np.exp2(np.arange(4) - 23.0)
            x[:, g, 11, :, 0] = 2.0 ** -10
            c = 1.0 if k[g] == 0 else -2.0 ** -30
            u[:, i, i, 0] = c
            u[:, i + 8, i] = c
            u[:, i + 11, i, 0] = c
        else:
            x[:, g, 10, :, 0] = (1 + s[:, g] % 8 * 0.125) * 2.0 ** -30
            u[:, i + 10, i, 0] = 2.0 ** -30 if k[g] == 2 else -2.0 ** -30
            if k[g] == 3: x[np.arange(N), g, 10, rng.integers(0, C, N), 0] = 2.0 ** 30
    return {"x": x.reshape(N, 128, 4 * C).astype(BF), "u": u.reshape(N, 128, 512), "v": d["v"], **lists(rng), **layers(rng, [0, 8, 9, 10, 11, 12, 13, 14, 15])}
def setup_inputs_huge(rng):
    d = numbers_of(rng)
    o = rng.permutation(N)
    x = 0.6 + 0.4 * rng.random((N, 8, 16, C, 4))
    x[o == 0] = 0.875 + 0.25 * (x[o == 0] - 0.5)
    c = rng.choice([-1.0, 1.0], (N, 1, 1, C, 1))
    c[o % 2 == 0] = -1
    u = d["u"].reshape(N, 128, 128, 4)
    a = 1 - 0.1 * rng.random((N, 128, 8, 4))
    a[o == 0] = 1
    a = 2.0 ** 30 * a * (rng.permutation(8) % 2 * 2.0 - 1.0)[:, None]
    u[:, :, ::16] = a.astype(np.float32).astype(BF)
    w = np.zeros((N, 128, 4, 128, 4), np.float32)
    i = np.arange(128)
    for b in range(4): w[:, i, b, i, b] = -1
    return {"x": (2.0 ** 30 * x * c).astype(np.float32).reshape(N, 128, 4 * C).astype(BF), "u": u.reshape(N, 128, 512), "v": d["v"], **lists(rng), **weights(rng, w.astype(BF))}
def setup_inputs_caps(rng):
    d = numbers_of(rng)
    u = d["u"].reshape(N, 128, 128, 4)
    u[:, :, ::16] = 0
    n, t = C // 8, T // 8
    back = {8: [[1], [6, 7]], 4: [[1, 2], [0, 2, 3]]}[N]
    size = rng.permutation(np.array([[t, t], [t, t], [t + 1, t - 1], [t - 1, t + 1], [n, 0], [0, n], [t, n - t], [n - t, t]]))
    a = np.zeros((N, 8, n, 8), int) + np.arange(8)
    for g in range(8):
        o = rng.permutation(n)
        i, j = int(size[g, 0]), int(size[g, 0] + size[g, 1])
        for r in back[0]: a[r, g, o[:i]] = np.arange(7, -1, -1)
        for r in back[1]: a[r, g, o[i:j]] = np.arange(7, -1, -1)
        for r in range(N): a[r, g, o[j:]] = np.array([7, 5, 6, 3, 4, 1, 2, 0] if r % 2 else [1, 0, 3, 2, 5, 4, 7, 6])
    return {"x": d["x"], "u": u.reshape(N, 128, 512), "v": d["v"], **lists(rng, a), **layers(rng)}
def setup_inputs_spread(rng):
    d = setup_inputs(rng)
    d["x"] = big(wide(rng, N, 128, 4 * C, cols=6))
    return d
def check_inputs(d):
    b = []
    for k in ("x", "u", "v"):
        a = np.abs(d[k].astype(np.float32))
        if not (np.isfinite(a).all() and ((a == 0) | (a >= 2.0 ** -30) & (a <= 2.0 ** 30)).all()): b.append("a value of " + k)
    none, least, most = [emit(mx_ref.quantize(np.full((128, 16), k, np.float32).astype(BF)))[1][0, 0] for k in (0.0, 2.0 ** -30, 2.0 ** 30)]
    for r in range(N):
        if (np.sort(gentries(d["p"][r]).reshape(8, -1, 8), axis=2).reshape(8, C) != np.arange(C)).any(): b.append("p: a block that doesn't hold its letters")
        if (np.sort(gentries(d["h"][r]), axis=1) != np.arange(C)).any(): b.append("h: a group that doesn't name every column once")
        if ((d["wc"][r] == 0x7F) | (d["wc"][r] == 0xFF)).any(): b.append("wc: a code that is no number")
        s = mx_ref.live(d["ws"][r])
        if ((s != none) & ((s < least) | (s > most))).any(): b.append("ws: a scale out of range")
    return b
def meet(a, b):
    a, b = a.reshape(8, -1, 8), np.argsort(b.reshape(8, -1, 8), axis=2)
    up = np.arange(8)[:, None] < np.arange(8)
    k = up & ((a[:, :, :, None] > a[:, :, None, :]) | (b[:, :, :, None] < b[:, :, None, :]))
    for i in range(8): k = k | (k[:, :, :, i:i + 1] & k[:, :, i:i + 1, :])
    return (np.sum(k, axis=2) + np.sum(up & ~k, axis=3)).reshape(8, C) + np.arange(C) // 8 * 8
def reference(x, u, v, p, h, wc, ws):
    qu = [mx_ref.quantize(u[r]) for r in range(N)]
    lay = [pk(wc[r], ws[r]) for r in range(N)]
    now = [x[r] for r in range(N)]
    word = [gentries(p[r]) for r in range(N)]
    home = [gentries(h[r]) for r in range(N)]
    for step in STEPS:
        for r in range(N):
            s = mx_ref.matmul(qu[r], mx_ref.quantize(now[r]))[::16] + np.float32(0.0)
            s = np.take_along_axis(s, np.take_along_axis(home[r], word[r], axis=1), axis=1).reshape(8, -1, 2)
            a = word[r].reshape(8, -1, 2)
            word[r] = np.where(s[:, :, :1] < s[:, :, 1:], a[:, :, ::-1], a).reshape(8, C)
        m = [None] * N
        for r in range(N):
            e = r ^ step
            if r < e:
                pos = meet(word[r], word[e])
                m[r] = m[e] = np.argsort(pos, axis=1)
                word[r], word[e] = np.take_along_axis(word[r], m[r], axis=1), np.take_along_axis(pos, word[e], axis=1)
        made, slot, sent = [], [], []
        for r in range(N):
            z = gcols(now[r], np.take_along_axis(home[r], word[r], axis=1))
            q = mx_ref.quantize(z)
            made.append(tile([mx_ref.matmul(pick(lay[r], np.arange(128 * b, 128 * b + 128)), q) * np.float32(0.03125) + z[:, b::4].astype(np.float32) for b in range(4)]))
            moved = m[r] != np.arange(C)
            o = np.argsort(~moved, axis=1, kind="stable")[:, :T]
            e = np.where(np.take_along_axis(moved, o, axis=1), o, -1)
            k = np.full((8, C + 1), -1)
            np.put_along_axis(k, np.where(e < 0, C, e), np.zeros((8, 1), int) + np.arange(T), axis=1)
            slot.append(k[:, :C])
            sent.append(mx_ref.quantize(gcols(made[r], e)))
        for r in range(N):
            came = gcols(decode(sent[r ^ step]).astype(BF), slot[r]).astype(np.float32)
            own = made[r].astype(np.float32)
            met = np.repeat(np.repeat(slot[r] >= 0, 16, axis=0), 4, axis=1)
            now[r] = np.where(met, (own + came) * np.float32(0.5), own).astype(BF)
    y, op = np.zeros((N, 128, C), np.float32), np.zeros((N, 8, C), np.float32)
    oc, osc = np.zeros((N, 128, 4 * C), np.uint8), np.zeros((N, 16, C), np.uint8)
    for r in range(N):
        q = mx_ref.quantize(now[r])
        y[r] = mx_ref.matmul(mx_ref.quantize(v[r]), q)
        op[r] = word[r]
        oc[r], osc[r] = emit(q)
    return {"y": y, "op": op, "oc": oc, "osc": osc}

@@ -1,0 +1,667 @@
+from concourse.bass import DstId, RemoteDMATransfer
+from concourse.mybir import dt, AluOpType, ActivationFunctionType
+
+C, TS, NR = 384, 160, 3
+H = C // 2
+YW = C + TS
+BIG = 1.0e29
+BF, F32, I32, U16, Q4, U8 = "bfloat16", "float32", "int32", "uint16", "float8_e4m3fn_x4", "uint8"
+
+SCRATCH = {}
+PLACE = {}
+
+
+def _decl(kind, names, into=None):
+    at = 0
+    for item in names.split():
+        name, n = item.split(":")
+        PLACE[name] = (into or name, at, int(n), kind)
+        if into:
+            at += (int(n) + 31) // 32 * 32
+        SCRATCH[into or name] = ("sbuf", [128, at or int(n)], kind)
+
+
+_decl(BF, "x0:1536 xs:1536 ut:512 vt:512 et:2048 xh:1536 z:1536 z32:1536 ym:2176 f:640 f16:640 "
+          "qt0:32 qt1:32 qt2:32 pw0:32 pw1:32 pw2:32 rw:32 ft:32 ft0:32 pq:32 ev:32 ed:32 ev0:32 ed0:32 pev:32 ped:32 rev:32 red:32 "
+          "t32:32 oa:192 ob:192 own:192 pu:192 lead:192 lcx:256 rxx:256 "
+          "rw2:320 t5:256 tt:256 t7:256 t9:256 pos:256 nm:256 fl:192 fsn:256 mkb:192 idn:128")
+_decl(F32, "irl:384 hrl:384 hw:384 ext:384 exs:384 s:384 sb:192 maskl:192 maskr:192 col:48 "
+           "wl:32 wt:32 vl:32 iv:256 ag:40 adf:32 dex:256 t11:256 nw:256 mv:32 pp:32 tp:64 tpt:64 "
+           "base:24 d0:48 d1:48 mm:48 ew:544 esn:160 yo:384")
+_decl(BF, "j16:384 dm:384 k16:384 k8:256 k4:256 ones:384 b8:192 kl:256 nk:256 kk:256 gij:256 sgn:256 k2:32 fone:192", "cb")
+_decl(F32, "kg:256 kb:256 cp:160 c16:24 cmin:32 k1000:24 cbig:160 pa:160", "cf")
+_decl(I32, "pin:24 hin:24 pidx:1 coli:8 qi:32 par:32 pl:24 pb:24")
+_decl(U16, "lst:180 w16:24 h16:24 xh16:96 lab:24 idx:24 e16:10 tot:2")
+_decl(Q4, "wq:512 uq:128 uq2:128 vq:128 xq:384 zq:384 eq:512 fq0:160 fq1:160 fq2:160 lq0:160 lq1:160 lq2:160 rq:160")
+_decl(U8, "wsc:512 us:128 us2:128 vs:128 xsc:384 zs:384 es:512 fs0:160 fs1:160 fs2:160 ls0:160 ls1:160 ls2:160 rsc:160")
+SCRATCH["ps"] = ("psum", [128, 4096], F32)
+PLACE["ps"] = ("ps", 0, 4096, F32)
+
+POOL = {"v": 40, "a": 24, "t": 12, "g": 16, "dma": 10}
+SEMAPHORES = (["%s%d" % (e, i) for e in POOL for i in range(POOL[e])]
+              + ["ae0", "aw0", "aw1", "aw2", "af0", "af1", "af2", "rea", "rda", "rwa", "rqa", "rsa", "sent", "outs"])
+
+A = AluOpType
+ACT = ActivationFunctionType
+
+L_PL, L_EI, L_EC, L_UP, L_U, L_V, L_LCX, L_RI, L_TI, L_RX, L_PI, L_EI8 = 0, 24, 40, 52, 60, 72, 84, 100, 116, 132, 148, 164
+
+KINDS = {"e": ("ev%d", "pev", "ae%d", "rev", "rea"), "d": ("ed%d", "ped", "ae%d", "red", "rda"),
+         "w": ("qt%d", "pw%d", "aw%d", "rw", "rwa"),
+         "q": ("fq%d", "lq%d", "af%d", "rq", "rqa"), "s": ("fs%d", "ls%d", "af%d", "rsc", "rsa")}
+SECOND = "ds"
+
+
+def names_of(kind, rnd):
+    return [n % rnd if "%" in n else n for n in KINDS[kind]]
+
+
+def partner_of(T, rank, rnd):
+    return T.cores[rank ^ (1 << rnd)]
+
+
+def relay_of(topo, src, dst, kind):
+    if topo.may_write(src, dst):
+        return None
+    near = [c for c in topo.cores_of(src) if topo.may_write(c, dst)]
+    near = [c for c in near if topo.die(c) == topo.die(src)] or near
+    return near[-1] if kind in SECOND else near[0]
+
+
+def engines_in(mask):
+    return bin(mask).count("1")
+
+
+def first_hop(topo, src, dst, kind):
+    hop = relay_of(topo, src, dst, kind)
+    if hop is None:
+        return dst, topo.mask(src, dst)
+    far = topo.mask(hop, dst)
+    rest = topo.mask(src, hop) & ~far
+    return hop, rest if kind in SECOND and engines_in(rest) == engines_in(far) else far
+
+
+def whole(T, name):
+    return T[name][:].bitcast(dt.uint8) if SCRATCH[name][2] == Q4 else T[name][:]
+
+
+def send(g, T, topo, src, dst, land, name, sem, mask):
+    rid, pid = topo.addr(dst, src)
+    g.remote_dma(whole(T, land), whole(T, name), T.sem[sem], T.sem["sent"], pid, rid, mask)
+
+
+def relay_program(g, core, T, topo):
+    total = 0
+    for rank, src in enumerate(T.cores):
+        for rnd in range(NR):
+            dst = partner_of(T, rank, rnd)
+            for kind in "edwqs" if rnd == 0 else "wqs":
+                if relay_of(topo, src, dst, kind) == core:
+                    _, land, sem, here, came = names_of(kind, rnd)
+                    g.wait_ge(T.sem[came], engines_in(first_hop(topo, src, dst, kind)[1]))
+                    send(g, T, topo, core, dst, land, here, sem, topo.mask(core, dst))
+                    total += engines_in(topo.mask(core, dst))
+    if total:
+        g.wait_ge(T.sem["sent"], total)
+
+
+def V(name, a=0, b=None, s=1):
+    return (name, a, PLACE[name][2] if b is None else b, s)
+
+
+def IND(win, off):
+    return ("ind", win, off)
+
+
+def rank_program(g, core, T, topo):
+    rank = T.rank_of(core)
+    if rank is None:
+        relay_program(g, core, T, topo)
+        return
+    ops = []
+    queues = {"v": g.vector, "a": g.scalar, "t": g.tensor, "g": g, "s": g.sync}
+
+    def ap(v):
+        if not isinstance(v, tuple):
+            return v
+        if v[0] == "ind":
+            return ap(v[1]).indirect(ap(v[2]))
+        name, a, b, s = v
+        buf, at = PLACE[name][:2]
+        return T[buf][:, at + a:at + b] if s == 1 else T[buf][:, at + a:at + b:s]
+
+    def regions(vs):
+        out = []
+        for v in vs:
+            if isinstance(v, tuple):
+                out += [v[1], v[2]] if v[0] == "ind" else [v]
+        return out
+
+    def add(eng, fn, writes, reads, kind="c", sem=None):
+        w, r = regions(writes), regions(reads)
+        banks = [("ps", v[1] // 512 * 512, v[1] // 512 * 512 + 512, 1) for v in w + r if v[0] == "ps"]
+        ops.append({"eng": eng, "fn": fn, "w": [v for v in w if v[0] != "ps"] + banks, "r": [v for v in r if v[0] != "ps"],
+                    "kind": kind, "sem": sem})
+
+    def cp(out, in_):
+        add("v", lambda: g.vector.tensor_copy(ap(out), ap(in_)), [out], [in_])
+
+    def scat(win, off, in_):
+        add("v", lambda: g.vector.tensor_copy(ap(IND(win, off)), ap(in_)), [win], [off, in_])
+
+    def tt(out, a, b, op):
+        add("v", lambda: g.vector.tensor_tensor(ap(out), ap(a), ap(b), op), [out], [a, b])
+
+    def ts(out, a, s1, op0, s2=None, op1=None):
+        if op1 is None:
+            add("v", lambda: g.vector.tensor_scalar(ap(out), ap(a), ap(s1), None, op0), [out], [a, s1])
+        else:
+            add("v", lambda: g.vector.tensor_scalar(ap(out), ap(a), ap(s1), ap(s2), op0, op1), [out], [a, s1, s2])
+
+    def scan(out, d0, d1, init, op0, op1):
+        add("v", lambda: g.vector.tensor_tensor_scan(ap(out), ap(d0), ap(d1), init, op0, op1), [out], [d0, d1])
+
+    def tr(out, in_):
+        add("v", lambda: g.vector.transpose(ap(out), ap(in_)), [out], [in_])
+
+    def ms(out, val):
+        add("v", lambda: g.vector.memset(ap(out), val), [out], [])
+
+    def quant(q, sc, in_):
+        add("v", lambda: g.vector.quantize_mx(ap(q), ap(sc), ap(in_)), [q, sc], [in_])
+
+    def act(out, in_, scale=None):
+        if scale is None:
+            add("a", lambda: g.scalar.activation(ap(out), ap(in_), ACT.Copy), [out], [in_])
+        else:
+            add("a", lambda: g.scalar.activation(ap(out), ap(in_), ACT.Copy, scale=scale), [out], [in_])
+
+    def actb(out, in_, bias):
+        add("a", lambda: g.scalar.activation(ap(out), ap(in_), ACT.Identity, bias=ap(bias)), [out], [in_, bias])
+
+    def mm(out, lq, ls, rq, rs):
+        add("t", lambda: g.tensor.matmul_mx(ap(out), ap(lq), ap(ls), ap(rq), ap(rs), True, True), [out], [lq, ls, rq, rs])
+
+    def iota(out, pattern, base=0, cm=0):
+        small = PLACE[out[0]][3] != I32
+        add("g", lambda: g.iota(ap(out), pattern, base, cm, allow_small_or_imprecise_dtypes=small), [out], [])
+
+    def load(eng, out, src, as_codes=False, after=()):
+        add(eng, lambda: queues[eng].dma_start(ap(out).bitcast(dt.uint8) if as_codes else ap(out), src), [out], list(after), kind="dma")
+
+    def store(eng, dst, src_ap, reads):
+        add(eng, lambda: queues[eng].dma_start(dst, src_ap), [], reads, kind="out")
+
+    sent = [0]
+
+    def route(rnd, kind, name=None):
+        dst = partner_of(T, rank, rnd)
+        to, mask = first_hop(topo, core, dst, kind)
+        src, land, sem, there, came = names_of(kind, rnd)
+        sent[0] += engines_in(mask)
+        return (to, land if to == dst else there, name or src, sem if to == dst else came, mask)
+
+    def remote(rnd, kind, name=None):
+        r = route(rnd, kind, name)
+        add("g", lambda: send(g, T, topo, core, *r), [], [V(r[2])], kind="remote")
+
+    def remote_pair(rnd, kinds):
+        rs = [route(rnd, k) for k in kinds]
+        if rs[0][4] & rs[1][4]:
+            for r in rs:
+                add("g", lambda r=r: send(g, T, topo, core, *r), [], [V(r[2])], kind="remote")
+            return
+        transfers = []
+        for to, land, src, sem, mask in rs:
+            rid, pid = topo.addr(to, core)
+            transfers.append(RemoteDMATransfer(dst_ids=[DstId(rid=rid, pnc=pid)], dma_engine_mask=mask, remote_sem=T.sem[sem],
+                                               src=whole(T, src), dst=whole(T, land)))
+        add("g", lambda: g.remote_dma_fused(transfers, local_sem=T.sem["sent"]), [], [V(r[2]) for r in rs], kind="remote")
+
+    def arrival(rnd, kinds):
+        src = partner_of(T, rank, rnd)
+        n = sum(engines_in(topo.mask(relay_of(topo, src, core, k) or src, core)) for k in kinds)
+        add(None, None, [V(names_of(k, rnd)[1]) for k in kinds], [], kind="arrive", sem=(names_of(kinds[0], rnd)[2], n))
+
+    def col(i):
+        return V("col", i, i + 1)
+
+    def lst(a, n):
+        return V("lst", a, a + n)
+
+    R_, R1, HI, LO, R3, R7, C5 = range(7)
+    C16P, R38, PF, RP = 8, 9, 10, 11
+    M1000 = 40
+    left = [rank & (1 << rnd) == 0 for rnd in range(NR)]
+    CP_PL, CP_EI, CP_EC, CP_8, CP_LC, CP_16, CP_TI, CP_I, CP_48 = [V("cp", a, b) for a, b in [
+        (0, 24), (24, 40), (40, 52), (52, 56), (56, 72), (72, 88), (88, 104), (104, 120), (120, 136)]]
+
+    load("s", V("pin"), T.p[:])
+    load("a", V("hin"), T.h[:])
+    load("a", V("ut"), T.u[:])
+    load("s", V("x0"), T.x[:])
+
+    iota(V("pidx"), [[1, 1]], 0, 1)
+    iota(V("c16"), [[16, 24]])
+    if not left[0]:
+        iota(CP_EI, [[8, 4], [0, 4]])
+        iota(V("kl"), [[0, 2], [1, 16], [0, 8]])
+    iota(V("irl"), [[1, C]])
+    iota(CP_PL, [[1, 2], [32, 12]])
+    if not left[0]:
+        iota(CP_EC, [[2, 12]])
+
+    ms(V("wl"), 0.0)
+    ms(V("k16"), 1.0)
+    ms(V("k8"), 1.0)
+    ms(V("ones"), 1.0)
+    for i, (sh, m) in enumerate([(0, 15), (1, 7), (2, 3), (0, 3), (3, 1), (0, 7), (0, 31)]):
+        ts(V("coli", i, i + 1), V("pidx"), sh, A.logical_shift_right, m, A.bitwise_and)
+    ms(V("k16", 0, C, 16), 0.0)
+    cp(V("col", 0, 7), V("coli", 0, 7))
+    ms(V("k8", 0, 256, 8), 0.0)
+    ts(col(C16P), col(C5), 16.0, A.mult)
+    ts(col(R38), col(R3), 8.0, A.mult, 10.0, A.add)
+    ts(col(RP), col(R_), 1.0, A.add)
+    ts(col(R1), col(R1), 1.0, A.add)
+    scan(V("j16"), V("k16"), V("ones"), 0.0, A.mult, A.add)
+    scan(V("b8"), V("k8", 0, H), V("ones", 0, H), 0.0, A.mult, A.add)
+    ts(V("dm"), V("j16"), col(RP), A.is_equal)
+    cp(lst(L_UP, 8), V("c16", 0, 8))
+    ms(V("fsn", H, 256), 0.0)
+
+    def right_consts():
+        actb(V("kg"), V("kl"), col(C16P))
+
+    def prepare(rnd, ev, ed):
+        if left[rnd]:
+            ts(V(ev), V("wt"), col(C16P), A.subtract)
+            tt(V(ed, 0, 32, 2), V("wt", 1, 32, 2), V("wt", 0, 32, 2), A.subtract)
+            tt(V(ed, 1, 32, 2), V("wt", 0, 32, 2), V("wt", 1, 32, 2), A.subtract)
+        else:
+            tt(V("nm"), IND(V("wt"), lst(L_EI, 16)), V("kg"), A.not_equal)
+            scan(V("iv"), V("nm"), V("ones", 0, 256), 0.0, A.mult, A.add)
+            cp(V("qi"), V("iv", 7, 256, 8))
+            cp(V(ev), V("iv", 7, 256, 8))
+            ts(V("par"), V("qi"), 1, A.bitwise_and)
+            ts(V(ed), V("par"), 2.0, A.mult, -1.0, A.add)
+
+    def prepare_mask():
+        tr(V("vl"), V("iv", 7, 256, 8))
+        ts(V("pl"), V("vl", 0, 24), -1.0, A.mult, col(R38), A.add)
+        ts(V("pb"), V("pl"), 1, A.logical_shift_right)
+        tt(V("mkb"), IND(V("pb"), lst(L_EC, 12)), V("b8"), A.not_equal)
+        act(V("maskr"), V("mkb"), -BIG)
+
+    def prepare_lists():
+        tt(V("ext"), IND(V("hw"), lst(L_PL, 24)), V("dm"), A.mult)
+        scan(V("exs"), V("k16"), V("ext"), 0.0, A.mult, A.add)
+        cp(V("lab"), V("exs", 15, C, 16))
+
+    def product(x, hf, last):
+        a, b = H * hf, H * hf + H
+        bank = 2048 + 512 * hf
+        quant(V("xq", a, b), V("xsc", a, b), V(x, 4 * a, 4 * b))
+        mm(V("ps", bank, bank + H), V("vq" if last else "uq2"), V("vs" if last else "us2"), V("xq", a, b), V("xsc", a, b))
+
+    def fetch(hf, last):
+        bank = 2048 + 512 * hf
+        (act if hf == 0 else cp)(V("yo" if last else "s", H * hf, H * hf + H), V("ps", bank, bank + H))
+
+    def lead_consts():
+        a3, i_, k1, e5, e7, r34, u0, u1, v1, t, v0 = [col(c) for c in range(12, 23)]
+        ts(a3, col(R7), 3.0, A.is_ge)
+        ts(e5, col(R7), 5.0, A.is_equal, 3.0, A.mult)
+        ts(e7, col(R7), 7.0, A.is_equal)
+        ts(i_, col(R7), 6.0, A.is_ge, a3, A.add)
+        ts(r34, col(R3), 4.0, A.mult)
+        ms(V("fone"), 0.0)
+        ts(k1, i_, -2.0, A.mult, col(R7), A.add)
+        ts(u1, i_, r34, A.add)
+        ts(lst(L_U, 4), CP_8, col(HI), A.add)
+        ts(u0, k1, e5, A.subtract, r34, A.add)
+        ts(t, k1, i_, A.subtract, 1.0, A.is_ge)
+        ms(V("fone", 128 + 7, 192, 8), 100.0)
+        ts(v1, e7, -2.0, A.mult, u0, A.add)
+        ts(v0, t, e7, A.subtract, u0, A.add)
+        ts(lst(L_U + 4, 4), CP_8, u0, A.add)
+        ts(lst(L_U + 8, 4), CP_8, u1, A.add)
+        ts(lst(L_V, 4), CP_8, col(LO), A.add, 4.0, A.add)
+        ts(lst(L_V + 8, 4), CP_8, v1, A.add, 1.0, A.add)
+        ts(lst(L_V + 4, 4), CP_8, v0, A.add)
+
+    def meet_consts():
+        mx, mn, mx4, mn16, t1, t2, d1, d2, s1, s2 = [col(c) for c in range(24, 34)]
+        ts(mx, col(LO), col(HI), A.max)
+        ts(mn, col(LO), col(HI), A.min)
+        ts(d1, col(LO), col(HI), A.is_le, 8.0, A.mult)
+        ts(d2, col(LO), col(HI), A.is_ge, 8.0, A.mult)
+        ts(mx4, mx, 4.0, A.mult)
+        ts(mn16, mn, 16.0, A.mult)
+        ts(t1, col(HI), 2.0, A.mult, mx, A.add)
+        ts(t2, mn, 2.0, A.mult, col(HI), A.add)
+        ms(V("k4"), 1.0)
+        ts(lst(L_LCX, 16), CP_LC, mx4, A.add)
+        ts(s1, t1, d1, A.max, 8.0, A.min)
+        ts(s2, t2, d2, A.max, 8.0, A.min)
+        ts(lst(L_TI, 16), CP_TI, mn16, A.add)
+        ms(V("k4", 0, 256, 4), 0.0)
+        ts(lst(L_RI, 16), CP_16, s1, A.add, -1.0, A.add)
+        ts(lst(L_RX, 16), CP_16, s2, A.add, 7.0, A.add)
+        i_, lo, hi, q4, a, b, b2, w, e = [V("pa", 16 * i, 16 * i + 16) for i in range(9)]
+        ts(i_, CP_I, col(R3), A.add)
+        ts(e, CP_EI, col(R7), A.add, 8.0, A.mult)
+        ts(lo, i_, col(R7), A.min)
+        ts(hi, i_, col(R7), A.max)
+        ts(lst(L_EI8, 16), e, 7.0, A.add)
+        ts(q4, lo, 4.0, A.is_ge, 4.0, A.mult)
+        ts(a, lo, 2.0, A.mult, -1.0, A.add)
+        ts(b, lo, 14.0, A.mult)
+        ts(b2, hi, 3.0, A.mult, 52.0, A.add)
+        ts(w, hi, 4.0, A.is_ge, 4.0, A.mult)
+        tt(a, a, hi, A.add)
+        tt(b, b, b2, A.add)
+        tt(w, w, q4, A.subtract)
+        tt(a, a, q4, A.subtract)
+        tt(b, b, CP_48, A.add)
+        ts(w, w, 0.25, A.mult)
+        tt(a, a, CP_16, A.add)
+        tt(b, b, w, A.mult)
+        ts(V("sgn"), V("gij"), -1.0, A.max, 1.0, A.min)
+        tt(a, a, b, A.add)
+        cp(lst(L_PI, 16), a)
+
+    def slot_consts():
+        ts(V("d1", 1, 48, 2), V("c16"), col(R_), A.add)
+        ms(V("tot", 0, 1), 15)
+        ms(V("tot", 1, 2), 31)
+        act(V("cbig"), V("dm", 0, TS), 1000.0)
+
+    def unpack_consts():
+        ms(V("et"), 0.0)
+        cp(col(PF), V("pidx"))
+        ts(V("idn"), V("irl", 0, 128), col(PF), A.is_equal, 16.0, A.mult)
+        for b in range(4):
+            cp(V("et", 512 * b + b, 512 * b + 512, 4), V("idn"))
+        quant(V("eq"), V("es"), V("et"))
+
+    if not left[0]:
+        ts(lst(L_EI, 16), CP_EI, col(R7), A.add)
+        right_consts()
+    cp(V("wl", 0, 24), V("pin"))
+    cp(V("h16"), V("hin"))
+    tr(V("wt"), V("wl"))
+    cp(V("w16"), V("pin"))
+    act(V("hrl"), IND(V("irl"), V("h16")))
+    act(V("hw"), IND(V("hrl"), V("w16")))
+    prepare(0, "ev0", "ed0")
+    remote_pair(0, "ed")
+    ts(lst(L_PL, 24), CP_PL, col(R_), A.add, col(R_), A.add)
+    quant(V("uq"), V("us"), V("ut"))
+    add("v", lambda: g.vector.tensor_copy(T.uq2[:].bitcast(dt.uint32), T.uq[:].bitcast(dt.uint32).indirect(ap(lst(L_UP, 8)))),
+        [V("uq2")], [V("uq"), lst(L_UP, 8)])
+    act(V("us2"), IND(V("us"), lst(L_UP, 8)))
+    if left[0]:
+        ts(V("maskl"), V("b8"), col(R1), A.not_equal, -BIG, A.mult)
+    else:
+        ts(lst(L_EC, 12), CP_EC, col(R3), A.add)
+        prepare_mask()
+    prepare_lists()
+    product("x0", 0, False)
+    product("x0", 1, False)
+    fetch(0, False)
+    fetch(1, False)
+    iota(CP_8, [[8, 4]])
+    if left[0]:
+        iota(CP_EI, [[8, 4], [0, 4]])
+    iota(CP_LC, [[16, 4], [1, 4]])
+    iota(CP_16, [[16, 4], [0, 4]])
+    iota(CP_TI, [[64, 4], [4, 4]], 3)
+    iota(CP_I, [[0, 4], [2, 4]])
+    iota(CP_48, [[48, 4], [0, 4]])
+
+    def late_iotas():
+        iota(V("gij"), [[0, 4], [1, 8], [-1, 8]])
+        if not all(left):
+            iota(V("nk"), [[0, 4], [-1, 8], [0, 8]], 8)
+            for y in range(2):
+                iota(V("kb", 128 * y, 128 * y + 128), [[8, 2], [0, 8], [-1, 8]], 1007)
+        if any(left):
+            iota(V("kk"), [[0, 4], [1, 8], [1, 8]], -7)
+        iota(V("k2"), [[0, 4], [2, 8]], -7)
+        if left[0] and not all(left):
+            iota(V("kl"), [[0, 2], [1, 16], [0, 8]])
+            iota(CP_EC, [[2, 12]])
+        iota(V("cmin"), [[0, 2], [1000, 16]], 1000)
+        iota(V("k1000"), [[0, 24]], 1000)
+        iota(V("base"), [[0, 24]], -617)
+        iota(V("d0"), [[0, 48]], -1000000)
+        iota(V("ew", C, YW), [[0, TS]], C - 1)
+
+    PI, EI8 = lst(L_PI, 16), lst(L_EI8, 16)
+    for rnd in range(NR):
+        last = rnd + 1 == NR
+        q = V("qt%d" % rnd)
+        ev, ed, ft = ("ev0", "ed0", "ft0") if rnd == 0 else ("ev", "ed", "ft")
+        tt(V("sb"), IND(V("s"), V("lab", 12, 24)), V("maskl" if left[rnd] else "maskr"), A.add)
+        tt(V("fl"), IND(V("s"), V("lab", 0, 12)), V("sb"), A.is_lt)
+        scan(V("fsn", 0, H), V("k8", 0, H), V("fl"), 0.0, A.mult, A.add)
+        tr(V(ft), V("fsn", 7, 256, 8))
+        if rnd == 0:
+            remote(rnd, "w", ft)
+            late_iotas()
+            for t in range(4):
+                ts(V("xh16", 24 * t, 24 * t + 24), V("hin"), 4.0, A.mult, float(t), A.add)
+            arrival(rnd, "ed")
+            load("s", V("wq"), T.wc[:], as_codes=True, after=[V("pev")])
+            load("s", V("wsc"), T.ws[:])
+        tt(V("t32"), V(ft), V(ed), A.mult)
+        tt(q, V("t32"), V(ev), A.add)
+        if rnd > 0:
+            remote(rnd, "w")
+        act(V("xh"), IND(V("x0" if rnd == 0 else "xs"), V("xh16")))
+        if rnd == 0:
+            lead_consts()
+        tt(V("oa"), IND(q, lst(L_U, 12)), V("fone"), A.add)
+        tt(V("ob"), IND(q, lst(L_V, 12)), V("oa"), A.is_lt)
+        ts(V("own"), V("ob"), 100.0, A.mult)
+        if rnd == 0:
+            if left[0]:
+                ts(lst(L_EI, 16), CP_EI, col(R7), A.add)
+            ms(V("ag", 32, 40), 0.0)
+            ms(col(M1000), -1000.0)
+            meet_consts()
+            if not all(left):
+                actb(V("kb"), V("kb"), col(C16P))
+        if left[rnd]:
+            ts(V("ag", 0, 32), q, col(C16P), A.add)
+            tt(V("adf"), V("ag", 0, 32), V("ag", 1, 33), A.subtract)
+            cp(V("adf", 7, 32, 8), V("ag", 7, 32, 8))
+            cp(V("dex"), IND(V("adf"), lst(L_EI, 16)))
+        else:
+            tt(V("nm"), IND(q, lst(L_EI, 16)), V("nk"), A.is_equal)
+            tt(V("t11"), V("nm"), V("kb"), A.mult)
+            actb(V("dex"), V("t11"), col(M1000))
+        if rnd == 0:
+            slot_consts()
+        pw = V("pw%d" % rnd)
+        arrival(rnd, "w")
+        if rnd == 0:
+            tt(V("t32"), pw, V("ped"), A.mult)
+            tt(V("pq"), V("t32"), V("pev"), A.add)
+            pw = V("pq")
+        tt(V("pu", 0, 64), IND(pw, lst(L_U, 4)), V("own", 0, 64), A.add)
+        tt(V("lead", 0, 64), IND(pw, lst(L_V, 4)), V("pu", 0, 64), A.is_lt)
+        act(V("lcx"), IND(V("lead", 0, 64), lst(L_LCX, 16)))
+        tt(V("pu", 64, 192), IND(pw, lst(L_U + 4, 8)), V("own", 64, 192), A.add)
+        tt(V("lead", 64, 192), IND(pw, lst(L_V + 4, 8)), V("pu", 64, 192), A.is_lt)
+        scan(V("rw2", 0, 64), V("lead", 64, 128), V("lead", 128, 192), 0.0, A.mult, A.max)
+        tt(V("rw2", 2, 64, 8), V("rw2", 2, 64, 8), V("rw2", 5, 64, 8), A.max)
+        act(V("rxx"), IND(V("rw2", 0, 64), lst(L_RX, 16)))
+        tt(V("t5"), IND(V("rw2", 0, 64), lst(L_RI, 16)), V("lcx"), A.mult)
+        scan(V("tt"), V("k4"), V("t5"), 0.0, A.mult, A.max)
+        tt(V("t7"), IND(V("tt"), lst(L_TI, 16)), V("rxx"), A.mult)
+        scan(V("rw2", 64, 320), V("k4"), V("t7"), 0.0, A.mult, A.max)
+        tt(V("t9"), IND(V("rw2"), PI), V("sgn"), A.mult)
+        scan(V("pos"), V("k8"), V("t9"), 0.0, A.mult, A.add)
+        if left[rnd]:
+            tt(V("nm"), IND(V("pos"), EI8), V("kk"), A.not_equal)
+            scan(V("nw"), V("nm"), V("dex"), 0.0, A.mult, A.add)
+        else:
+            tt(V("t11"), IND(V("pos"), EI8), V("dex"), A.add)
+            scan(V("nw"), V("k8"), V("t11"), 0.0, A.mult, A.max)
+        tr(V("wl"), V("nw", 7, 256, 8))
+        cp(V("w16"), V("wl", 0, 24))
+        for t in range(4):
+            act(V("z", t, 4 * C, 4), IND(V("xh", C * t, C * t + C), V("w16")))
+        for b in range(4):
+            act(V("z32", C * b, C * b + C), V("z", b, 4 * C, 4), 32.0)
+        if rnd == 0:
+            load("s", V("vt"), T.v[:], after=[V("w16")])
+        tt(V("mv"), V("pos", 7, 256, 8), V("k2"), A.not_equal)
+        scan(V("pp"), V("cmin"), V("mv"), 1000.0, A.min, A.add)
+        tt(V("tp", 32, 64), V("pp"), V("mv"), A.mult)
+        cp(V("tp", 0, 32), IND(V("pp"), V("tot")))
+        tr(V("tpt"), V("tp"))
+        scan(V("base", 1, 24), V("tpt", 0, 23), V("k1000", 0, 23), -617.0, A.add, A.subtract)
+        tt(V("d0", 1, 48, 2), V("base"), V("tpt", 32, 56), A.add)
+        ts(V("d1", 0, 48, 2), V("d0", 1, 48, 2), float(YW), A.subtract, -1000.0, A.mult)
+        scan(V("mm"), V("d0"), V("d1"), 0.0, A.min, A.max)
+        cp(V("idx"), V("mm", 1, 48, 2))
+        scat(V("ew"), V("idx"), V("irl"))
+        scan(V("esn"), V("cbig"), V("ew", C, YW), 0.0, A.add, A.min)
+        cp(V("e16"), V("esn", 15, TS, 16))
+        if last:
+            cp(V("wt"), V("nw", 7, 256, 8))
+            for gr in range(8):
+                a, y = gr // 2, gr % 2
+                store("s", T.op[gr:gr + 1, :], T.wt[32 * a:32 * a + 24, 16 * y:16 * y + 16], [V("wt")])
+        pieces = [(0, 0, H, 0), (0, H, C, 3072), (1, 0, C, 512), (2, 0, C, 1024), (3, 0, C, 1536)]
+        for hf in range(2):
+            quant(V("zq", H * hf, H * hf + H), V("zs", H * hf, H * hf + H), V("z", 4 * H * hf, 4 * H * hf + 4 * H))
+        for b, lo, hi, bank in pieces:
+            mm(V("ps", bank, bank + hi - lo), V("wq", 128 * b, 128 * b + 128), V("wsc", 128 * b, 128 * b + 128), V("zq", lo, hi), V("zs", lo, hi))
+        for b, lo, hi, bank in pieces:
+            tt(V("ym", YW * b + lo, YW * b + hi), V("ps", bank, bank + hi - lo), V("z32", C * b + lo, C * b + hi), A.add)
+            if hi == C and b < 3:
+                act(V("f", b, 4 * TS, 4), IND(V("ym", YW * b, YW * b + C), V("e16")), 0.03125)
+        ts(V("f", 3, 4 * TS, 4), IND(V("ym", YW * 3, YW * 3 + C), V("e16")), 0.03125, A.mult)
+        quant(V("fq%d" % rnd), V("fs%d" % rnd), V("f"))
+        remote(rnd, "q")
+        remote(rnd, "s")
+        ts(V("f16"), V("f"), 16.0, A.mult)
+        if rnd == 0:
+            unpack_consts()
+            if left[0] and not all(left):
+                right_consts()
+                ts(lst(L_EC, 12), CP_EC, col(R3), A.add)
+            if any(left) and not left[0]:
+                ts(V("maskl"), V("b8"), col(R1), A.not_equal, -BIG, A.mult)
+        if not last:
+            cp(V("wt"), V("nw", 7, 256, 8))
+            act(V("hw"), IND(V("hrl"), V("w16")))
+            iota(V("ew", C, YW), [[0, TS]], C - 1)
+            prepare(rnd + 1, "ev", "ed")
+            if not left[rnd + 1]:
+                prepare_mask()
+            prepare_lists()
+        else:
+            quant(V("vq"), V("vs"), V("vt"))
+        arrival(rnd, "qs")
+        for b in range(4):
+            mm(V("ps", 512 * b, 512 * b + TS), V("eq", 128 * b, 128 * b + 128), V("es", 128 * b, 128 * b + 128),
+               V("lq%d" % rnd), V("ls%d" % rnd))
+
+        def pick(eng, b, hf):
+            out = V("xs", 4 * H * hf + b, 4 * H * hf + 4 * H, 4)
+            src = IND(V("ym", YW * b, YW * b + YW), V("idx", 12 * hf, 12 * hf + 12))
+            if eng == "a":
+                act(out, src, 0.03125)
+            else:
+                ts(out, src, 0.03125, A.mult)
+
+        for b in range(4):
+            tt(V("ym", YW * b + C, YW * b + YW), V("ps", 512 * b, 512 * b + TS), V("f16", b, 4 * TS, 4), A.add)
+            if b < 3:
+                pick("a", b, 0)
+        pick("v", 3, 0)
+        pick("a", 0, 1)
+        pick("a", 1, 1)
+        pick("v", 3, 1)
+        product("xs", 0, last)
+        if last:
+            store("s", T.oc[:, 0:4 * H], T.xq[:, 0:H].bitcast(dt.uint8), [V("xq", 0, H)])
+        pick("v", 2, 1)
+        product("xs", 1, last)
+        fetch(0, last)
+        fetch(1, last)
+
+    store("a", T.y[:, 0:H], T.yo[:, 0:H], [V("yo", 0, H)])
+    store("s", T.oc[:, 4 * H:4 * C], T.xq[:, H:C].bitcast(dt.uint8), [V("xq", H, C)])
+    for k in range(4):
+        store("s" if k < 2 else "a", T.osc[4 * k:4 * k + 4, :], T.xsc[32 * k:32 * k + 4, :], [V("xsc")])
+    store("s", T.y[:, H:C], T.yo[:, H:C], [V("yo", H, C)])
+
+    emit(g, T, ops, queues, sent[0])
+
+
+def emit(g, T, ops, queues, sent):
+    cache = {}
+
+    def cols(v):
+        if v not in cache:
+            cache[v] = sum(1 << i for i in range(v[1], v[2], v[3]))
+        return cache[v]
+
+    hist = {}
+    known = {e: set() for e in queues}
+    at_issue, waits = [], []
+    for i, op in enumerate(ops):
+        deps = set()
+        for v in op["w"]:
+            deps |= {j for j, m, wr in hist.get(v[0], []) if m & cols(v)}
+        for v in op["r"]:
+            deps |= {j for j, m, wr in hist.get(v[0], []) if wr and m & cols(v)}
+        for v in op["w"]:
+            hist[v[0]] = [(j, m & ~cols(v), wr) for j, m, wr in hist.get(v[0], []) if m & ~cols(v)] + [(i, cols(v), True)]
+        for v in op["r"]:
+            hist.setdefault(v[0], []).append((i, cols(v), False))
+        deps.discard(i)
+        mine = []
+        if op["eng"] is not None:
+            kn = known[op["eng"]]
+            for j in sorted(deps, reverse=True):
+                if j not in kn:
+                    mine.append(j)
+                    kn.add(j)
+                    kn |= at_issue[j]
+            at_issue.append(set(kn))
+        else:
+            at_issue.append(set())
+        waits.append(mine[::-1])
+    needed = {j for w in waits for j in w}
+    signal, used = {}, {e: [] for e in POOL}
+    outs = 0
+    for i, op in enumerate(ops):
+        if op["kind"] == "arrive":
+            signal[i] = op["sem"]
+            continue
+        queue = queues[op["eng"]]
+        pool = "dma" if op["kind"] == "dma" else op["eng"]
+        if i in needed:
+            n = len(used[pool])
+            if n >= POOL[pool] and used[pool][n - POOL[pool]] not in at_issue[i]:
+                waits[i] = waits[i] + [used[pool][n - POOL[pool]]]
+            step = 16 if pool == "dma" else 1
+            signal[i] = ("%s%d" % (pool, n % POOL[pool]), step * (n // POOL[pool] + 1))
+            used[pool].append(i)
+        for j in waits[i]:
+            queue.wait_ge(T.sem[signal[j][0]], signal[j][1])
+        ins = op["fn"]()
+        if op["kind"] == "out":
+            ins.then_inc(T.sem["outs"], 16)
+            outs += 16
+        elif i in needed:
+            ins.then_inc(T.sem[signal[i][0]], 16 if pool == "dma" else 1)
+    g.wait_ge(T.sem["sent"], sent)
+    g.sync.wait_ge(T.sem["outs"], outs)

@@ -229,6 +229,16 @@ def rank_program(g, core, T, topo):
     def lst(a, n):
         return V("lst", a, a + n)
 
+    def weave(*parts):
+        chains = []
+        for part in parts:
+            at = len(ops)
+            part()
+            chains.append(ops[at:])
+            del ops[at:]
+        for i in range(max(len(c) for c in chains)):
+            ops.extend(c[i] for c in chains if i < len(c))
+
     R_, R1, HI, LO, R3, R7, C5 = range(7)
     C16P, R38, PF, RP = 8, 9, 10, 11
     M1000 = 40
@@ -258,13 +268,13 @@ def rank_program(g, core, T, topo):
     for i, (sh, m) in enumerate([(0, 15), (1, 7), (2, 3), (0, 3), (3, 1), (0, 7), (0, 31)]):
         ts(V("coli", i, i + 1), V("pidx"), sh, A.logical_shift_right, m, A.bitwise_and)
     ms(V("k16", 0, C, 16), 0.0)
-    cp(V("col", 0, 7), V("coli", 0, 7))
     ms(V("k8", 0, 256, 8), 0.0)
-    ts(col(C16P), col(C5), 16.0, A.mult)
-    ts(col(R38), col(R3), 8.0, A.mult, 10.0, A.add)
-    ts(col(RP), col(R_), 1.0, A.add)
-    ts(col(R1), col(R1), 1.0, A.add)
+    cp(V("col", 0, 7), V("coli", 0, 7))
     scan(V("j16"), V("k16"), V("ones"), 0.0, A.mult, A.add)
+    ts(col(C16P), col(C5), 16.0, A.mult)
+    ts(col(RP), col(R_), 1.0, A.add)
+    ts(col(R38), col(R3), 8.0, A.mult, 10.0, A.add)
+    ts(col(R1), col(R1), 1.0, A.add)
     scan(V("b8"), V("k8", 0, H), V("ones", 0, H), 0.0, A.mult, A.add)
     ts(V("dm"), V("j16"), col(RP), A.is_equal)
     cp(lst(L_UP, 8), V("c16", 0, 8))
@@ -351,6 +361,7 @@ def rank_program(g, core, T, topo):
         i_, lo, hi, q4, a, b, b2, w, e = [V("pa", 16 * i, 16 * i + 16) for i in range(9)]
         ts(i_, CP_I, col(R3), A.add)
         ts(e, CP_EI, col(R7), A.add, 8.0, A.mult)
+        ts(V("sgn"), V("gij"), -1.0, A.max, 1.0, A.min)
         ts(lo, i_, col(R7), A.min)
         ts(hi, i_, col(R7), A.max)
         ts(lst(L_EI8, 16), e, 7.0, A.add)
@@ -366,49 +377,63 @@ def rank_program(g, core, T, topo):
         tt(b, b, CP_48, A.add)
         ts(w, w, 0.25, A.mult)
         tt(a, a, CP_16, A.add)
+        ms(V("tot", 0, 1), 15)
         tt(b, b, w, A.mult)
-        ts(V("sgn"), V("gij"), -1.0, A.max, 1.0, A.min)
+        ms(V("tot", 1, 2), 31)
+        ts(V("d1", 1, 48, 2), V("c16"), col(R_), A.add)
         tt(a, a, b, A.add)
+        act(V("cbig"), V("dm", 0, TS), 1000.0)
+        ms(V("ag", 32, 40), 0.0)
+        ms(col(M1000), -1000.0)
         cp(lst(L_PI, 16), a)
 
-    def slot_consts():
-        ts(V("d1", 1, 48, 2), V("c16"), col(R_), A.add)
-        ms(V("tot", 0, 1), 15)
-        ms(V("tot", 1, 2), 31)
-        act(V("cbig"), V("dm", 0, TS), 1000.0)
-
     def unpack_consts():
-        ms(V("et"), 0.0)
         cp(col(PF), V("pidx"))
+        ms(V("et"), 0.0)
         ts(V("idn"), V("irl", 0, 128), col(PF), A.is_equal, 16.0, A.mult)
         for b in range(4):
             cp(V("et", 512 * b + b, 512 * b + 512, 4), V("idn"))
         quant(V("eq"), V("es"), V("et"))
+
+    def spread_u():
+        ts(lst(L_PL, 24), CP_PL, col(R_), A.add, col(R_), A.add)
+        quant(V("uq"), V("us"), V("ut"))
+        add("v", lambda: g.vector.tensor_copy(T.uq2[:].bitcast(dt.uint32), T.uq[:].bitcast(dt.uint32).indirect(ap(lst(L_UP, 8)))),
+            [V("uq2")], [V("uq"), lst(L_UP, 8)])
+        act(V("us2"), IND(V("us"), lst(L_UP, 8)))
+
+    def first_mask():
+        if left[0]:
+            ts(V("maskl"), V("b8"), col(R1), A.not_equal, -BIG, A.mult)
+        else:
+            ts(lst(L_EC, 12), CP_EC, col(R3), A.add)
+            prepare_mask()
+
+    def first_scores():
+        product("x0", 0, False)
+        product("x0", 1, False)
 
     if not left[0]:
         ts(lst(L_EI, 16), CP_EI, col(R7), A.add)
         right_consts()
     cp(V("wl", 0, 24), V("pin"))
     cp(V("h16"), V("hin"))
-    tr(V("wt"), V("wl"))
     cp(V("w16"), V("pin"))
+    tr(V("wt"), V("wl"))
     act(V("hrl"), IND(V("irl"), V("h16")))
     act(V("hw"), IND(V("hrl"), V("w16")))
-    prepare(0, "ev0", "ed0")
-    remote_pair(0, "ed")
-    ts(lst(L_PL, 24), CP_PL, col(R_), A.add, col(R_), A.add)
-    quant(V("uq"), V("us"), V("ut"))
-    add("v", lambda: g.vector.tensor_copy(T.uq2[:].bitcast(dt.uint32), T.uq[:].bitcast(dt.uint32).indirect(ap(lst(L_UP, 8)))),
-        [V("uq2")], [V("uq"), lst(L_UP, 8)])
-    act(V("us2"), IND(V("us"), lst(L_UP, 8)))
     if left[0]:
-        ts(V("maskl"), V("b8"), col(R1), A.not_equal, -BIG, A.mult)
+        prepare(0, "ev0", "ed0")
+        remote_pair(0, "ed")
+        spread_u()
+        first_mask()
+        prepare_lists()
+        first_scores()
     else:
-        ts(lst(L_EC, 12), CP_EC, col(R3), A.add)
-        prepare_mask()
-    prepare_lists()
-    product("x0", 0, False)
-    product("x0", 1, False)
+        weave(lambda: prepare(0, "ev0", "ed0"), spread_u)
+        remote_pair(0, "ed")
+        weave(first_mask, prepare_lists)
+        first_scores()
     fetch(0, False)
     fetch(1, False)
     iota(CP_8, [[8, 4]])
@@ -426,6 +451,7 @@ def rank_program(g, core, T, topo):
             iota(V("nk"), [[0, 4], [-1, 8], [0, 8]], 8)
             for y in range(2):
                 iota(V("kb", 128 * y, 128 * y + 128), [[8, 2], [0, 8], [-1, 8]], 1007)
+        iota(V("d0"), [[0, 48]], -1000000)
         if any(left):
             iota(V("kk"), [[0, 4], [1, 8], [1, 8]], -7)
         iota(V("k2"), [[0, 4], [2, 8]], -7)
@@ -435,17 +461,32 @@ def rank_program(g, core, T, topo):
         iota(V("cmin"), [[0, 2], [1000, 16]], 1000)
         iota(V("k1000"), [[0, 24]], 1000)
         iota(V("base"), [[0, 24]], -617)
-        iota(V("d0"), [[0, 48]], -1000000)
         iota(V("ew", C, YW), [[0, TS]], C - 1)
 
-    PI, EI8 = lst(L_PI, 16), lst(L_EI8, 16)
+    def hv(name, hf, at=0):
+        return V(name, at + 128 * hf, at + 128 * hf + 128)
+
+    def hind(name, l, hf, at=0):
+        return IND(V(name, 0, at + 128 * hf + 128), lst(l + 8 * hf, 8))
+
+    def pick(eng, b, c0, c1):
+        out = V("xs", 64 * c0 + b, 64 * c1, 4)
+        src = IND(V("ym", YW * b, YW * b + YW), V("idx", c0, c1))
+        if eng == "a":
+            act(out, src, 0.03125)
+        else:
+            ts(out, src, 0.03125, A.mult)
+
     for rnd in range(NR):
         last = rnd + 1 == NR
         q = V("qt%d" % rnd)
         ev, ed, ft = ("ev0", "ed0", "ft0") if rnd == 0 else ("ev", "ed", "ft")
-        tt(V("sb"), IND(V("s"), V("lab", 12, 24)), V("maskl" if left[rnd] else "maskr"), A.add)
-        tt(V("fl"), IND(V("s"), V("lab", 0, 12)), V("sb"), A.is_lt)
-        scan(V("fsn", 0, H), V("k8", 0, H), V("fl"), 0.0, A.mult, A.add)
+        for a in (0, 96):
+            tt(V("sb", a, a + 96), IND(V("s"), V("lab", 12 + a // 16, 18 + a // 16)), V("maskl" if left[rnd] else "maskr", a, a + 96), A.add)
+        for a in (0, 96):
+            tt(V("fl", a, a + 96), IND(V("s"), V("lab", a // 16, 6 + a // 16)), V("sb", a, a + 96), A.is_lt)
+        for a in (0, 96):
+            scan(V("fsn", a, a + 96), V("k8", a, a + 96), V("fl", a, a + 96), 0.0, A.mult, A.add)
         tr(V(ft), V("fsn", 7, 256, 8))
         if rnd == 0:
             remote(rnd, "w", ft)
@@ -456,34 +497,37 @@ def rank_program(g, core, T, topo):
             load("s", V("wq"), T.wc[:], as_codes=True, after=[V("pev")])
             load("s", V("wsc"), T.ws[:])
         tt(V("t32"), V(ft), V(ed), A.mult)
+        if rnd == 0:
+            act(V("xh"), IND(V("x0"), V("xh16")))
+            lead_consts()
         tt(q, V("t32"), V(ev), A.add)
         if rnd > 0:
             remote(rnd, "w")
-        act(V("xh"), IND(V("x0" if rnd == 0 else "xs"), V("xh16")))
-        if rnd == 0:
-            lead_consts()
-        tt(V("oa"), IND(q, lst(L_U, 12)), V("fone"), A.add)
-        tt(V("ob"), IND(q, lst(L_V, 12)), V("oa"), A.is_lt)
-        ts(V("own"), V("ob"), 100.0, A.mult)
+            act(V("xh"), IND(V("xs"), V("xh16")))
+
+        def own_half():
+            tt(V("oa"), IND(q, lst(L_U, 12)), V("fone"), A.add)
+            tt(V("ob"), IND(q, lst(L_V, 12)), V("oa"), A.is_lt)
+            ts(V("own"), V("ob"), 100.0, A.mult)
+
+        def word_half():
+            if left[rnd]:
+                ts(V("ag", 0, 32), q, col(C16P), A.add)
+                tt(V("adf"), V("ag", 0, 32), V("ag", 1, 33), A.subtract)
+                cp(V("adf", 7, 32, 8), V("ag", 7, 32, 8))
+                cp(V("dex"), IND(V("adf"), lst(L_EI, 16)))
+            else:
+                tt(V("nm"), IND(q, lst(L_EI, 16)), V("nk"), A.is_equal)
+                tt(V("t11"), V("nm"), V("kb"), A.mult)
+                actb(V("dex"), V("t11"), col(M1000))
+
         if rnd == 0:
             if left[0]:
                 ts(lst(L_EI, 16), CP_EI, col(R7), A.add)
-            ms(V("ag", 32, 40), 0.0)
-            ms(col(M1000), -1000.0)
             meet_consts()
             if not all(left):
                 actb(V("kb"), V("kb"), col(C16P))
-        if left[rnd]:
-            ts(V("ag", 0, 32), q, col(C16P), A.add)
-            tt(V("adf"), V("ag", 0, 32), V("ag", 1, 33), A.subtract)
-            cp(V("adf", 7, 32, 8), V("ag", 7, 32, 8))
-            cp(V("dex"), IND(V("adf"), lst(L_EI, 16)))
-        else:
-            tt(V("nm"), IND(q, lst(L_EI, 16)), V("nk"), A.is_equal)
-            tt(V("t11"), V("nm"), V("kb"), A.mult)
-            actb(V("dex"), V("t11"), col(M1000))
-        if rnd == 0:
-            slot_consts()
+        weave(own_half, word_half)
         pw = V("pw%d" % rnd)
         arrival(rnd, "w")
         if rnd == 0:
@@ -491,26 +535,33 @@ def rank_program(g, core, T, topo):
             tt(V("pq"), V("t32"), V("pev"), A.add)
             pw = V("pq")
         tt(V("pu", 0, 64), IND(pw, lst(L_U, 4)), V("own", 0, 64), A.add)
-        tt(V("lead", 0, 64), IND(pw, lst(L_V, 4)), V("pu", 0, 64), A.is_lt)
-        act(V("lcx"), IND(V("lead", 0, 64), lst(L_LCX, 16)))
         tt(V("pu", 64, 192), IND(pw, lst(L_U + 4, 8)), V("own", 64, 192), A.add)
+        tt(V("lead", 0, 64), IND(pw, lst(L_V, 4)), V("pu", 0, 64), A.is_lt)
+        for hf in range(2):
+            act(hv("lcx", hf), IND(V("lead", 0, 64), lst(L_LCX + 8 * hf, 8)))
         tt(V("lead", 64, 192), IND(pw, lst(L_V + 4, 8)), V("pu", 64, 192), A.is_lt)
         scan(V("rw2", 0, 64), V("lead", 64, 128), V("lead", 128, 192), 0.0, A.mult, A.max)
         tt(V("rw2", 2, 64, 8), V("rw2", 2, 64, 8), V("rw2", 5, 64, 8), A.max)
         act(V("rxx"), IND(V("rw2", 0, 64), lst(L_RX, 16)))
-        tt(V("t5"), IND(V("rw2", 0, 64), lst(L_RI, 16)), V("lcx"), A.mult)
-        scan(V("tt"), V("k4"), V("t5"), 0.0, A.mult, A.max)
-        tt(V("t7"), IND(V("tt"), lst(L_TI, 16)), V("rxx"), A.mult)
-        scan(V("rw2", 64, 320), V("k4"), V("t7"), 0.0, A.mult, A.max)
-        tt(V("t9"), IND(V("rw2"), PI), V("sgn"), A.mult)
-        scan(V("pos"), V("k8"), V("t9"), 0.0, A.mult, A.add)
-        if left[rnd]:
-            tt(V("nm"), IND(V("pos"), EI8), V("kk"), A.not_equal)
-            scan(V("nw"), V("nm"), V("dex"), 0.0, A.mult, A.add)
-        else:
-            tt(V("t11"), IND(V("pos"), EI8), V("dex"), A.add)
-            scan(V("nw"), V("k8"), V("t11"), 0.0, A.mult, A.max)
+
+        def closure(hf):
+            tt(hv("t5", hf), IND(V("rw2", 0, 64), lst(L_RI + 8 * hf, 8)), hv("lcx", hf), A.mult)
+            scan(hv("tt", hf), hv("k4", hf), hv("t5", hf), 0.0, A.mult, A.max)
+            tt(hv("t7", hf), hind("tt", L_TI, hf), hv("rxx", hf), A.mult)
+            scan(hv("rw2", hf, 64), hv("k4", hf), hv("t7", hf), 0.0, A.mult, A.max)
+            tt(hv("t9", hf), hind("rw2", L_PI, hf, 64), hv("sgn", hf), A.mult)
+            scan(hv("pos", hf), hv("k8", hf), hv("t9", hf), 0.0, A.mult, A.add)
+            if left[rnd]:
+                tt(hv("nm", hf), hind("pos", L_EI8, hf), hv("kk", hf), A.not_equal)
+                scan(hv("nw", hf), hv("nm", hf), hv("dex", hf), 0.0, A.mult, A.add)
+            else:
+                tt(hv("t11", hf), hind("pos", L_EI8, hf), hv("dex", hf), A.add)
+                scan(hv("nw", hf), hv("k8", hf), hv("t11", hf), 0.0, A.mult, A.max)
+
+        weave(lambda: closure(0), lambda: closure(1))
+        tt(V("mv"), V("pos", 7, 256, 8), V("k2"), A.not_equal)
         tr(V("wl"), V("nw", 7, 256, 8))
+        scan(V("pp"), V("cmin"), V("mv"), 1000.0, A.min, A.add)
         cp(V("w16"), V("wl", 0, 24))
         for t in range(4):
             act(V("z", t, 4 * C, 4), IND(V("xh", C * t, C * t + C), V("w16")))
@@ -518,10 +569,9 @@ def rank_program(g, core, T, topo):
             act(V("z32", C * b, C * b + C), V("z", b, 4 * C, 4), 32.0)
         if rnd == 0:
             load("s", V("vt"), T.v[:], after=[V("w16")])
-        tt(V("mv"), V("pos", 7, 256, 8), V("k2"), A.not_equal)
-        scan(V("pp"), V("cmin"), V("mv"), 1000.0, A.min, A.add)
         tt(V("tp", 32, 64), V("pp"), V("mv"), A.mult)
         cp(V("tp", 0, 32), IND(V("pp"), V("tot")))
+        cp(V("wt"), V("nw", 7, 256, 8))
         tr(V("tpt"), V("tp"))
         scan(V("base", 1, 24), V("tpt", 0, 23), V("k1000", 0, 23), -617.0, A.add, A.subtract)
         tt(V("d0", 1, 48, 2), V("base"), V("tpt", 32, 56), A.add)
@@ -529,16 +579,15 @@ def rank_program(g, core, T, topo):
         scan(V("mm"), V("d0"), V("d1"), 0.0, A.min, A.max)
         cp(V("idx"), V("mm", 1, 48, 2))
         scat(V("ew"), V("idx"), V("irl"))
-        scan(V("esn"), V("cbig"), V("ew", C, YW), 0.0, A.add, A.min)
-        cp(V("e16"), V("esn", 15, TS, 16))
         if last:
-            cp(V("wt"), V("nw", 7, 256, 8))
             for gr in range(8):
                 a, y = gr // 2, gr % 2
                 store("s", T.op[gr:gr + 1, :], T.wt[32 * a:32 * a + 24, 16 * y:16 * y + 16], [V("wt")])
         pieces = [(0, 0, H, 0), (0, H, C, 3072), (1, 0, C, 512), (2, 0, C, 1024), (3, 0, C, 1536)]
         for hf in range(2):
             quant(V("zq", H * hf, H * hf + H), V("zs", H * hf, H * hf + H), V("z", 4 * H * hf, 4 * H * hf + 4 * H))
+        scan(V("esn"), V("cbig"), V("ew", C, YW), 0.0, A.add, A.min)
+        cp(V("e16"), V("esn", 15, TS, 16))
         for b, lo, hi, bank in pieces:
             mm(V("ps", bank, bank + hi - lo), V("wq", 128 * b, 128 * b + 128), V("wsc", 128 * b, 128 * b + 128), V("zq", lo, hi), V("zs", lo, hi))
         for b, lo, hi, bank in pieces:
@@ -558,40 +607,33 @@ def rank_program(g, core, T, topo):
             if any(left) and not left[0]:
                 ts(V("maskl"), V("b8"), col(R1), A.not_equal, -BIG, A.mult)
         if not last:
-            cp(V("wt"), V("nw", 7, 256, 8))
             act(V("hw"), IND(V("hrl"), V("w16")))
             iota(V("ew", C, YW), [[0, TS]], C - 1)
             prepare(rnd + 1, "ev", "ed")
-            if not left[rnd + 1]:
-                prepare_mask()
-            prepare_lists()
+            if left[rnd + 1]:
+                prepare_lists()
+            else:
+                weave(prepare_mask, prepare_lists)
         else:
             quant(V("vq"), V("vs"), V("vt"))
         arrival(rnd, "qs")
-        for b in range(4):
+        for b in (0, 3, 1, 2):
             mm(V("ps", 512 * b, 512 * b + TS), V("eq", 128 * b, 128 * b + 128), V("es", 128 * b, 128 * b + 128),
                V("lq%d" % rnd), V("ls%d" % rnd))
-
-        def pick(eng, b, hf):
-            out = V("xs", 4 * H * hf + b, 4 * H * hf + 4 * H, 4)
-            src = IND(V("ym", YW * b, YW * b + YW), V("idx", 12 * hf, 12 * hf + 12))
-            if eng == "a":
-                act(out, src, 0.03125)
-            else:
-                ts(out, src, 0.03125, A.mult)
-
-        for b in range(4):
+        for b in (0, 3, 1, 2):
             tt(V("ym", YW * b + C, YW * b + YW), V("ps", 512 * b, 512 * b + TS), V("f16", b, 4 * TS, 4), A.add)
-            if b < 3:
-                pick("a", b, 0)
-        pick("v", 3, 0)
-        pick("a", 0, 1)
-        pick("a", 1, 1)
-        pick("v", 3, 1)
+            if b < 2:
+                pick("a", b, 0, 12)
+        pick("v", 3, 0, 12)
+        pick("v", 2, 0, 12)
+        pick("a", 0, 12, 24)
+        pick("a", 1, 12, 24)
+        pick("v", 3, 12, 24)
         product("xs", 0, last)
         if last:
             store("s", T.oc[:, 0:4 * H], T.xq[:, 0:H].bitcast(dt.uint8), [V("xq", 0, H)])
-        pick("v", 2, 1)
+        pick("v", 2, 12, 18)
+        pick("a", 2, 18, 24)
         product("xs", 1, last)
         fetch(0, last)
         fetch(1, last)

@@ -3,7 +3,9 @@ from concourse.mybir import dt, AluOpType, ActivationFunctionType
 
 C, TS, NR = 384, 160, 3
 H = C // 2
-YW = C + TS
+YW = TS + C
+SEG, NP = 9, 224
+EW = 1200
 BIG = 1.0e29
 BF, F32, I32, U16, Q4, U8 = "bfloat16", "float32", "int32", "uint16", "float8_e4m3fn_x4", "uint8"
 
@@ -22,29 +24,48 @@ def _decl(kind, names, into=None):
 
 
 _decl(BF, "x0:1536 xs:1536 ut:512 vt:512 et:2048 xh:1536 z:1536 z32:1536 ym:2176 f:640 f16:640 "
-          "qt0:32 qt1:32 qt2:32 pw0:32 pw1:32 pw2:32 rw:32 ft:32 ft0:32 pq:32 ev:32 ed:32 ev0:32 ed0:32 pev:32 ped:32 rev:32 red:32 "
-          "t32:32 oa:192 ob:192 own:192 pu:192 lead:192 lcx:256 rxx:256 "
-          "rw2:320 t5:256 tt:256 t7:256 t9:256 pos:256 nm:256 fl:192 fsn:256 mkb:192 idn:128")
-_decl(F32, "irl:384 hrl:384 hw:384 ext:384 exs:384 s:384 sb:192 maskl:192 maskr:192 col:48 "
-           "wl:32 wt:32 vl:32 iv:256 ag:40 adf:32 dex:256 t11:256 nw:256 mv:32 pp:32 tp:64 tpt:64 "
-           "base:24 d0:48 d1:48 mm:48 ew:544 esn:160 yo:384")
-_decl(BF, "j16:384 dm:384 k16:384 k8:256 k4:256 ones:384 b8:192 kl:256 nk:256 kk:256 gij:256 sgn:256 k2:32 fone:192", "cb")
-_decl(F32, "kg:256 kb:256 cp:160 c16:24 cmin:32 k1000:24 cbig:160 pa:160", "cf")
-_decl(I32, "pin:24 hin:24 pidx:1 coli:8 qi:32 par:32 pl:24 pb:24")
-_decl(U16, "lst:180 w16:24 h16:24 xh16:96 lab:24 idx:24 e16:10 tot:2")
+          "qt0:32 qt1:32 qt2:32 pw0:32 pw1:32 pw2:32 rw:32 ft0:32 ev0:32 ed0:32 pev:32 ped:32 rev:32 red:32")
+_decl(BF, "pq:32 ev:32 ed:32 t32:32 oa:192 own:192 pu:192 lead:192 rr:64 pg:128 kp:128 ps2:160 lm:64 nl:64 tn:128 tb:128 "
+          "rl:128 d1:128 fin:128 fs:128 nm:256 iv:256 fl:224 fsn:288 cc:288 mkb:224 vl:32 wr:32 pb:32 pb0:32 e1:32 v8:32 mv:32 idn:128", "wb")
+_decl(F32, "irl:384 hrl:384 hw:384 s:384 ew:1200 yo:384")
+_decl(F32, "ext:448 exs:448 sb:224 maskl:224 maskr:224 col:64 wl:32 wt:32 ag:40 adf:32 dex:256 t11:256 nw:256 pp:32 uu:32 "
+           "tp:64 tpt:64 base:24 sl:24 i1:24 i2:24 i3:24 esn:160 tab:16 tabn:16 tmp:64 lsf:160", "wf")
+_decl(BF, "j16:448 dm:448 k16:448 k8:256 k4:64 kbig:64 ones:256 t9:225 b9:224 nk:256 kk:256 cg:64 k2:32 fone:192", "cb")
+_decl(F32, "blk:32 rows:96 c16:28 negk:32 k160:24 six:24 cbig:160", "cf")
+_decl(I32, "pin:24 hin:24 pidx:1 coli:16 cq:14 tabi:16 taba:16")
+_decl(U16, "lst:160 w16:24 h16:24 xh16:96 lab:28 idx:24 sl16:24 e16:10")
 _decl(Q4, "wq:512 uq:128 uq2:128 vq:128 xq:384 zq:384 eq:512 fq0:160 fq1:160 fq2:160 lq0:160 lq1:160 lq2:160 rq:160")
 _decl(U8, "wsc:512 us:128 us2:128 vs:128 xsc:384 zs:384 es:512 fs0:160 fs1:160 fs2:160 ls0:160 ls1:160 ls2:160 rsc:160")
 SCRATCH["ps"] = ("psum", [128, 4096], F32)
 PLACE["ps"] = ("ps", 0, 4096, F32)
 
-POOL = {"v": 40, "a": 24, "t": 12, "g": 16, "dma": 10}
+POOL = {"v": 60, "a": 30, "t": 12, "g": 20, "dma": 10}
 SEMAPHORES = (["%s%d" % (e, i) for e in POOL for i in range(POOL[e])]
               + ["ae0", "aw0", "aw1", "aw2", "af0", "af1", "af2", "rea", "rda", "rwa", "rqa", "rsa", "sent", "outs"])
 
 A = AluOpType
 ACT = ActivationFunctionType
 
-L_PL, L_EI, L_EC, L_UP, L_U, L_V, L_LCX, L_RI, L_TI, L_RX, L_PI, L_EI8 = 0, 24, 40, 52, 60, 72, 84, 100, 116, 132, 148, 164
+LISTS = {}
+for _name, _n in [("pl", 28), ("ec", 14), ("ei", 16), ("up", 8), ("u", 12), ("v", 12), ("pg", 4), ("rank", 4), ("turn", 4),
+                  ("relr", 4), ("rell", 4), ("addr", 4), ("addl", 4), ("topr", 4), ("topl", 4), ("pos", 16), ("mv", 2), ("tot", 2)]:
+    LISTS[_name] = (sum(n for _, n in LISTS.values()), _n)
+
+TABLES = {
+    "to": [1, 2, 3, 2, 3, 1, 3, 1],
+    "link": [1, 1, 2, 2, 2, 0, 3, 1],
+    "direct": [0, 0, 0, 1, 1, 1, 2, 2],
+    "count": [2, 0, 1, 7, 7, 4, 3, 0, 1, 3, 6, 7, 2, 5, 4, 6],
+    "by": [0, 0, 0, 1, 0, 0, 1, 2, 0, 0, 0, 1, 2, 3, 0, 0],
+    "relr": [7, 7, 0, 7, 7, 1, 3, 7, 7, 2, 5, 4, 6, 7, 7, 7],
+    "rell": [7, 7, 6, 7, 7, 4, 3, 7, 7, 2, 5, 1, 0, 7, 7, 7],
+    "addr": [0, 5, 4, 1, 5, 4, 4, 2, 5, 4, 4, 4, 4, 3, 5, 5],
+    "addl": [3, 5, 4, 2, 5, 4, 4, 1, 5, 4, 4, 4, 4, 0, 5, 5],
+    "data": [1, 0, 0, 1, 0, 0, 0, 1, 0, 0, 0, 0, 0, 1, 0, 0],
+    "end2": [6, 3, 1, 0, 0, 1, 3, 6],
+    "end1": [1, 1, 1, 0, 0, 1, 1, 1],
+}
+NEGATED = [0, 1, 2, 3, 4, 5, 6, 10, 11]
 
 KINDS = {"e": ("ev%d", "pev", "ae%d", "rev", "rea"), "d": ("ed%d", "ped", "ae%d", "red", "rda"),
          "w": ("qt%d", "pw%d", "aw%d", "rw", "rwa"),
@@ -113,6 +134,41 @@ def IND(win, off):
     return ("ind", win, off)
 
 
+def count(v):
+    return 16 * count(v[2]) if v[0] == "ind" else len(range(*v[1:]))
+
+
+CYCLE, WAKE, LOAD, PASSES = 1.04, 120.0, 1200.0, 3
+HOP = {"ed": 2000.0, "w": 1350.0, "qs": 2300.0}
+
+
+def length(eng, kind, form, writes, reads):
+    if kind != "c":
+        return 0.0 if kind == "arrive" else 100.0
+    n = count(reads[1] if form == "scatter" else writes[0])
+    full = [v for v in writes + reads if isinstance(v, tuple) and count(v) == n]
+    if eng == "t":
+        return 0.63 * (n + 16)
+    if eng == "g":
+        return 130 + 2 * CYCLE * n
+    if form == "pack":
+        return 12 + 0.88 * n
+    if form == "scatter":
+        return 50 + 3.8 * CYCLE * n
+    if any(v[0] == "ind" for v in full):
+        return (65 if eng == "a" else 50) + 1.56 * CYCLE * n
+    if eng == "a":
+        return 65 + CYCLE * n
+    if form == "two":
+        return CYCLE * max(64, n if any(v[0] == "ps" for v in full) else 2 * n)
+    return CYCLE * max(64, n / 2 if all(PLACE[v[0]][3] in (BF, U16) for v in full) else n)
+
+
+def octal(digits):
+    n = sum(d << 3 * i for i, d in enumerate(digits))
+    return n - (1 << 24) if n >= 1 << 23 else n
+
+
 def rank_program(g, core, T, topo):
     rank = T.rank_of(core)
     if rank is None:
@@ -137,20 +193,20 @@ def rank_program(g, core, T, topo):
                 out += [v[1], v[2]] if v[0] == "ind" else [v]
         return out
 
-    def add(eng, fn, writes, reads, kind="c", sem=None):
+    def add(eng, fn, writes, reads, kind="c", sem=None, form=None, lag=0.0):
         w, r = regions(writes), regions(reads)
         banks = [("ps", v[1] // 512 * 512, v[1] // 512 * 512 + 512, 1) for v in w + r if v[0] == "ps"]
         ops.append({"eng": eng, "fn": fn, "w": [v for v in w if v[0] != "ps"] + banks, "r": [v for v in r if v[0] != "ps"],
-                    "kind": kind, "sem": sem})
+                    "kind": kind, "sem": sem, "len": length(eng, kind, form, writes, reads), "lag": lag})
 
     def cp(out, in_):
         add("v", lambda: g.vector.tensor_copy(ap(out), ap(in_)), [out], [in_])
 
     def scat(win, off, in_):
-        add("v", lambda: g.vector.tensor_copy(ap(IND(win, off)), ap(in_)), [win], [off, in_])
+        add("v", lambda: g.vector.tensor_copy(ap(IND(win, off)), ap(in_)), [win], [off, in_], form="scatter")
 
     def tt(out, a, b, op):
-        add("v", lambda: g.vector.tensor_tensor(ap(out), ap(a), ap(b), op), [out], [a, b])
+        add("v", lambda: g.vector.tensor_tensor(ap(out), ap(a), ap(b), op), [out], [a, b], form="two")
 
     def ts(out, a, s1, op0, s2=None, op1=None):
         if op1 is None:
@@ -159,7 +215,7 @@ def rank_program(g, core, T, topo):
             add("v", lambda: g.vector.tensor_scalar(ap(out), ap(a), ap(s1), ap(s2), op0, op1), [out], [a, s1, s2])
 
     def scan(out, d0, d1, init, op0, op1):
-        add("v", lambda: g.vector.tensor_tensor_scan(ap(out), ap(d0), ap(d1), init, op0, op1), [out], [d0, d1])
+        add("v", lambda: g.vector.tensor_tensor_scan(ap(out), ap(d0), ap(d1), ap(init), op0, op1), [out], [d0, d1, init])
 
     def tr(out, in_):
         add("v", lambda: g.vector.transpose(ap(out), ap(in_)), [out], [in_])
@@ -168,16 +224,16 @@ def rank_program(g, core, T, topo):
         add("v", lambda: g.vector.memset(ap(out), val), [out], [])
 
     def quant(q, sc, in_):
-        add("v", lambda: g.vector.quantize_mx(ap(q), ap(sc), ap(in_)), [q, sc], [in_])
+        add("v", lambda: g.vector.quantize_mx(ap(q), ap(sc), ap(in_)), [q, sc], [in_], form="pack")
 
-    def act(out, in_, scale=None):
-        if scale is None:
+    def act(out, in_, scale=None, bias=None):
+        if bias is not None:
+            add("a", lambda: g.scalar.activation(ap(out), ap(in_), ACT.Identity, bias=ap(bias), scale=1.0 if scale is None else ap(scale)),
+                [out], [in_, bias, scale])
+        elif scale is None:
             add("a", lambda: g.scalar.activation(ap(out), ap(in_), ACT.Copy), [out], [in_])
         else:
             add("a", lambda: g.scalar.activation(ap(out), ap(in_), ACT.Copy, scale=scale), [out], [in_])
-
-    def actb(out, in_, bias):
-        add("a", lambda: g.scalar.activation(ap(out), ap(in_), ACT.Identity, bias=ap(bias)), [out], [in_, bias])
 
     def mm(out, lq, ls, rq, rs):
         add("t", lambda: g.tensor.matmul_mx(ap(out), ap(lq), ap(ls), ap(rq), ap(rs), True, True), [out], [lq, ls, rq, rs])
@@ -187,10 +243,11 @@ def rank_program(g, core, T, topo):
         add("g", lambda: g.iota(ap(out), pattern, base, cm, allow_small_or_imprecise_dtypes=small), [out], [])
 
     def load(eng, out, src, as_codes=False, after=()):
-        add(eng, lambda: queues[eng].dma_start(ap(out).bitcast(dt.uint8) if as_codes else ap(out), src), [out], list(after), kind="dma")
+        add(eng, lambda: queues[eng].dma_start(ap(out).bitcast(dt.uint8) if as_codes else ap(out), src), [out], list(after), kind="dma",
+            lag=LOAD + count(out) * (4 if as_codes else 2))
 
     def store(eng, dst, src_ap, reads):
-        add(eng, lambda: queues[eng].dma_start(dst, src_ap), [], reads, kind="out")
+        add(eng, lambda: queues[eng].dma_start(dst, src_ap), [], reads, kind="out", lag=LOAD)
 
     sent = [0]
 
@@ -221,13 +278,23 @@ def rank_program(g, core, T, topo):
     def arrival(rnd, kinds):
         src = partner_of(T, rank, rnd)
         n = sum(engines_in(topo.mask(relay_of(topo, src, core, k) or src, core)) for k in kinds)
-        add(None, None, [V(names_of(k, rnd)[1]) for k in kinds], [], kind="arrive", sem=(names_of(kinds[0], rnd)[2], n))
+        hops = 1 if topo.may_write(src, core) else 2
+        add(None, None, [V(names_of(k, rnd)[1]) for k in kinds], [], kind="arrive", sem=(names_of(kinds[0], rnd)[2], n),
+            lag=hops * HOP[kinds])
 
-    def col(i):
+    cols = {}
+
+    def col(name):
+        i = cols.setdefault(name, len(cols))
         return V("col", i, i + 1)
 
-    def lst(a, n):
-        return V("lst", a, a + n)
+    def tab(name):
+        i = list(TABLES).index(name)
+        return V("tab", i, i + 1)
+
+    def lst(name, a=0, n=None):
+        at, all_ = LISTS[name]
+        return V("lst", at + a, at + a + (all_ - a if n is None else n))
 
     def weave(*parts):
         chains = []
@@ -239,74 +306,94 @@ def rank_program(g, core, T, topo):
         for i in range(max(len(c) for c in chains)):
             ops.extend(c[i] for c in chains if i < len(c))
 
-    R_, R1, HI, LO, R3, R7, C5 = range(7)
-    C16P, R38, PF, RP = 8, 9, 10, 11
-    M1000 = 40
     left = [rank & (1 << rnd) == 0 for rnd in range(NR)]
-    CP_PL, CP_EI, CP_EC, CP_8, CP_LC, CP_16, CP_TI, CP_I, CP_48 = [V("cp", a, b) for a, b in [
-        (0, 24), (24, 40), (40, 52), (52, 56), (56, 72), (72, 88), (88, 104), (104, 120), (120, 136)]]
+    ROW_EI, ROW_IN, ROW_8, ROW_16, ROW_POS, ROW_32 = [V("rows", a, b) for a, b in [(0, 16), (16, 20), (20, 24), (24, 28), (32, 48), (48, 50)]]
+    FIELDS = {"r": (0, 15), "pair": (1, 7), "s": (0, 7), "r8": (3, 1), "c": (0, 31), "hi": (2, 3), "lo": (0, 3),
+              "b0": (0, 1), "b1": (1, 1), "b2": (2, 1)}
+    for name in FIELDS:
+        col(name)
+
+    def fields(a, b):
+        for i, (sh, m) in list(enumerate(FIELDS.values()))[a:b]:
+            ts(V("coli", i, i + 1), V("pidx"), sh, A.logical_shift_right, m, A.bitwise_and)
+        cp(V("col", a, b), V("coli", a, b))
 
     load("s", V("pin"), T.p[:])
     load("a", V("hin"), T.h[:])
     load("a", V("ut"), T.u[:])
-    load("s", V("x0"), T.x[:])
+    load("s", V("x0", 0, 4 * H), T.x[:, 0:4 * H])
+    load("s", V("x0", 4 * H, 4 * C), T.x[:, 4 * H:4 * C])
 
     iota(V("pidx"), [[1, 1]], 0, 1)
-    iota(V("c16"), [[16, 24]])
-    if not left[0]:
-        iota(CP_EI, [[8, 4], [0, 4]])
-        iota(V("kl"), [[0, 2], [1, 16], [0, 8]])
+    iota(V("c16"), [[16, 28]])
     iota(V("irl"), [[1, C]])
-    iota(CP_PL, [[1, 2], [32, 12]])
-    if not left[0]:
-        iota(CP_EC, [[2, 12]])
+    iota(ROW_EI, [[8, 4], [0, 4]])
+    iota(V("blk"), [[0, 2], [8, 2], [0, 8]])
+    iota(V("kk"), [[0, 4], [1, 8], [0, 8]])
+    iota(V("t9"), [[0, 25], [1, SEG]], -1)
+    iota(V("j16"), [[0, 28], [1, 16]])
 
-    ms(V("wl"), 0.0)
     ms(V("k16"), 1.0)
-    ms(V("k8"), 1.0)
-    ms(V("ones"), 1.0)
-    for i, (sh, m) in enumerate([(0, 15), (1, 7), (2, 3), (0, 3), (3, 1), (0, 7), (0, 31)]):
-        ts(V("coli", i, i + 1), V("pidx"), sh, A.logical_shift_right, m, A.bitwise_and)
-    ms(V("k16", 0, C, 16), 0.0)
-    ms(V("k8", 0, 256, 8), 0.0)
-    cp(V("col", 0, 7), V("coli", 0, 7))
-    scan(V("j16"), V("k16"), V("ones"), 0.0, A.mult, A.add)
-    ts(col(C16P), col(C5), 16.0, A.mult)
-    ts(col(RP), col(R_), 1.0, A.add)
-    ts(col(R38), col(R3), 8.0, A.mult, 10.0, A.add)
-    ts(col(R1), col(R1), 1.0, A.add)
-    scan(V("b8"), V("k8", 0, H), V("ones", 0, H), 0.0, A.mult, A.add)
-    ts(V("dm"), V("j16"), col(RP), A.is_equal)
-    cp(lst(L_UP, 8), V("c16", 0, 8))
-    ms(V("fsn", H, 256), 0.0)
+    ms(V("wl", 24, 32), 0.0)
+    fields(0, 5)
+    ms(V("k16", 0, 2 * NP, 16), 0.0)
+    ms(V("cc"), 0.0)
+    cp(lst("up"), V("c16", 0, 8))
+    ts(col("16c"), col("c"), 16.0, A.mult)
+    ts(V("dm"), V("j16"), col("r"), A.is_equal)
+    ms(V("cc", 0, 288, SEG), 1.0)
+    ms(V("fsn", NP, 288), 0.0)
+    act(V("blk"), V("blk"), bias=col("16c"))
+    ts(lst("ei"), ROW_EI, col("s"), A.add)
+    if not all(left):
+        ms(V("ones"), 1.0)
 
-    def right_consts():
-        actb(V("kg"), V("kl"), col(C16P))
+    def pair_lists():
+        j, e = V("tmp", 0, 14), V("tmp", 16, 30)
+        ts(j, V("c16", 0, 14), col("r"), A.add)
+        ts(V("cq"), j, -4.0, A.add, 1.0 / SEG, A.mult)
+        tt(e, j, V("cq"), A.subtract)
+        ts(j, e, 2.0, A.mult, -2.0, A.add)
+        ts(lst("pl", 0, 14), j, C - 2.0, A.min)
+        ts(lst("pl", 14, 14), j, C - 2.0, A.min, 1.0, A.add)
 
-    def prepare(rnd, ev, ed):
-        if left[rnd]:
-            ts(V(ev), V("wt"), col(C16P), A.subtract)
-            tt(V(ed, 0, 32, 2), V("wt", 1, 32, 2), V("wt", 0, 32, 2), A.subtract)
-            tt(V(ed, 1, 32, 2), V("wt", 0, 32, 2), V("wt", 1, 32, 2), A.subtract)
-        else:
-            tt(V("nm"), IND(V("wt"), lst(L_EI, 16)), V("kg"), A.not_equal)
-            scan(V("iv"), V("nm"), V("ones", 0, 256), 0.0, A.mult, A.add)
-            cp(V("qi"), V("iv", 7, 256, 8))
-            cp(V(ev), V("iv", 7, 256, 8))
-            ts(V("par"), V("qi"), 1, A.bitwise_and)
-            ts(V(ed), V("par"), 2.0, A.mult, -1.0, A.add)
+    def right_mask_consts():
+        ts(lst("ec"), V("cq"), 23.0, A.min)
+        act(col("128-4r8"), col("r8"), -4.0, 128.0)
+        act(V("b9"), V("t9", 0, NP), bias=col("128-4r8"))
 
-    def prepare_mask():
-        tr(V("vl"), V("iv", 7, 256, 8))
-        ts(V("pl"), V("vl", 0, 24), -1.0, A.mult, col(R38), A.add)
-        ts(V("pb"), V("pl"), 1, A.logical_shift_right)
-        tt(V("mkb"), IND(V("pb"), lst(L_EC, 12)), V("b8"), A.not_equal)
-        act(V("maskr"), V("mkb"), -BIG)
+    def left_mask():
+        ts(V("maskl"), V("t9", 0, NP), col("pair"), A.not_equal, BIG, A.mult)
+        act(V("maskl", 0, NP, SEG), V("t9", 0, NP, SEG), BIG)
 
-    def prepare_lists():
-        tt(V("ext"), IND(V("hw"), lst(L_PL, 24)), V("dm"), A.mult)
-        scan(V("exs"), V("k16"), V("ext"), 0.0, A.mult, A.add)
-        cp(V("lab"), V("exs", 15, C, 16))
+    def inverse():
+        tt(V("wr"), V("wt"), V("blk"), A.subtract)
+        tt(V("nm"), IND(V("wr"), lst("ei")), V("kk"), A.not_equal)
+        scan(V("iv"), V("nm"), V("ones"), 0.0, A.mult, A.add)
+
+    def left_change(ev, ed):
+        ts(ev, V("wt"), col("16c"), A.subtract, 0.0625, A.mult)
+        tt(V(ed[0], 0, 32, 2), V(ev[0], 1, 32, 2), V(ev[0], 0, 32, 2), A.subtract)
+        tt(V(ed[0], 1, 32, 2), V(ev[0], 0, 32, 2), V(ev[0], 1, 32, 2), A.subtract)
+
+    def right_change(iv, pb, ev, ed):
+        act(pb, iv, -0.5, 131.75)
+        act(V("v8"), iv, 0.125)
+        act(V("e1"), pb, -0.25, 527.0 / 16)
+        act(ev, iv, 0.0625)
+        tt(ed, V("e1"), V("v8"), A.subtract)
+
+    def right_mask():
+        tt(V("mkb"), IND(V("pb"), lst("ec")), V("b9"), A.not_equal)
+        act(V("maskr"), V("mkb"), BIG)
+        act(V("maskr", 0, NP, SEG), V("t9", 0, NP, SEG), BIG)
+
+    def score_lists():
+        for a in (NP, 0):
+            tt(V("ext", a, a + NP), IND(V("hw"), lst("pl", a // 16, 14)), V("dm", a, a + NP), A.mult)
+        for a in (NP, 0):
+            scan(V("exs", a, a + NP), V("k16", a, a + NP), V("ext", a, a + NP), 0.0, A.mult, A.add)
+        cp(V("lab"), V("exs", 15, 2 * NP, 16))
 
     def product(x, hf, last):
         a, b = H * hf, H * hf + H
@@ -318,156 +405,118 @@ def rank_program(g, core, T, topo):
         bank = 2048 + 512 * hf
         (act if hf == 0 else cp)(V("yo" if last else "s", H * hf, H * hf + H), V("ps", bank, bank + H))
 
-    def lead_consts():
-        a3, i_, k1, e5, e7, r34, u0, u1, v1, t, v0 = [col(c) for c in range(12, 23)]
-        ts(a3, col(R7), 3.0, A.is_ge)
-        ts(e5, col(R7), 5.0, A.is_equal, 3.0, A.mult)
-        ts(e7, col(R7), 7.0, A.is_equal)
-        ts(i_, col(R7), 6.0, A.is_ge, a3, A.add)
-        ts(r34, col(R3), 4.0, A.mult)
-        ms(V("fone"), 0.0)
-        ts(k1, i_, -2.0, A.mult, col(R7), A.add)
-        ts(u1, i_, r34, A.add)
-        ts(lst(L_U, 4), CP_8, col(HI), A.add)
-        ts(u0, k1, e5, A.subtract, r34, A.add)
-        ts(t, k1, i_, A.subtract, 1.0, A.is_ge)
-        ms(V("fone", 128 + 7, 192, 8), 100.0)
-        ts(v1, e7, -2.0, A.mult, u0, A.add)
-        ts(v0, t, e7, A.subtract, u0, A.add)
-        ts(lst(L_U + 4, 4), CP_8, u0, A.add)
-        ts(lst(L_U + 8, 4), CP_8, u1, A.add)
-        ts(lst(L_V, 4), CP_8, col(LO), A.add, 4.0, A.add)
-        ts(lst(L_V + 8, 4), CP_8, v1, A.add, 1.0, A.add)
-        ts(lst(L_V + 4, 4), CP_8, v0, A.add)
+    def tables():
+        fields(5, 10)
+        for i in range(3):
+            act(col("w%d" % i), col("b%d" % i), 8.0 ** -(1 << i) - 1.0, 1.0)
+        for i, t in enumerate(TABLES.values()):
+            lo, hi = octal(t[:8]), octal(t[-8:])
+            if lo == hi:
+                iota(V("tabn", i, i + 1), [[0, 1]], lo)
+            else:
+                act(V("tabn", i, i + 1), col("r8"), float(hi - lo), float(lo))
+        ts(col("w"), col("w0"), col("w1"), A.mult, col("w2"), A.mult)
+        ts(col("half"), col("w"), -0.5, A.mult, 0.5, A.add)
+        n = len(TABLES)
+        ts(V("tabi", 0, n), V("tabn", 0, n), col("w"), A.mult, col("half"), A.subtract)
+        ts(V("taba", 0, n), V("tabi", 0, n), 7, A.bitwise_and)
+        cp(V("tab", 0, n), V("taba", 0, n))
 
-    def meet_consts():
-        mx, mn, mx4, mn16, t1, t2, d1, d2, s1, s2 = [col(c) for c in range(24, 34)]
-        ts(mx, col(LO), col(HI), A.max)
-        ts(mn, col(LO), col(HI), A.min)
-        ts(d1, col(LO), col(HI), A.is_le, 8.0, A.mult)
-        ts(d2, col(LO), col(HI), A.is_ge, 8.0, A.mult)
-        ts(mx4, mx, 4.0, A.mult)
-        ts(mn16, mn, 16.0, A.mult)
-        ts(t1, col(HI), 2.0, A.mult, mx, A.add)
-        ts(t2, mn, 2.0, A.mult, col(HI), A.add)
-        ms(V("k4"), 1.0)
-        ts(lst(L_LCX, 16), CP_LC, mx4, A.add)
-        ts(s1, t1, d1, A.max, 8.0, A.min)
-        ts(s2, t2, d2, A.max, 8.0, A.min)
-        ts(lst(L_TI, 16), CP_TI, mn16, A.add)
-        ms(V("k4", 0, 256, 4), 0.0)
-        ts(lst(L_RI, 16), CP_16, s1, A.add, -1.0, A.add)
-        ts(lst(L_RX, 16), CP_16, s2, A.add, 7.0, A.add)
-        i_, lo, hi, q4, a, b, b2, w, e = [V("pa", 16 * i, 16 * i + 16) for i in range(9)]
-        ts(i_, CP_I, col(R3), A.add)
-        ts(e, CP_EI, col(R7), A.add, 8.0, A.mult)
-        ts(V("sgn"), V("gij"), -1.0, A.max, 1.0, A.min)
-        ts(lo, i_, col(R7), A.min)
-        ts(hi, i_, col(R7), A.max)
-        ts(lst(L_EI8, 16), e, 7.0, A.add)
-        ts(q4, lo, 4.0, A.is_ge, 4.0, A.mult)
-        ts(a, lo, 2.0, A.mult, -1.0, A.add)
-        ts(b, lo, 14.0, A.mult)
-        ts(b2, hi, 3.0, A.mult, 52.0, A.add)
-        ts(w, hi, 4.0, A.is_ge, 4.0, A.mult)
-        tt(a, a, hi, A.add)
-        tt(b, b, b2, A.add)
-        tt(w, w, q4, A.subtract)
-        tt(a, a, q4, A.subtract)
-        tt(b, b, CP_48, A.add)
-        ts(w, w, 0.25, A.mult)
-        tt(a, a, CP_16, A.add)
-        ms(V("tot", 0, 1), 15)
-        tt(b, b, w, A.mult)
-        ms(V("tot", 1, 2), 31)
-        ts(V("d1", 1, 48, 2), V("c16"), col(R_), A.add)
-        tt(a, a, b, A.add)
-        act(V("cbig"), V("dm", 0, TS), 1000.0)
-        ms(V("ag", 32, 40), 0.0)
-        ms(col(M1000), -1000.0)
-        cp(lst(L_PI, 16), a)
+    def lead_lists():
+        act(V("rows", 52, 56), ROW_IN, bias=col("8r8"))
+        ts(lst("u", 0, 4), V("rows", 52, 56), tab("link"), A.add)
+        ts(lst("u", 4, 4), V("rows", 52, 56), tab("direct"), A.add)
+        ts(lst("u", 8), ROW_8, col("lo"), A.add)
+        ts(lst("v", 0, 4), V("rows", 52, 56), tab("to"), A.add)
+        ts(lst("v", 4, 4), V("rows", 52, 56), tab("to"), A.add)
+        ts(lst("v", 8), ROW_8, col("hi"), A.add, 4.0, A.add)
+
+    def meet_lists():
+        for name, src, scale, bias in [
+                ("rank", col("lo"), 4.0, 3.0), ("turn", col("lo"), 4.0, col("hi")), ("topr", tab("by"), 4.0, 3.0),
+                ("topl", tab("by"), -4.0, 15.0), ("cell", tab("data"), -48.0, 51.0), ("end", tab("end2"), 2.0, tab("end1")),
+                ("addr", tab("addr"), 4.0, col("cell")), ("addl", tab("addl"), 4.0, col("cell")), ("pos", col("b2"), 64.0, col("end")),
+                ("mv", col("r8"), 16.0, col("pos")), ("399+r", col("r"), 1.0, 399.0), ("160+r", col("r"), 1.0, float(TS)),
+                ("-16c", col("c"), -16.0, -400.0), ("dex0", col("c"), 16.0, -1000.0), ("dex1", col("c"), 16.0, -992.0)]:
+            act(col(name), src, scale, bias)
+        for name, row, scale, bias in [
+                ("pg", ROW_8, 1.0, tab("count")), ("rank", ROW_16, 1.0, col("rank")), ("turn", ROW_16, 1.0, col("turn")),
+                ("relr", ROW_8, 1.0, tab("relr")), ("rell", ROW_8, 1.0, tab("rell")),
+                ("addr", ROW_16, tab("data"), col("addr")), ("addl", ROW_16, tab("data"), col("addl")),
+                ("topr", ROW_16, 1.0, col("topr")), ("topl", ROW_16, 1.0, col("topl")),
+                ("pos", ROW_POS, 1.0, col("pos")), ("mv", ROW_32, 1.0, col("mv")), ("tot", ROW_16[:2] + (26, 1), 1.0, 15.0)]:
+            act(("lsf",) + lst(name)[1:], row, scale, bias)
+        for a, b in [("pg", "addl"), ("topr", "tot")]:
+            at, end = lst(a)[1], lst(b)[2]
+            cp(V("lst", at, end), V("lsf", at, end))
+        act(V("k160"), V("c16", 0, 24), bias=col("160+r"))
+        act(V("base", 0, 1), col("399+r"))
+
+    def meet_rows():
+        iota(V("ag", 32, 40), [[0, 8]])
+        iota(V("cg"), [[0, 4], [-1, 2], [0, 8]], 1)
+        for i in range(16):
+            if (i in NEGATED) != (i < 8):
+                iota(V("cg", i, 64, 16), [[0, 4]], int(i in NEGATED))
+        iota(V("kp"), [[0, 128]], 1)
+        iota(V("kp", 0, 128, 4), [[0, 32]])
+        for at, reset in [(64, 64), (144, -64)]:
+            iota(V("ps2", at, at + 16), [[0, 2], [reset, 2], [0, 4]])
+        iota(V("k4"), [[0, 64]], 1)
+        iota(V("k4", 0, 64, 4), [[0, 16]])
+        iota(V("kbig"), [[0, 64]])
+        iota(V("kbig", 0, 64, 4), [[0, 16]], 64)
+        iota(V("k2"), [[0, 4], [1, 8]])
+        iota(V("six"), [[0, 24]], 16)
+        iota(V("ew", 0, TS), [[0, TS]], C - 1)
+        for b in range(4):
+            iota(V("et", 512 * b, 512 * b + 512), [[0, 512]])
 
     def unpack_consts():
-        cp(col(PF), V("pidx"))
-        ms(V("et"), 0.0)
-        ts(V("idn"), V("irl", 0, 128), col(PF), A.is_equal, 16.0, A.mult)
+        cp(col("p"), V("pidx"))
+        ts(V("idn"), V("irl", 0, 128), col("p"), A.is_equal, 16.0, A.mult)
         for b in range(4):
             cp(V("et", 512 * b + b, 512 * b + 512, 4), V("idn"))
-        quant(V("eq"), V("es"), V("et"))
 
     def spread_u():
-        ts(lst(L_PL, 24), CP_PL, col(R_), A.add, col(R_), A.add)
         quant(V("uq"), V("us"), V("ut"))
-        add("v", lambda: g.vector.tensor_copy(T.uq2[:].bitcast(dt.uint32), T.uq[:].bitcast(dt.uint32).indirect(ap(lst(L_UP, 8)))),
-            [V("uq2")], [V("uq"), lst(L_UP, 8)])
-        act(V("us2"), IND(V("us"), lst(L_UP, 8)))
+        add("v", lambda: g.vector.tensor_copy(T.uq2[:].bitcast(dt.uint32), T.uq[:].bitcast(dt.uint32).indirect(ap(lst("up")))),
+            [V("uq2")], [V("uq"), lst("up")])
+        act(V("us2"), IND(V("us"), lst("up")))
 
-    def first_mask():
-        if left[0]:
-            ts(V("maskl"), V("b8"), col(R1), A.not_equal, -BIG, A.mult)
-        else:
-            ts(lst(L_EC, 12), CP_EC, col(R3), A.add)
-            prepare_mask()
-
-    def first_scores():
-        product("x0", 0, False)
-        product("x0", 1, False)
-
-    if not left[0]:
-        ts(lst(L_EI, 16), CP_EI, col(R7), A.add)
-        right_consts()
-    cp(V("wl", 0, 24), V("pin"))
     cp(V("h16"), V("hin"))
     cp(V("w16"), V("pin"))
-    tr(V("wt"), V("wl"))
+    cp(V("wl", 0, 24), V("pin"))
     act(V("hrl"), IND(V("irl"), V("h16")))
     act(V("hw"), IND(V("hrl"), V("w16")))
+    tr(V("wt"), V("wl"))
     if left[0]:
-        prepare(0, "ev0", "ed0")
+        weave(lambda: left_change(V("ev0"), V("ed0")), pair_lists)
         remote_pair(0, "ed")
         spread_u()
-        first_mask()
-        prepare_lists()
-        first_scores()
+        left_mask()
     else:
-        weave(lambda: prepare(0, "ev0", "ed0"), spread_u)
+        weave(inverse, pair_lists)
+        right_mask_consts()
+        tr(V("vl"), V("iv", 7, 256, 8))
+        act(V("pb"), V("vl"), -0.5, 131.75)
+        right_change(V("iv", 7, 256, 8), V("pb0"), V("ev0"), V("ed0"))
         remote_pair(0, "ed")
-        weave(first_mask, prepare_lists)
-        first_scores()
+        spread_u()
+        right_mask()
+    product("x0", 0, False)
+    score_lists()
+    product("x0", 1, False)
     fetch(0, False)
     fetch(1, False)
-    iota(CP_8, [[8, 4]])
-    if left[0]:
-        iota(CP_EI, [[8, 4], [0, 4]])
-    iota(CP_LC, [[16, 4], [1, 4]])
-    iota(CP_16, [[16, 4], [0, 4]])
-    iota(CP_TI, [[64, 4], [4, 4]], 3)
-    iota(CP_I, [[0, 4], [2, 4]])
-    iota(CP_48, [[48, 4], [0, 4]])
-
-    def late_iotas():
-        iota(V("gij"), [[0, 4], [1, 8], [-1, 8]])
-        if not all(left):
-            iota(V("nk"), [[0, 4], [-1, 8], [0, 8]], 8)
-            for y in range(2):
-                iota(V("kb", 128 * y, 128 * y + 128), [[8, 2], [0, 8], [-1, 8]], 1007)
-        iota(V("d0"), [[0, 48]], -1000000)
-        if any(left):
-            iota(V("kk"), [[0, 4], [1, 8], [1, 8]], -7)
-        iota(V("k2"), [[0, 4], [2, 8]], -7)
-        if left[0] and not all(left):
-            iota(V("kl"), [[0, 2], [1, 16], [0, 8]])
-            iota(CP_EC, [[2, 12]])
-        iota(V("cmin"), [[0, 2], [1000, 16]], 1000)
-        iota(V("k1000"), [[0, 24]], 1000)
-        iota(V("base"), [[0, 24]], -617)
-        iota(V("ew", C, YW), [[0, TS]], C - 1)
-
-    def hv(name, hf, at=0):
-        return V(name, at + 128 * hf, at + 128 * hf + 128)
-
-    def hind(name, l, hf, at=0):
-        return IND(V(name, 0, at + 128 * hf + 128), lst(l + 8 * hf, 8))
+    iota(ROW_IN, [[4, 2], [16, 2]])
+    iota(ROW_8, [[8, 4]])
+    iota(ROW_16, [[16, 4]])
+    iota(ROW_POS, [[16, 4], [0, 4]])
+    iota(ROW_32, [[32, 2]])
+    iota(V("fone"), [[0, 192]])
+    iota(V("fone", 64 + 7, 128, 8), [[0, 8]], 2)
+    act(col("8r8"), col("r8"), 8.0)
 
     def pick(eng, b, c0, c1):
         out = V("xs", 64 * c0 + b, 64 * c1, 4)
@@ -480,148 +529,180 @@ def rank_program(g, core, T, topo):
     for rnd in range(NR):
         last = rnd + 1 == NR
         q = V("qt%d" % rnd)
-        ev, ed, ft = ("ev0", "ed0", "ft0") if rnd == 0 else ("ev", "ed", "ft")
-        for a in (0, 96):
-            tt(V("sb", a, a + 96), IND(V("s"), V("lab", 12 + a // 16, 18 + a // 16)), V("maskl" if left[rnd] else "maskr", a, a + 96), A.add)
-        for a in (0, 96):
-            tt(V("fl", a, a + 96), IND(V("s"), V("lab", a // 16, 6 + a // 16)), V("sb", a, a + 96), A.is_lt)
-        for a in (0, 96):
-            scan(V("fsn", a, a + 96), V("k8", a, a + 96), V("fl", a, a + 96), 0.0, A.mult, A.add)
-        tr(V(ft), V("fsn", 7, 256, 8))
+        for a, b in ((0, 128), (128, NP)):
+            tt(V("sb", a, b), IND(V("s"), V("lab", 14 + a // 16, 14 + b // 16)), V("maskl" if left[rnd] else "maskr", a, b), A.add)
+        for a, b in ((0, 128), (128, NP)):
+            tt(V("fl", a, b), IND(V("s"), V("lab", a // 16, b // 16)), V("sb", a, b), A.is_lt)
+        for a, b in ((0, 14 * SEG), (14 * SEG, NP)):
+            scan(V("fsn", a, b), V("fl", a, b), V("cc", a, b), 0.0, A.mult, A.add)
         if rnd == 0:
-            remote(rnd, "w", ft)
-            late_iotas()
+            tr(V("ft0"), V("fsn", SEG - 1, 288, SEG))
+            remote(rnd, "w", "ft0")
+            meet_rows()
             for t in range(4):
                 ts(V("xh16", 24 * t, 24 * t + 24), V("hin"), 4.0, A.mult, float(t), A.add)
             arrival(rnd, "ed")
             load("s", V("wq"), T.wc[:], as_codes=True, after=[V("pev")])
             load("s", V("wsc"), T.ws[:])
-        tt(V("t32"), V(ft), V(ed), A.mult)
-        if rnd == 0:
-            act(V("xh"), IND(V("x0"), V("xh16")))
-            lead_consts()
-        tt(q, V("t32"), V(ev), A.add)
-        if rnd > 0:
+            tt(V("t32"), V("ft0"), V("ed0"), A.mult)
+            if not all(left):
+                act(V("nk"), V("kk"), -0.0625, 0.5)
+                iota(V("k8"), [[0, 256]], 1)
+                iota(V("k8", 0, 256, 8), [[0, 32]])
+            tables()
+            tt(q, V("t32"), V("ev0"), A.add)
+            lead_lists()
+        else:
+            tr(q, V("fsn", SEG - 1, 288, SEG))
             remote(rnd, "w")
-            act(V("xh"), IND(V("xs"), V("xh16")))
+        for i in range(8):
+            act(V("xh", H * i, H * i + H), IND(V("xs" if rnd else "x0"), V("xh16", 12 * i, 12 * i + 12)))
 
         def own_half():
-            tt(V("oa"), IND(q, lst(L_U, 12)), V("fone"), A.add)
-            tt(V("ob"), IND(q, lst(L_V, 12)), V("oa"), A.is_lt)
-            ts(V("own"), V("ob"), 100.0, A.mult)
+            tt(V("oa"), IND(q, lst("u")), V("fone"), A.add)
+            tt(V("own"), IND(q, lst("v")), V("oa"), A.is_lt)
 
         def word_half():
             if left[rnd]:
-                ts(V("ag", 0, 32), q, col(C16P), A.add)
+                ts(V("ag", 0, 32), q, 16.0, A.mult, col("16c"), A.add)
                 tt(V("adf"), V("ag", 0, 32), V("ag", 1, 33), A.subtract)
                 cp(V("adf", 7, 32, 8), V("ag", 7, 32, 8))
-                cp(V("dex"), IND(V("adf"), lst(L_EI, 16)))
+                cp(V("dex"), IND(V("adf"), lst("ei")))
             else:
-                tt(V("nm"), IND(q, lst(L_EI, 16)), V("nk"), A.is_equal)
-                tt(V("t11"), V("nm"), V("kb"), A.mult)
-                actb(V("dex"), V("t11"), col(M1000))
+                tt(V("nm"), IND(q, lst("ei")), V("nk"), A.is_equal)
+                for bk in range(4):
+                    act(V("dex", 64 * bk, 64 * bk + 64), V("nm", 64 * bk, 64 * bk + 64), 1000.0, col("dex%d" % (bk % 2)))
 
         if rnd == 0:
-            if left[0]:
-                ts(lst(L_EI, 16), CP_EI, col(R7), A.add)
-            meet_consts()
-            if not all(left):
-                actb(V("kb"), V("kb"), col(C16P))
-        weave(own_half, word_half)
+            weave(own_half, meet_lists)
+            act(V("negk"), V("j16", 0, 32), -1.0, col("-16c"))
+            act(V("cbig"), V("dm", 0, TS), 1000.0)
+            word_half()
+        else:
+            weave(own_half, word_half)
         pw = V("pw%d" % rnd)
         arrival(rnd, "w")
         if rnd == 0:
             tt(V("t32"), pw, V("ped"), A.mult)
             tt(V("pq"), V("t32"), V("pev"), A.add)
             pw = V("pq")
-        tt(V("pu", 0, 64), IND(pw, lst(L_U, 4)), V("own", 0, 64), A.add)
-        tt(V("pu", 64, 192), IND(pw, lst(L_U + 4, 8)), V("own", 64, 192), A.add)
-        tt(V("lead", 0, 64), IND(pw, lst(L_V, 4)), V("pu", 0, 64), A.is_lt)
+        tt(V("pu", 0, 128), IND(pw, lst("u", 0, 8)), V("own", 0, 128), A.add)
+        tt(V("pu", 128, 192), IND(pw, lst("u", 8)), V("own", 128, 192), A.add)
+        tt(V("lead", 0, 128), IND(pw, lst("v", 0, 8)), V("pu", 0, 128), A.is_lt)
+        tt(V("lead", 128, 192), IND(pw, lst("v", 8)), V("pu", 128, 192), A.is_lt)
+        scan(V("rr"), V("lead", 0, 64), V("lead", 64, 128), 0.0, A.mult, A.max)
+        for at in (1, 13):
+            act(V("kp", at, 128, 16), V("rr", 5, 64, 8), -1.0, 1.0)
+        act(V("lm"), V("lead", 128, 192), 8.0, -7.0)
+        act(V("nl"), IND(V("lead", 128, 192), lst("turn")), -4.0, 4.0)
+        act(V("rl", 64, 128), IND(V("rr", 32, 64), lst("relr")))
+        act(V("rl", 0, 64), IND(V("rr", 0, 32), lst("rell")), -4.0, 4.0)
         for hf in range(2):
-            act(hv("lcx", hf), IND(V("lead", 0, 64), lst(L_LCX + 8 * hf, 8)))
-        tt(V("lead", 64, 192), IND(pw, lst(L_V + 4, 8)), V("pu", 64, 192), A.is_lt)
-        scan(V("rw2", 0, 64), V("lead", 64, 128), V("lead", 128, 192), 0.0, A.mult, A.max)
-        tt(V("rw2", 2, 64, 8), V("rw2", 2, 64, 8), V("rw2", 5, 64, 8), A.max)
-        act(V("rxx"), IND(V("rw2", 0, 64), lst(L_RX, 16)))
+            tt(V("pg", 64 * hf, 64 * hf + 64), IND(V("rr", 32 * hf, 32 * hf + 32), lst("pg")), V("cg"), A.not_equal)
+        for hf in range(2):
+            scan(V("ps2", 80 * hf, 80 * hf + 64), V("kp", 64 * hf, 64 * hf + 64), V("pg", 64 * hf, 64 * hf + 64), 0.0, A.mult, A.add)
+        act(V("d1", 64, 128), IND(V("ps2", 80, 160), lst("addr")))
+        act(V("d1", 0, 64), IND(V("ps2", 0, 80), lst("addl")))
+        tt(V("tn", 0, 64), IND(V("ps2", 0, 64), lst("rank")), V("lm"), A.add)
+        tt(V("tn", 64, 128), IND(V("ps2", 80, 144), lst("rank")), V("nl"), A.max)
+        scan(V("tb", 0, 64), V("k4"), V("tn", 0, 64), 0.0, A.mult, A.max)
+        scan(V("tb", 64, 128), V("kbig"), V("tn", 64, 128), 0.0, A.add, A.min)
+        tt(V("fin", 64, 128), IND(V("tb", 0, 64), lst("topr")), V("rl", 64, 128), A.mult)
+        tt(V("fin", 0, 64), IND(V("tb", 64, 128), lst("topl")), V("rl", 0, 64), A.max)
+        scan(V("fs", 64, 128), V("fin", 64, 128), V("d1", 64, 128), 0.0, A.max, A.add)
+        scan(V("fs", 0, 64), V("fin", 0, 64), V("d1", 0, 64), 64.0, A.min, A.add)
 
-        def closure(hf):
-            tt(hv("t5", hf), IND(V("rw2", 0, 64), lst(L_RI + 8 * hf, 8)), hv("lcx", hf), A.mult)
-            scan(hv("tt", hf), hv("k4", hf), hv("t5", hf), 0.0, A.mult, A.max)
-            tt(hv("t7", hf), hind("tt", L_TI, hf), hv("rxx", hf), A.mult)
-            scan(hv("rw2", hf, 64), hv("k4", hf), hv("t7", hf), 0.0, A.mult, A.max)
-            tt(hv("t9", hf), hind("rw2", L_PI, hf, 64), hv("sgn", hf), A.mult)
-            scan(hv("pos", hf), hv("k8", hf), hv("t9", hf), 0.0, A.mult, A.add)
+        def new_word(hf):
+            a, b = 128 * hf, 128 * hf + 128
+            at = IND(V("fs"), lst("pos", 8 * hf, 8))
             if left[rnd]:
-                tt(hv("nm", hf), hind("pos", L_EI8, hf), hv("kk", hf), A.not_equal)
-                scan(hv("nw", hf), hv("nm", hf), hv("dex", hf), 0.0, A.mult, A.add)
+                tt(V("nm", a, b), at, V("kk", a, b), A.not_equal)
+                scan(V("nw", a, b), V("nm", a, b), V("dex", a, b), 0.0, A.mult, A.add)
             else:
-                tt(hv("t11", hf), hind("pos", L_EI8, hf), hv("dex", hf), A.add)
-                scan(hv("nw", hf), hv("k8", hf), hv("t11", hf), 0.0, A.mult, A.max)
+                tt(V("t11", a, b), at, V("dex", a, b), A.add)
+                scan(V("nw", a, b), V("k8", a, b), V("t11", a, b), 0.0, A.mult, A.max)
 
-        weave(lambda: closure(0), lambda: closure(1))
-        tt(V("mv"), V("pos", 7, 256, 8), V("k2"), A.not_equal)
+        weave(lambda: new_word(0), lambda: new_word(1))
+        tt(V("mv"), IND(V("fs"), lst("mv")), V("k2"), A.not_equal)
         tr(V("wl"), V("nw", 7, 256, 8))
-        scan(V("pp"), V("cmin"), V("mv"), 1000.0, A.min, A.add)
+        scan(V("pp"), V("k16", 0, 32), V("mv"), 0.0, A.mult, A.add)
         cp(V("w16"), V("wl", 0, 24))
-        for t in range(4):
-            act(V("z", t, 4 * C, 4), IND(V("xh", C * t, C * t + C), V("w16")))
+        for hf in range(2):
+            for t in range(4):
+                act(V("z", 4 * H * hf + t, 4 * H * hf + 4 * H, 4), IND(V("xh", C * t, C * t + C), V("w16", 12 * hf, 12 * hf + 12)))
         for b in range(4):
-            act(V("z32", C * b, C * b + C), V("z", b, 4 * C, 4), 32.0)
+            act(V("z32", 4 * H + b, 4 * C, 4), V("z", 4 * H + b, 4 * C, 4), 32.0)
         if rnd == 0:
             load("s", V("vt"), T.v[:], after=[V("w16")])
-        tt(V("tp", 32, 64), V("pp"), V("mv"), A.mult)
-        cp(V("tp", 0, 32), IND(V("pp"), V("tot")))
+        tt(V("uu"), V("mv"), V("negk"), A.mult)
+        cp(V("tp", 32, 64), IND(V("pp"), lst("tot")))
+        tt(V("tp", 0, 32), V("pp"), V("uu"), A.add)
         cp(V("wt"), V("nw", 7, 256, 8))
         tr(V("tpt"), V("tp"))
-        scan(V("base", 1, 24), V("tpt", 0, 23), V("k1000", 0, 23), -617.0, A.add, A.subtract)
-        tt(V("d0", 1, 48, 2), V("base"), V("tpt", 32, 56), A.add)
-        ts(V("d1", 0, 48, 2), V("d0", 1, 48, 2), float(YW), A.subtract, -1000.0, A.mult)
-        scan(V("mm"), V("d0"), V("d1"), 0.0, A.min, A.max)
-        cp(V("idx"), V("mm", 1, 48, 2))
-        scat(V("ew"), V("idx"), V("irl"))
+        scan(V("base", 1, 24), V("tpt", 32, 55), V("six", 0, 23), col("399+r"), A.add, A.add)
+        tt(V("sl"), V("base"), V("tpt", 0, 24), A.add)
+        cp(V("sl16"), V("sl"))
+        scat(V("ew"), V("sl16"), V("irl"))
         if last:
             for gr in range(8):
                 a, y = gr // 2, gr % 2
-                store("s", T.op[gr:gr + 1, :], T.wt[32 * a:32 * a + 24, 16 * y:16 * y + 16], [V("wt")])
-        pieces = [(0, 0, H, 0), (0, H, C, 3072), (1, 0, C, 512), (2, 0, C, 1024), (3, 0, C, 1536)]
-        for hf in range(2):
-            quant(V("zq", H * hf, H * hf + H), V("zs", H * hf, H * hf + H), V("z", 4 * H * hf, 4 * H * hf + 4 * H))
-        scan(V("esn"), V("cbig"), V("ew", C, YW), 0.0, A.add, A.min)
+                store("s", T.op[gr:gr + 1, :], T.wf[32 * a:32 * a + 24, PLACE["wt"][1] + 16 * y:PLACE["wt"][1] + 16 * y + 16], [V("wt")])
+        quant(V("zq", 0, H), V("zs", 0, H), V("z", 0, 4 * H))
+        scan(V("esn"), V("cbig"), V("ew", 0, TS), 0.0, A.add, A.min)
+        ts(V("z32", 0, 4 * H), V("z", 0, 4 * H), 32.0, A.mult)
         cp(V("e16"), V("esn", 15, TS, 16))
-        for b, lo, hi, bank in pieces:
-            mm(V("ps", bank, bank + hi - lo), V("wq", 128 * b, 128 * b + 128), V("wsc", 128 * b, 128 * b + 128), V("zq", lo, hi), V("zs", lo, hi))
-        for b, lo, hi, bank in pieces:
-            tt(V("ym", YW * b + lo, YW * b + hi), V("ps", bank, bank + hi - lo), V("z32", C * b + lo, C * b + hi), A.add)
-            if hi == C and b < 3:
-                act(V("f", b, 4 * TS, 4), IND(V("ym", YW * b, YW * b + C), V("e16")), 0.03125)
-        ts(V("f", 3, 4 * TS, 4), IND(V("ym", YW * 3, YW * 3 + C), V("e16")), 0.03125, A.mult)
+        quant(V("zq", H, C), V("zs", H, C), V("z", 4 * H, 4 * C))
+        for hf in range(2):
+            for b in range(4):
+                bank = 512 * (2 * b + hf)
+                mm(V("ps", bank, bank + H), V("wq", 128 * b, 128 * b + 128), V("wsc", 128 * b, 128 * b + 128),
+                   V("zq", H * hf, H * hf + H), V("zs", H * hf, H * hf + H))
+        for b, hf in [(0, 0), (1, 0), (0, 1), (1, 1), (2, 0), (2, 1), (3, 0), (3, 1)]:
+            bank, at = 512 * (2 * b + hf), YW * b + TS + H * hf
+            tt(V("ym", at, at + H), V("ps", bank, bank + H), V("z32", 4 * H * hf + b, 4 * H * hf + 4 * H, 4), A.add)
+            if hf == 1 and b < 3:
+                act(V("f", b, 4 * TS, 4), IND(V("ym", YW * b + TS, YW * b + YW), V("e16")), 0.03125)
+        ts(V("f", 3, 4 * TS, 4), IND(V("ym", YW * 3 + TS, YW * 3 + YW), V("e16")), 0.03125, A.mult)
         quant(V("fq%d" % rnd), V("fs%d" % rnd), V("f"))
         remote(rnd, "q")
         remote(rnd, "s")
-        ts(V("f16"), V("f"), 16.0, A.mult)
+        if not last:
+            act(V("hw"), IND(V("hrl"), V("w16")))
+            iota(V("ew", 0, TS), [[0, TS]], C - 1)
+        act(V("f16"), V("f"), 16.0)
+
+        def slots():
+            ts(V("i1"), V("sl"), float(TS), A.is_ge, 1000.0, A.mult)
+            tt(V("i2"), V("i1"), V("sl"), A.add)
+            tt(V("i3"), V("i2"), V("k160"), A.min)
+            cp(V("idx"), V("i3"))
+
         if rnd == 0:
             unpack_consts()
             if left[0] and not all(left):
-                right_consts()
-                ts(lst(L_EC, 12), CP_EC, col(R3), A.add)
+                right_mask_consts()
             if any(left) and not left[0]:
-                ts(V("maskl"), V("b8"), col(R1), A.not_equal, -BIG, A.mult)
-        if not last:
-            act(V("hw"), IND(V("hrl"), V("w16")))
-            iota(V("ew", C, YW), [[0, TS]], C - 1)
-            prepare(rnd + 1, "ev", "ed")
-            if left[rnd + 1]:
-                prepare_lists()
-            else:
-                weave(prepare_mask, prepare_lists)
+                left_mask()
+        if last:
+            weave(slots, lambda: quant(V("vq"), V("vs"), V("vt")))
+        elif left[rnd + 1]:
+            weave(slots, lambda: left_change(V("ev"), V("ed")))
+            tr(V("cc", SEG - 1, 288, SEG), V("ev"))
+            tr(V("cc", 0, 288, SEG), V("ed"))
+            score_lists()
         else:
-            quant(V("vq"), V("vs"), V("vt"))
+            weave(slots, inverse)
+            tr(V("vl"), V("iv", 7, 256, 8))
+            right_change(V("vl"), V("pb"), V("cc", SEG - 1, 288, SEG), V("cc", 0, 288, SEG))
+            weave(score_lists, right_mask)
+        if rnd == 0:
+            quant(V("eq"), V("es"), V("et"))
         arrival(rnd, "qs")
         for b in (0, 3, 1, 2):
             mm(V("ps", 512 * b, 512 * b + TS), V("eq", 128 * b, 128 * b + 128), V("es", 128 * b, 128 * b + 128),
                V("lq%d" % rnd), V("ls%d" % rnd))
         for b in (0, 3, 1, 2):
-            tt(V("ym", YW * b + C, YW * b + YW), V("ps", 512 * b, 512 * b + TS), V("f16", b, 4 * TS, 4), A.add)
+            tt(V("ym", YW * b, YW * b + TS), V("ps", 512 * b, 512 * b + TS), V("f16", b, 4 * TS, 4), A.add)
             if b < 2:
                 pick("a", b, 0, 12)
         pick("v", 3, 0, 12)
@@ -647,7 +728,7 @@ def rank_program(g, core, T, topo):
     emit(g, T, ops, queues, sent[0])
 
 
-def emit(g, T, ops, queues, sent):
+def touching(ops):
     cache = {}
 
     def cols(v):
@@ -655,9 +736,7 @@ def emit(g, T, ops, queues, sent):
             cache[v] = sum(1 << i for i in range(v[1], v[2], v[3]))
         return cache[v]
 
-    hist = {}
-    known = {e: set() for e in queues}
-    at_issue, waits = [], []
+    hist, out = {}, []
     for i, op in enumerate(ops):
         deps = set()
         for v in op["w"]:
@@ -669,6 +748,61 @@ def emit(g, T, ops, queues, sent):
         for v in op["r"]:
             hist.setdefault(v[0], []).append((i, cols(v), False))
         deps.discard(i)
+        out.append(deps)
+    return out
+
+
+def arrange(ops):
+    deps = touching(ops)
+    remote = None
+    issued = {}
+    for i, op in enumerate(ops):
+        if op["kind"] in ("remote", "arrive") and remote is not None:
+            deps[i].add(remote)
+        if op["kind"] == "remote":
+            remote = i
+        if op["kind"] == "dma":
+            issued[i] = max(issued, default=None)
+    after = [[] for _ in ops]
+    for i, d in enumerate(deps):
+        for j in d:
+            after[j].append(i)
+
+    def place(order, before, forward):
+        busy, span = {}, {}
+        for i in order:
+            op = ops[i]
+            t = max([span[j][1] + WAKE for j in before[i]], default=0.0) + (0.0 if forward else op["lag"])
+            if forward and issued.get(i) in span:
+                t = max(t, span[issued[i]][0])
+            taken = busy.setdefault(op["eng"], [])
+            at = 0
+            for a, b in taken if op["eng"] else []:
+                if t + op["len"] <= a:
+                    break
+                t, at = max(t, b), at + 1
+            taken.insert(at, (t, t + op["len"]))
+            span[i] = (t, t + op["len"] + (op["lag"] if forward else 0.0))
+        return span
+
+    order, best = list(range(len(ops))), None
+    for _ in range(PASSES):
+        span = place(order, deps, True)
+        end = max(b for _, b in span.values())
+        if best is None or end < best[0]:
+            best = (end, sorted(span, key=lambda i: (span[i][0], order.index(i))))
+        back = place(sorted(span, key=lambda i: (-span[i][1], -span[i][0], -i)), after, False)
+        order = sorted(back, key=lambda i: (-back[i][1], -back[i][0], i))
+        first = [i for i in issued if not deps[i]]
+        order = first + [i for i in order if i not in first]
+    return [ops[i] for i in best[1]]
+
+
+def emit(g, T, ops, queues, sent):
+    ops = arrange(ops)
+    known = {e: set() for e in queues}
+    at_issue, waits = [], []
+    for op, deps in zip(ops, touching(ops)):
         mine = []
         if op["eng"] is not None:
             kn = known[op["eng"]]

@@ -6,7 +6,10 @@ H = C // 2
 YW = TS + C
 SEG, NP = 9, 224
 EW = 1200
-BIG = 1.0e29
+BIG, FAR = 1.0e29, 2.0 ** 46
+PARTS = [(0, 256), (256, C)]
+PICKS = ["aavv", "aaav"]
+HALVES = [(0, H), (H, C)]
 BF, F32, I32, U16, Q4, U8 = "bfloat16", "float32", "int32", "uint16", "float8_e4m3fn_x4", "uint8"
 
 SCRATCH = {}
@@ -23,14 +26,14 @@ def _decl(kind, names, into=None):
         SCRATCH[into or name] = ("sbuf", [128, at or int(n)], kind)
 
 
-_decl(BF, "x0:1536 xs:1536 ut:512 vt:512 et:2048 xh:1536 z:1536 z32:1536 ym:2176 f:640 f16:640 "
-          "qt0:32 qt1:32 qt2:32 pw0:32 pw1:32 pw2:32 rw:32 ft0:32 ev0:32 ed0:32 pev:32 ped:32 rev:32 red:32")
+_decl(BF, "x0:1536 xs:1536 ut:512 vt:512 et:2048 e0:512 xh:1536 z:1536 z32:1536 ym:2176 f:640 f16:640 "
+          "qt0:32 qt1:32 qt2:32 pw0:32 pw1:32 pw2:32 rw:32 ft0:32 ev0:32 pev:32 rev:32")
 _decl(BF, "pq:32 ev:32 ed:32 t32:32 oa:192 own:192 pu:192 lead:192 rr:64 pg:128 kp:128 ps2:160 lm:64 nl:64 tn:128 tb:128 "
           "rl:128 d1:128 fin:128 fs:128 nm:256 iv:256 fl:224 fsn:288 cc:288 mkb:224 vl:32 wr:32 pb:32 pb0:32 e1:32 v8:32 mv:32 idn:128", "wb")
 _decl(F32, "irl:384 hrl:384 hw:384 s:384 ew:1200 yo:384")
 _decl(F32, "ext:448 exs:448 sb:224 maskl:224 maskr:224 col:64 wl:32 wt:32 ag:40 adf:32 dex:256 t11:256 nw:256 pp:32 uu:32 "
-           "tp:64 tpt:64 base:24 sl:24 i1:24 i2:24 i3:24 esn:160 tab:16 tabn:16 tmp:64 lsf:160", "wf")
-_decl(BF, "j16:448 dm:448 k16:448 k8:256 k4:64 kbig:64 ones:256 t9:225 b9:224 nk:256 kk:256 cg:64 k2:32 fone:192", "cb")
+           "tp:64 tpt:64 base:24 sl:24 i1:24 i2:24 i3:24 esn:160 tab:16 tabn:16 tmp:64 lsf:160 far:8", "wf")
+_decl(BF, "j16:224 dm:224 k16:224 k8:256 k4:64 kbig:64 ones:256 t9:225 b9:224 nk:256 kk:256 cg:64 k2:32 fone:192", "cb")
 _decl(F32, "blk:32 rows:96 c16:28 negk:32 k160:24 six:24 cbig:160", "cf")
 _decl(I32, "pin:24 hin:24 pidx:1 coli:16 cq:14 tabi:16 taba:16")
 _decl(U16, "lst:160 w16:24 h16:24 xh16:96 lab:28 idx:24 sl16:24 e16:10")
@@ -41,13 +44,13 @@ PLACE["ps"] = ("ps", 0, 4096, F32)
 
 POOL = {"v": 60, "a": 30, "t": 12, "g": 20, "dma": 10}
 SEMAPHORES = (["%s%d" % (e, i) for e in POOL for i in range(POOL[e])]
-              + ["ae0", "aw0", "aw1", "aw2", "af0", "af1", "af2", "rea", "rda", "rwa", "rqa", "rsa", "sent", "outs"])
+              + ["ae0", "aw0", "aw1", "aw2", "af0", "af1", "af2", "rea", "rwa", "rqa", "rsa", "sent", "outs"])
 
 A = AluOpType
 ACT = ActivationFunctionType
 
 LISTS = {}
-for _name, _n in [("pl", 28), ("ec", 14), ("ei", 16), ("up", 8), ("u", 12), ("v", 12), ("pg", 4), ("rank", 4), ("turn", 4),
+for _name, _n in [("pl", 28), ("ei", 16), ("up", 8), ("u", 12), ("v", 12), ("pg", 4), ("rank", 4), ("turn", 4),
                   ("relr", 4), ("rell", 4), ("addr", 4), ("addl", 4), ("topr", 4), ("topl", 4), ("pos", 16), ("mv", 2), ("tot", 2)]:
     LISTS[_name] = (sum(n for _, n in LISTS.values()), _n)
 
@@ -67,10 +70,9 @@ TABLES = {
 }
 NEGATED = [0, 1, 2, 3, 4, 5, 6, 10, 11]
 
-KINDS = {"e": ("ev%d", "pev", "ae%d", "rev", "rea"), "d": ("ed%d", "ped", "ae%d", "red", "rda"),
-         "w": ("qt%d", "pw%d", "aw%d", "rw", "rwa"),
+KINDS = {"e": ("ev%d", "pev", "ae%d", "rev", "rea"), "w": ("qt%d", "pw%d", "aw%d", "rw", "rwa"),
          "q": ("fq%d", "lq%d", "af%d", "rq", "rqa"), "s": ("fs%d", "ls%d", "af%d", "rsc", "rsa")}
-SECOND = "ds"
+HANDS = {"e": [0, 1], "w": [0], "q": [0], "s": [1]}
 
 
 def names_of(kind, rnd):
@@ -81,34 +83,40 @@ def partner_of(T, rank, rnd):
     return T.cores[rank ^ (1 << rnd)]
 
 
-def relay_of(topo, src, dst, kind):
-    if topo.may_write(src, dst):
-        return None
-    near = [c for c in topo.cores_of(src) if topo.may_write(c, dst)]
-    near = [c for c in near if topo.die(c) == topo.die(src)] or near
-    return near[-1] if kind in SECOND else near[0]
-
-
 def engines_in(mask):
     return bin(mask).count("1")
 
 
-def first_hop(topo, src, dst, kind):
-    hop = relay_of(topo, src, dst, kind)
-    if hop is None:
-        return dst, topo.mask(src, dst)
-    far = topo.mask(hop, dst)
-    rest = topo.mask(src, hop) & ~far
-    return hop, rest if kind in SECOND and engines_in(rest) == engines_in(far) else far
+def pieces(topo, src, dst, kind):
+    n = PLACE[KINDS[kind][0] % 0][2]
+    if topo.may_write(src, dst):
+        return [(dst, topo.mask(src, dst), 0, n)]
+    near = [c for c in topo.cores_of(src) if topo.may_write(c, dst) and topo.die(c) == topo.die(src)]
+    hands = [near[0], near[-1]]
+    leaving = topo.mask(near[0], dst)
+    masks = [leaving, topo.mask(src, near[-1]) & ~leaving]
+    if len(HANDS[kind]) == 1:
+        masks = [topo.mask(src, c) for c in hands]
+    step = n // len(HANDS[kind])
+    return [(hands[h], masks[h], step * i, step * i + step) for i, h in enumerate(HANDS[kind])]
 
 
-def whole(T, name):
-    return T[name][:].bitcast(dt.uint8) if SCRATCH[name][2] == Q4 else T[name][:]
+def run_of(T, name, a, b):
+    return T[name][:, a:b].bitcast(dt.uint8) if SCRATCH[name][2] == Q4 else T[name][:, a:b]
 
 
-def send(g, T, topo, src, dst, land, name, sem, mask):
-    rid, pid = topo.addr(dst, src)
-    g.remote_dma(whole(T, land), whole(T, name), T.sem[sem], T.sem["sent"], pid, rid, mask)
+def send(g, T, topo, src, writes):
+    if len(writes) == 1:
+        to, land, name, sem, mask, a, b = writes[0]
+        rid, pid = topo.addr(to, src)
+        g.remote_dma(run_of(T, land, a, b), run_of(T, name, a, b), T.sem[sem], T.sem["sent"], pid, rid, mask)
+        return
+    transfers = []
+    for to, land, name, sem, mask, a, b in writes:
+        rid, pid = topo.addr(to, src)
+        transfers.append(RemoteDMATransfer(dst_ids=[DstId(rid=rid, pnc=pid)], dma_engine_mask=mask, remote_sem=T.sem[sem],
+                                           src=run_of(T, name, a, b), dst=run_of(T, land, a, b)))
+    g.remote_dma_fused(transfers, local_sem=T.sem["sent"])
 
 
 def relay_program(g, core, T, topo):
@@ -116,12 +124,13 @@ def relay_program(g, core, T, topo):
     for rank, src in enumerate(T.cores):
         for rnd in range(NR):
             dst = partner_of(T, rank, rnd)
-            for kind in "edwqs" if rnd == 0 else "wqs":
-                if relay_of(topo, src, dst, kind) == core:
-                    _, land, sem, here, came = names_of(kind, rnd)
-                    g.wait_ge(T.sem[came], engines_in(first_hop(topo, src, dst, kind)[1]))
-                    send(g, T, topo, core, dst, land, here, sem, topo.mask(core, dst))
-                    total += engines_in(topo.mask(core, dst))
+            for kind in "ewqs" if rnd == 0 else "wqs":
+                for to, mask, a, b in pieces(topo, src, dst, kind):
+                    if to == core:
+                        _, land, sem, here, came = names_of(kind, rnd)
+                        g.wait_ge(T.sem[came], engines_in(mask))
+                        send(g, T, topo, core, [(dst, land, here, sem, topo.mask(core, dst), a, b)])
+                        total += engines_in(topo.mask(core, dst))
     if total:
         g.wait_ge(T.sem["sent"], total)
 
@@ -138,8 +147,8 @@ def count(v):
     return 16 * count(v[2]) if v[0] == "ind" else len(range(*v[1:]))
 
 
-CYCLE, WAKE, LOAD, PASSES = 1.04, 120.0, 1200.0, 3
-HOP = {"ed": 2000.0, "w": 1350.0, "qs": 2300.0}
+CYCLE, WAKE, LOAD, BYTE, TWO, PASSES = 1.04, 110.0, 1200.0, 0.65, 2.4, 3
+HOP = {"e": 2300.0, "w": 1000.0, "qs": 2000.0}
 
 
 def length(eng, kind, form, writes, reads):
@@ -174,7 +183,7 @@ def rank_program(g, core, T, topo):
     if rank is None:
         relay_program(g, core, T, topo)
         return
-    ops = []
+    ops, queued = [], [0]
     queues = {"v": g.vector, "a": g.scalar, "t": g.tensor, "g": g, "s": g.sync}
 
     def ap(v):
@@ -223,12 +232,12 @@ def rank_program(g, core, T, topo):
     def ms(out, val):
         add("v", lambda: g.vector.memset(ap(out), val), [out], [])
 
-    def quant(q, sc, in_):
-        add("v", lambda: g.vector.quantize_mx(ap(q), ap(sc), ap(in_)), [q, sc], [in_], form="pack")
+    def quant(q, sc, in_, after=()):
+        add("v", lambda: g.vector.quantize_mx(ap(q), ap(sc), ap(in_)), [q, sc], [in_] + list(after), form="pack")
 
-    def act(out, in_, scale=None, bias=None):
+    def act(out, in_, scale=None, bias=None, func=ACT.Identity):
         if bias is not None:
-            add("a", lambda: g.scalar.activation(ap(out), ap(in_), ACT.Identity, bias=ap(bias), scale=1.0 if scale is None else ap(scale)),
+            add("a", lambda: g.scalar.activation(ap(out), ap(in_), func, bias=ap(bias), scale=1.0 if scale is None else ap(scale)),
                 [out], [in_, bias, scale])
         elif scale is None:
             add("a", lambda: g.scalar.activation(ap(out), ap(in_), ACT.Copy), [out], [in_])
@@ -243,42 +252,28 @@ def rank_program(g, core, T, topo):
         add("g", lambda: g.iota(ap(out), pattern, base, cm, allow_small_or_imprecise_dtypes=small), [out], [])
 
     def load(eng, out, src, as_codes=False, after=()):
+        queued[0] = (0 if after else queued[0]) + count(out) * (4 if as_codes else 2)
         add(eng, lambda: queues[eng].dma_start(ap(out).bitcast(dt.uint8) if as_codes else ap(out), src), [out], list(after), kind="dma",
-            lag=LOAD + count(out) * (4 if as_codes else 2))
+            lag=LOAD + BYTE * queued[0])
 
     def store(eng, dst, src_ap, reads):
         add(eng, lambda: queues[eng].dma_start(dst, src_ap), [], reads, kind="out", lag=LOAD)
 
     sent = [0]
 
-    def route(rnd, kind, name=None):
-        dst = partner_of(T, rank, rnd)
-        to, mask = first_hop(topo, core, dst, kind)
-        src, land, sem, there, came = names_of(kind, rnd)
-        sent[0] += engines_in(mask)
-        return (to, land if to == dst else there, name or src, sem if to == dst else came, mask)
-
-    def remote(rnd, kind, name=None):
-        r = route(rnd, kind, name)
-        add("g", lambda: send(g, T, topo, core, *r), [], [V(r[2])], kind="remote")
-
-    def remote_pair(rnd, kinds):
-        rs = [route(rnd, k) for k in kinds]
-        if rs[0][4] & rs[1][4]:
-            for r in rs:
-                add("g", lambda r=r: send(g, T, topo, core, *r), [], [V(r[2])], kind="remote")
-            return
-        transfers = []
-        for to, land, src, sem, mask in rs:
-            rid, pid = topo.addr(to, core)
-            transfers.append(RemoteDMATransfer(dst_ids=[DstId(rid=rid, pnc=pid)], dma_engine_mask=mask, remote_sem=T.sem[sem],
-                                               src=whole(T, src), dst=whole(T, land)))
-        add("g", lambda: g.remote_dma_fused(transfers, local_sem=T.sem["sent"]), [], [V(r[2]) for r in rs], kind="remote")
+    def remote(rnd, kinds, name=None):
+        dst, writes = partner_of(T, rank, rnd), []
+        for kind in kinds:
+            src, land, sem, there, came = names_of(kind, rnd)
+            for to, mask, a, b in pieces(topo, core, dst, kind):
+                sent[0] += engines_in(mask)
+                writes.append((to, land if to == dst else there, name or src, sem if to == dst else came, mask, a, b))
+        add("g", lambda: send(g, T, topo, core, writes), [], [V(w[2]) for w in writes], kind="remote")
 
     def arrival(rnd, kinds):
         src = partner_of(T, rank, rnd)
-        n = sum(engines_in(topo.mask(relay_of(topo, src, core, k) or src, core)) for k in kinds)
-        hops = 1 if topo.may_write(src, core) else 2
+        n = sum(engines_in(topo.mask(src if to == core else to, core)) for k in kinds for to, _, _, _ in pieces(topo, src, core, k))
+        hops = 1 if topo.may_write(src, core) else TWO
         add(None, None, [V(names_of(k, rnd)[1]) for k in kinds], [], kind="arrive", sem=(names_of(kinds[0], rnd)[2], n),
             lag=hops * HOP[kinds])
 
@@ -321,32 +316,37 @@ def rank_program(g, core, T, topo):
     load("s", V("pin"), T.p[:])
     load("a", V("hin"), T.h[:])
     load("a", V("ut"), T.u[:])
-    load("s", V("x0", 0, 4 * H), T.x[:, 0:4 * H])
-    load("s", V("x0", 4 * H, 4 * C), T.x[:, 4 * H:4 * C])
+    for a, b in PARTS:
+        load("s", V("x0", 4 * a, 4 * b), T.x[:, 4 * a:4 * b])
 
     iota(V("pidx"), [[1, 1]], 0, 1)
     iota(V("c16"), [[16, 28]])
-    iota(V("irl"), [[1, C]])
-    iota(ROW_EI, [[8, 4], [0, 4]])
-    iota(V("blk"), [[0, 2], [8, 2], [0, 8]])
-    iota(V("kk"), [[0, 4], [1, 8], [0, 8]])
-    iota(V("t9"), [[0, 25], [1, SEG]], -1)
-    iota(V("j16"), [[0, 28], [1, 16]])
-
+    iota(V("irl", 0, 128), [[1, 128]])
+    for a in (128, 256):
+        act(V("irl", a, a + 128), V("irl", 0, 128), bias=float(a))
     ms(V("k16"), 1.0)
     ms(V("wl", 24, 32), 0.0)
-    fields(0, 5)
-    ms(V("k16", 0, 2 * NP, 16), 0.0)
+    fields(0, 10)
+    ms(V("k16", 0, NP, 16), 0.0)
     ms(V("cc"), 0.0)
+    ms(V("fsn", NP, 288), 0.0)
     cp(lst("up"), V("c16", 0, 8))
     ts(col("16c"), col("c"), 16.0, A.mult)
+
+    def block_rows():
+        iota(ROW_EI, [[8, 4], [0, 4]])
+        ts(lst("ei"), ROW_EI, col("s"), A.add)
+        if not all(left):
+            iota(V("blk"), [[0, 2], [8, 2], [0, 8]])
+            ms(V("ones"), 1.0)
+            act(V("blk"), V("blk"), bias=col("16c"))
+        iota(V("kk"), [[0, 4], [1, 8], [0, 8]])
+
+    if not left[0]:
+        block_rows()
+    iota(V("j16"), [[0, 14], [1, 16]])
+    iota(V("t9"), [[0, 25], [1, SEG]], -1)
     ts(V("dm"), V("j16"), col("r"), A.is_equal)
-    ms(V("cc", 0, 288, SEG), 1.0)
-    ms(V("fsn", NP, 288), 0.0)
-    act(V("blk"), V("blk"), bias=col("16c"))
-    ts(lst("ei"), ROW_EI, col("s"), A.add)
-    if not all(left):
-        ms(V("ones"), 1.0)
 
     def pair_lists():
         j, e = V("tmp", 0, 14), V("tmp", 16, 30)
@@ -358,9 +358,9 @@ def rank_program(g, core, T, topo):
         ts(lst("pl", 14, 14), j, C - 2.0, A.min, 1.0, A.add)
 
     def right_mask_consts():
-        ts(lst("ec"), V("cq"), 23.0, A.min)
-        act(col("128-4r8"), col("r8"), -4.0, 128.0)
-        act(V("b9"), V("t9", 0, NP), bias=col("128-4r8"))
+        act(col("4r8-128"), col("r8"), 4.0 * FAR, -128.0 * FAR)
+        act(V("far"), V("t9", 1, SEG), -FAR, col("4r8-128"))
+        act(V("maskr", 0, NP, SEG), V("t9", 0, NP, SEG), BIG)
 
     def left_mask():
         ts(V("maskl"), V("t9", 0, NP), col("pair"), A.not_equal, BIG, A.mult)
@@ -376,45 +376,43 @@ def rank_program(g, core, T, topo):
         tt(V(ed[0], 0, 32, 2), V(ev[0], 1, 32, 2), V(ev[0], 0, 32, 2), A.subtract)
         tt(V(ed[0], 1, 32, 2), V(ev[0], 0, 32, 2), V(ev[0], 1, 32, 2), A.subtract)
 
-    def right_change(iv, pb, ev, ed):
-        act(pb, iv, -0.5, 131.75)
+    def right_change(iv, ev, ed):
+        act(V("pb"), iv, -0.5, 131.75)
         act(V("v8"), iv, 0.125)
-        act(V("e1"), pb, -0.25, 527.0 / 16)
-        act(ev, iv, 0.0625)
+        act(V("e1"), V("pb"), -0.25, 527.0 / 16)
+        if ev:
+            act(ev, iv, 0.0625)
         tt(ed, V("e1"), V("v8"), A.subtract)
 
     def right_mask():
-        tt(V("mkb"), IND(V("pb"), lst("ec")), V("b9"), A.not_equal)
-        act(V("maskr"), V("mkb"), BIG)
-        act(V("maskr", 0, NP, SEG), V("t9", 0, NP, SEG), BIG)
+        for t in range(1, SEG):
+            out = V("maskr", t, NP, SEG)
+            act(out, V("pb", 0, count(out)), FAR, V("far", t - 1, t), ACT.Square)
 
     def score_lists():
         for a in (NP, 0):
-            tt(V("ext", a, a + NP), IND(V("hw"), lst("pl", a // 16, 14)), V("dm", a, a + NP), A.mult)
+            tt(V("ext", a, a + NP), IND(V("hw"), lst("pl", a // 16, 14)), V("dm"), A.mult)
         for a in (NP, 0):
-            scan(V("exs", a, a + NP), V("k16", a, a + NP), V("ext", a, a + NP), 0.0, A.mult, A.add)
+            scan(V("exs", a, a + NP), V("k16"), V("ext", a, a + NP), 0.0, A.mult, A.add)
         cp(V("lab"), V("exs", 15, 2 * NP, 16))
 
-    def product(x, hf, last):
-        a, b = H * hf, H * hf + H
-        bank = 2048 + 512 * hf
+    def product(x, i, last):
+        a, b = (HALVES if last else PARTS)[i]
+        bank = 2048 + 512 * i
         quant(V("xq", a, b), V("xsc", a, b), V(x, 4 * a, 4 * b))
-        mm(V("ps", bank, bank + H), V("vq" if last else "uq2"), V("vs" if last else "us2"), V("xq", a, b), V("xsc", a, b))
+        mm(V("ps", bank, bank + b - a), V("vq" if last else "uq2"), V("vs" if last else "us2"), V("xq", a, b), V("xsc", a, b))
 
-    def fetch(hf, last):
-        bank = 2048 + 512 * hf
-        (act if hf == 0 else cp)(V("yo" if last else "s", H * hf, H * hf + H), V("ps", bank, bank + H))
+    def fetch(i, last, eng="a"):
+        a, b = (HALVES if last else PARTS)[i]
+        bank = 2048 + 512 * i
+        (act if eng == "a" else cp)(V("yo" if last else "s", a, b), V("ps", bank, bank + b - a))
 
     def tables():
-        fields(5, 10)
         for i in range(3):
             act(col("w%d" % i), col("b%d" % i), 8.0 ** -(1 << i) - 1.0, 1.0)
         for i, t in enumerate(TABLES.values()):
             lo, hi = octal(t[:8]), octal(t[-8:])
-            if lo == hi:
-                iota(V("tabn", i, i + 1), [[0, 1]], lo)
-            else:
-                act(V("tabn", i, i + 1), col("r8"), float(hi - lo), float(lo))
+            act(V("tabn", i, i + 1), col("r8"), float(hi - lo), float(lo))
         ts(col("w"), col("w0"), col("w1"), A.mult, col("w2"), A.mult)
         ts(col("half"), col("w"), -0.5, A.mult, 0.5, A.add)
         n = len(TABLES)
@@ -423,12 +421,9 @@ def rank_program(g, core, T, topo):
         cp(V("tab", 0, n), V("taba", 0, n))
 
     def lead_lists():
-        act(V("rows", 52, 56), ROW_IN, bias=col("8r8"))
-        ts(lst("u", 0, 4), V("rows", 52, 56), tab("link"), A.add)
-        ts(lst("u", 4, 4), V("rows", 52, 56), tab("direct"), A.add)
+        for out, by in [(lst("u", 0, 4), "link"), (lst("u", 4, 4), "direct"), (lst("v", 0, 4), "to"), (lst("v", 4, 4), "to")]:
+            ts(out, ROW_IN, tab(by), A.add, col("8r8"), A.add)
         ts(lst("u", 8), ROW_8, col("lo"), A.add)
-        ts(lst("v", 0, 4), V("rows", 52, 56), tab("to"), A.add)
-        ts(lst("v", 4, 4), V("rows", 52, 56), tab("to"), A.add)
         ts(lst("v", 8), ROW_8, col("hi"), A.add, 4.0, A.add)
 
     def meet_lists():
@@ -454,6 +449,8 @@ def rank_program(g, core, T, topo):
 
     def meet_rows():
         iota(V("ag", 32, 40), [[0, 8]])
+        ms(V("fone"), 0.0)
+        ms(V("fone", 64 + 7, 128, 8), 2.0)
         iota(V("cg"), [[0, 4], [-1, 2], [0, 8]], 1)
         for i in range(16):
             if (i in NEGATED) != (i < 8):
@@ -469,14 +466,13 @@ def rank_program(g, core, T, topo):
         iota(V("k2"), [[0, 4], [1, 8]])
         iota(V("six"), [[0, 24]], 16)
         iota(V("ew", 0, TS), [[0, TS]], C - 1)
-        for b in range(4):
-            iota(V("et", 512 * b, 512 * b + 512), [[0, 512]])
 
     def unpack_consts():
-        cp(col("p"), V("pidx"))
-        ts(V("idn"), V("irl", 0, 128), col("p"), A.is_equal, 16.0, A.mult)
+        iota(V("e0"), [[0, 512]], 16)
         for b in range(4):
-            cp(V("et", 512 * b + b, 512 * b + 512, 4), V("idn"))
+            out = V("et", 512 * b, 512 * b + 512)
+            add("g", lambda out=out, b=b: g.affine_select(ap(out), ap(V("e0")), [[-4, 128], [-1, 4]], A.is_equal, 0.0, b, 4),
+                [out], [V("e0")])
 
     def spread_u():
         quant(V("uq"), V("us"), V("ut"))
@@ -491,48 +487,48 @@ def rank_program(g, core, T, topo):
     act(V("hw"), IND(V("hrl"), V("w16")))
     tr(V("wt"), V("wl"))
     if left[0]:
-        weave(lambda: left_change(V("ev0"), V("ed0")), pair_lists)
-        remote_pair(0, "ed")
-        spread_u()
-        left_mask()
+        weave(lambda: left_change(V("ev0"), V("ed")), pair_lists)
+        remote(0, "e")
+        tr(V("cc", 0, 288, SEG), V("ed"))
     else:
         weave(inverse, pair_lists)
+        act(V("ev0"), V("iv", 7, 256, 8), 0.0625)
+        remote(0, "e")
         right_mask_consts()
         tr(V("vl"), V("iv", 7, 256, 8))
-        act(V("pb"), V("vl"), -0.5, 131.75)
-        right_change(V("iv", 7, 256, 8), V("pb0"), V("ev0"), V("ed0"))
-        remote_pair(0, "ed")
-        spread_u()
-        right_mask()
-    product("x0", 0, False)
-    score_lists()
-    product("x0", 1, False)
+        right_change(V("vl"), None, V("cc", 0, 288, SEG))
+    arrival(0, "e")
+    spread_u()
+    tables()
+    weave(score_lists, lambda: [product("x0", i, False) for i in range(2)])
+    (left_mask if left[0] else right_mask)()
     fetch(0, False)
-    fetch(1, False)
+    fetch(1, False, "v")
     iota(ROW_IN, [[4, 2], [16, 2]])
     iota(ROW_8, [[8, 4]])
     iota(ROW_16, [[16, 4]])
     iota(ROW_POS, [[16, 4], [0, 4]])
     iota(ROW_32, [[32, 2]])
-    iota(V("fone"), [[0, 192]])
-    iota(V("fone", 64 + 7, 128, 8), [[0, 8]], 2)
+    if left[0]:
+        block_rows()
     act(col("8r8"), col("r8"), 8.0)
 
-    def pick(eng, b, c0, c1):
-        out = V("xs", 64 * c0 + b, 64 * c1, 4)
-        src = IND(V("ym", YW * b, YW * b + YW), V("idx", c0, c1))
+    def scaled(eng, out, src, by):
         if eng == "a":
-            act(out, src, 0.03125)
+            act(out, src, by)
         else:
-            ts(out, src, 0.03125, A.mult)
+            ts(out, src, by, A.mult)
 
     for rnd in range(NR):
         last = rnd + 1 == NR
         q = V("qt%d" % rnd)
+        def scores(a, b):
+            return IND(V("s"), V("lab", a // 16, b // 16))
+
         for a, b in ((0, 128), (128, NP)):
-            tt(V("sb", a, b), IND(V("s"), V("lab", 14 + a // 16, 14 + b // 16)), V("maskl" if left[rnd] else "maskr", a, b), A.add)
+            tt(V("sb", a, b), scores(NP + a, NP + b), V("maskl" if left[rnd] else "maskr", a, b), A.add)
         for a, b in ((0, 128), (128, NP)):
-            tt(V("fl", a, b), IND(V("s"), V("lab", a // 16, b // 16)), V("sb", a, b), A.is_lt)
+            tt(V("fl", a, b), scores(a, b), V("sb", a, b), A.is_lt)
         for a, b in ((0, 14 * SEG), (14 * SEG, NP)):
             scan(V("fsn", a, b), V("fl", a, b), V("cc", a, b), 0.0, A.mult, A.add)
         if rnd == 0:
@@ -541,16 +537,11 @@ def rank_program(g, core, T, topo):
             meet_rows()
             for t in range(4):
                 ts(V("xh16", 24 * t, 24 * t + 24), V("hin"), 4.0, A.mult, float(t), A.add)
-            arrival(rnd, "ed")
-            load("s", V("wq"), T.wc[:], as_codes=True, after=[V("pev")])
-            load("s", V("wsc"), T.ws[:])
-            tt(V("t32"), V("ft0"), V("ed0"), A.mult)
             if not all(left):
                 act(V("nk"), V("kk"), -0.0625, 0.5)
-                iota(V("k8"), [[0, 256]], 1)
-                iota(V("k8", 0, 256, 8), [[0, 32]])
-            tables()
-            tt(q, V("t32"), V("ev0"), A.add)
+                ms(V("k8"), 1.0)
+                ms(V("k8", 0, 256, 8), 0.0)
+            tt(q, V("ft0"), V("ev0"), A.add)
             lead_lists()
         else:
             tr(q, V("fsn", SEG - 1, 288, SEG))
@@ -567,9 +558,10 @@ def rank_program(g, core, T, topo):
                 ts(V("ag", 0, 32), q, 16.0, A.mult, col("16c"), A.add)
                 tt(V("adf"), V("ag", 0, 32), V("ag", 1, 33), A.subtract)
                 cp(V("adf", 7, 32, 8), V("ag", 7, 32, 8))
-                cp(V("dex"), IND(V("adf"), lst("ei")))
+                act(V("dex"), IND(V("adf"), lst("ei")))
             else:
-                tt(V("nm"), IND(q, lst("ei")), V("nk"), A.is_equal)
+                for a in (0, 128):
+                    tt(V("nm", a, a + 128), IND(q, lst("ei", a // 16, 8)), V("nk", a, a + 128), A.is_equal)
                 for bk in range(4):
                     act(V("dex", 64 * bk, 64 * bk + 64), V("nm", 64 * bk, 64 * bk + 64), 1000.0, col("dex%d" % (bk % 2)))
 
@@ -583,8 +575,10 @@ def rank_program(g, core, T, topo):
         pw = V("pw%d" % rnd)
         arrival(rnd, "w")
         if rnd == 0:
-            tt(V("t32"), pw, V("ped"), A.mult)
-            tt(V("pq"), V("t32"), V("pev"), A.add)
+            load("s", V("wq"), T.wc[:], as_codes=True, after=[pw])
+            load("s", V("wsc"), T.ws[:], after=[pw])
+            unpack_consts()
+            tt(V("pq"), pw, V("pev"), A.add)
             pw = V("pq")
         tt(V("pu", 0, 128), IND(pw, lst("u", 0, 8)), V("own", 0, 128), A.add)
         tt(V("pu", 128, 192), IND(pw, lst("u", 8)), V("own", 128, 192), A.add)
@@ -612,57 +606,66 @@ def rank_program(g, core, T, topo):
         scan(V("fs", 64, 128), V("fin", 64, 128), V("d1", 64, 128), 0.0, A.max, A.add)
         scan(V("fs", 0, 64), V("fin", 0, 64), V("d1", 0, 64), 64.0, A.min, A.add)
 
-        def new_word(hf):
+        def match(hf):
             a, b = 128 * hf, 128 * hf + 128
             at = IND(V("fs"), lst("pos", 8 * hf, 8))
             if left[rnd]:
                 tt(V("nm", a, b), at, V("kk", a, b), A.not_equal)
-                scan(V("nw", a, b), V("nm", a, b), V("dex", a, b), 0.0, A.mult, A.add)
             else:
                 tt(V("t11", a, b), at, V("dex", a, b), A.add)
+
+        def new_word(hf):
+            a, b = 128 * hf, 128 * hf + 128
+            if left[rnd]:
+                scan(V("nw", a, b), V("nm", a, b), V("dex", a, b), 0.0, A.mult, A.add)
+            else:
                 scan(V("nw", a, b), V("k8", a, b), V("t11", a, b), 0.0, A.mult, A.max)
 
-        weave(lambda: new_word(0), lambda: new_word(1))
+        match(0)
+        match(1)
         tt(V("mv"), IND(V("fs"), lst("mv")), V("k2"), A.not_equal)
-        tr(V("wl"), V("nw", 7, 256, 8))
+        new_word(0)
+        new_word(1)
         scan(V("pp"), V("k16", 0, 32), V("mv"), 0.0, A.mult, A.add)
-        cp(V("w16"), V("wl", 0, 24))
-        for hf in range(2):
-            for t in range(4):
-                act(V("z", 4 * H * hf + t, 4 * H * hf + 4 * H, 4), IND(V("xh", C * t, C * t + C), V("w16", 12 * hf, 12 * hf + 12)))
-        for b in range(4):
-            act(V("z32", 4 * H + b, 4 * C, 4), V("z", 4 * H + b, 4 * C, 4), 32.0)
-        if rnd == 0:
-            load("s", V("vt"), T.v[:], after=[V("w16")])
         tt(V("uu"), V("mv"), V("negk"), A.mult)
-        cp(V("tp", 32, 64), IND(V("pp"), lst("tot")))
+        tr(V("wl"), V("nw", 7, 256, 8))
+        act(V("tp", 32, 64), IND(V("pp"), lst("tot")))
         tt(V("tp", 0, 32), V("pp"), V("uu"), A.add)
-        cp(V("wt"), V("nw", 7, 256, 8))
+        cp(V("w16"), V("wl", 0, 24))
+        act(V("wt"), V("nw", 7, 256, 8))
+        if last:
+            load("s", V("vt"), T.v[:], after=[V("wt")])
+            for gr in range(8):
+                a, y = gr // 2, gr % 2
+                store("s", T.op[gr:gr + 1, :], T.wf[32 * a:32 * a + 24, PLACE["wt"][1] + 16 * y:PLACE["wt"][1] + 16 * y + 16], [V("wt")])
+        for lo, hi in HALVES:
+            for b in range(4):
+                act(V("z", 4 * lo + b, 4 * hi, 4), IND(V("xh", C * b, C * b + C), V("w16", lo // 16, hi // 16)))
         tr(V("tpt"), V("tp"))
         scan(V("base", 1, 24), V("tpt", 32, 55), V("six", 0, 23), col("399+r"), A.add, A.add)
         tt(V("sl"), V("base"), V("tpt", 0, 24), A.add)
         cp(V("sl16"), V("sl"))
         scat(V("ew"), V("sl16"), V("irl"))
-        if last:
-            for gr in range(8):
-                a, y = gr // 2, gr % 2
-                store("s", T.op[gr:gr + 1, :], T.wf[32 * a:32 * a + 24, PLACE["wt"][1] + 16 * y:PLACE["wt"][1] + 16 * y + 16], [V("wt")])
-        quant(V("zq", 0, H), V("zs", 0, H), V("z", 0, 4 * H))
+
+        def layer(hf):
+            lo, hi = HALVES[hf]
+            quant(V("zq", lo, hi), V("zs", lo, hi), V("z", 4 * lo, 4 * hi))
+            for b in range(4):
+                bank = 512 * (2 * b + hf)
+                mm(V("ps", bank, bank + H), V("wq", 128 * b, 128 * b + 128), V("wsc", 128 * b, 128 * b + 128), V("zq", lo, hi), V("zs", lo, hi))
+
+        layer(0)
         scan(V("esn"), V("cbig"), V("ew", 0, TS), 0.0, A.add, A.min)
         ts(V("z32", 0, 4 * H), V("z", 0, 4 * H), 32.0, A.mult)
         cp(V("e16"), V("esn", 15, TS, 16))
-        quant(V("zq", H, C), V("zs", H, C), V("z", 4 * H, 4 * C))
-        for hf in range(2):
-            for b in range(4):
-                bank = 512 * (2 * b + hf)
-                mm(V("ps", bank, bank + H), V("wq", 128 * b, 128 * b + 128), V("wsc", 128 * b, 128 * b + 128),
-                   V("zq", H * hf, H * hf + H), V("zs", H * hf, H * hf + H))
+        for b in range(4):
+            act(V("z32", 4 * H + b, 4 * C, 4), V("z", 4 * H + b, 4 * C, 4), 32.0)
+        layer(1)
         for b, hf in [(0, 0), (1, 0), (0, 1), (1, 1), (2, 0), (2, 1), (3, 0), (3, 1)]:
-            bank, at = 512 * (2 * b + hf), YW * b + TS + H * hf
-            tt(V("ym", at, at + H), V("ps", bank, bank + H), V("z32", 4 * H * hf + b, 4 * H * hf + 4 * H, 4), A.add)
-            if hf == 1 and b < 3:
-                act(V("f", b, 4 * TS, 4), IND(V("ym", YW * b + TS, YW * b + YW), V("e16")), 0.03125)
-        ts(V("f", 3, 4 * TS, 4), IND(V("ym", YW * 3 + TS, YW * 3 + YW), V("e16")), 0.03125, A.mult)
+            (lo, hi), bank, at = HALVES[hf], 512 * (2 * b + hf), YW * b + TS
+            tt(V("ym", at + lo, at + hi), V("ps", bank, bank + H), V("z32", 4 * lo + b, 4 * hi, 4), A.add)
+        for eng, b, lo, hi in [("a", 0, 0, 10), ("a", 1, 0, 10), ("a", 2, 0, 10), ("v", 3, 0, 6), ("a", 3, 6, 10)]:
+            scaled(eng, V("f", 64 * lo + b, 64 * hi, 4), IND(V("ym", YW * b + TS, YW * b + YW), V("e16", lo, hi)), 0.03125)
         quant(V("fq%d" % rnd), V("fs%d" % rnd), V("f"))
         remote(rnd, "q")
         remote(rnd, "s")
@@ -678,7 +681,6 @@ def rank_program(g, core, T, topo):
             cp(V("idx"), V("i3"))
 
         if rnd == 0:
-            unpack_consts()
             if left[0] and not all(left):
                 right_mask_consts()
             if any(left) and not left[0]:
@@ -693,37 +695,31 @@ def rank_program(g, core, T, topo):
         else:
             weave(slots, inverse)
             tr(V("vl"), V("iv", 7, 256, 8))
-            right_change(V("vl"), V("pb"), V("cc", SEG - 1, 288, SEG), V("cc", 0, 288, SEG))
+            right_change(V("vl"), V("cc", SEG - 1, 288, SEG), V("cc", 0, 288, SEG))
             weave(score_lists, right_mask)
         if rnd == 0:
-            quant(V("eq"), V("es"), V("et"))
+            for b in range(4):
+                quant(V("eq", 128 * b, 128 * b + 128), V("es", 128 * b, 128 * b + 128), V("et", 512 * b, 512 * b + 512), [V("fs0")])
         arrival(rnd, "qs")
         for b in (0, 3, 1, 2):
             mm(V("ps", 512 * b, 512 * b + TS), V("eq", 128 * b, 128 * b + 128), V("es", 128 * b, 128 * b + 128),
                V("lq%d" % rnd), V("ls%d" % rnd))
         for b in (0, 3, 1, 2):
             tt(V("ym", YW * b, YW * b + TS), V("ps", 512 * b, 512 * b + TS), V("f16", b, 4 * TS, 4), A.add)
-            if b < 2:
-                pick("a", b, 0, 12)
-        pick("v", 3, 0, 12)
-        pick("v", 2, 0, 12)
-        pick("a", 0, 12, 24)
-        pick("a", 1, 12, 24)
-        pick("v", 3, 12, 24)
-        product("xs", 0, last)
-        if last:
-            store("s", T.oc[:, 0:4 * H], T.xq[:, 0:H].bitcast(dt.uint8), [V("xq", 0, H)])
-        pick("v", 2, 12, 18)
-        pick("a", 2, 18, 24)
-        product("xs", 1, last)
-        fetch(0, last)
-        fetch(1, last)
+        parts = HALVES if last else PARTS
+        for i, (a, b) in enumerate(parts):
+            for pl in (0, 1, 3, 2):
+                scaled(PICKS[i][pl], V("xs", 4 * a + pl, 4 * b, 4), IND(V("ym", YW * pl, YW * pl + YW), V("idx", a // 16, b // 16)), 0.03125)
+            product("xs", i, last)
+            if last:
+                store("s", T.oc[:, 4 * a:4 * b], T.xq[:, a:b].bitcast(dt.uint8), [V("xq", a, b)])
+        for i, (a, b) in enumerate(parts):
+            fetch(i, last, "v" if last else "av"[i])
+            if last:
+                store("as"[i % 2], T.y[:, a:b], T.yo[:, a:b], [V("yo", a, b)])
 
-    store("a", T.y[:, 0:H], T.yo[:, 0:H], [V("yo", 0, H)])
-    store("s", T.oc[:, 4 * H:4 * C], T.xq[:, H:C].bitcast(dt.uint8), [V("xq", H, C)])
     for k in range(4):
-        store("s" if k < 2 else "a", T.osc[4 * k:4 * k + 4, :], T.xsc[32 * k:32 * k + 4, :], [V("xsc")])
-    store("s", T.y[:, H:C], T.yo[:, H:C], [V("yo", H, C)])
+        store("a", T.osc[4 * k:4 * k + 4, :], T.xsc[32 * k:32 * k + 4, :], [V("xsc")])
 
     emit(g, T, ops, queues, sent[0])
 
@@ -753,16 +749,20 @@ def touching(ops):
 
 
 def arrange(ops):
-    deps = touching(ops)
-    remote = None
+    deps, kept = touching(ops), {}
+    remote = own = None
     issued = {}
     for i, op in enumerate(ops):
-        if op["kind"] in ("remote", "arrive") and remote is not None:
+        if op["kind"] == "arrive":
             deps[i].add(remote)
         if op["kind"] == "remote":
             remote = i
+        if op["eng"] == "g":
+            kept[i], own = own, i
         if op["kind"] == "dma":
             issued[i] = max(issued, default=None)
+    for i, j in kept.items():
+        deps[i] |= {j} - {None}
     after = [[] for _ in ops]
     for i, d in enumerate(deps):
         for j in d:
@@ -772,7 +772,8 @@ def arrange(ops):
         busy, span = {}, {}
         for i in order:
             op = ops[i]
-            t = max([span[j][1] + WAKE for j in before[i]], default=0.0) + (0.0 if forward else op["lag"])
+            t = max([span[j][1] + (0.0 if j == kept.get(i) or i == kept.get(j) else WAKE) for j in before[i]], default=0.0)
+            t += 0.0 if forward else op["lag"]
             if forward and issued.get(i) in span:
                 t = max(t, span[issued[i]][0])
             taken = busy.setdefault(op["eng"], [])

from concourse.bass import DstId, RemoteDMATransfer
from concourse.mybir import dt, AluOpType, ActivationFunctionType

C, TS, NR = 384, 160, 3
H = C // 2
YW = TS + C
SEG, NP = 9, 224
EW = 1200
BIG, FAR = 1.0e29, 2.0 ** 46
PARTS = [(0, 256), (256, C)]
PICKS = ["aavv", "aaav"]
HALVES = [(0, H), (H, C)]
BF, F32, I32, U16, Q4, U8 = "bfloat16", "float32", "int32", "uint16", "float8_e4m3fn_x4", "uint8"

SCRATCH = {}
PLACE = {}


def _decl(kind, names, into=None):
    at = 0
    for item in names.split():
        name, n = item.split(":")
        PLACE[name] = (into or name, at, int(n), kind)
        if into:
            at += (int(n) + 31) // 32 * 32
        SCRATCH[into or name] = ("sbuf", [128, at or int(n)], kind)


_decl(BF, "x0:1536 xs:1536 ut:512 vt:512 et:2048 e0:512 xh:1536 z:1536 z32:1536 ym:2176 f:640 f16:640 "
          "qt0:32 qt1:32 qt2:32 pw0:32 pw1:32 pw2:32 rw:32 ft0:32 ev0:32 pev:32 rev:32")
_decl(BF, "pq:32 ev:32 ed:32 t32:32 oa:192 own:192 pu:192 lead:192 rr:64 pg:128 kp:128 ps2:160 lm:64 nl:64 tn:128 tb:128 "
          "rl:128 d1:128 fin:128 fs:128 nm:256 iv:256 fl:224 fsn:288 cc:288 mkb:224 vl:32 wr:32 pb:32 pb0:32 e1:32 v8:32 mv:32 idn:128", "wb")
_decl(F32, "irl:384 hrl:384 hw:384 s:384 ew:1200 yo:384")
_decl(F32, "ext:448 exs:448 sb:224 maskl:224 maskr:224 col:64 wl:32 wt:32 ag:40 adf:32 dex:256 t11:256 nw:256 pp:32 uu:32 "
           "tp:64 tpt:64 base:24 sl:24 i1:24 i2:24 i3:24 esn:160 tab:16 tabn:16 tmp:64 lsf:160 far:8", "wf")
_decl(BF, "j16:224 dm:224 k16:224 k8:256 k4:64 kbig:64 ones:256 t9:225 b9:224 nk:256 kk:256 cg:64 k2:32 fone:192", "cb")
_decl(F32, "blk:32 rows:96 c16:28 negk:32 k160:24 six:24 cbig:160", "cf")
_decl(I32, "pin:24 hin:24 pidx:1 coli:16 cq:14 tabi:16 taba:16")
_decl(U16, "lst:160 w16:24 h16:24 xh16:96 lab:28 idx:24 sl16:24 e16:10")
_decl(Q4, "wq:512 uq:128 uq2:128 vq:128 xq:384 zq:384 eq:512 fq0:160 fq1:160 fq2:160 lq0:160 lq1:160 lq2:160 rq:160")
_decl(U8, "wsc:512 us:128 us2:128 vs:128 xsc:384 zs:384 es:512 fs0:160 fs1:160 fs2:160 ls0:160 ls1:160 ls2:160 rsc:160")
SCRATCH["ps"] = ("psum", [128, 4096], F32)
PLACE["ps"] = ("ps", 0, 4096, F32)

POOL = {"v": 60, "a": 30, "t": 12, "g": 20, "dma": 10}
SEMAPHORES = (["%s%d" % (e, i) for e in POOL for i in range(POOL[e])]
              + ["ae0", "aw0", "aw1", "aw2", "af0", "af1", "af2", "rea", "rwa", "rqa", "rsa", "sent", "outs"])

A = AluOpType
ACT = ActivationFunctionType

LISTS = {}
for _name, _n in [("pl", 28), ("ei", 16), ("up", 8), ("u", 12), ("v", 12), ("pg", 4), ("rank", 4), ("turn", 4),
                  ("relr", 4), ("rell", 4), ("addr", 4), ("addl", 4), ("topr", 4), ("topl", 4), ("pos", 16), ("mv", 2), ("tot", 2)]:
    LISTS[_name] = (sum(n for _, n in LISTS.values()), _n)

TABLES = {
    "to": [1, 2, 3, 2, 3, 1, 3, 1],
    "link": [1, 1, 2, 2, 2, 0, 3, 1],
    "direct": [0, 0, 0, 1, 1, 1, 2, 2],
    "count": [2, 0, 1, 7, 7, 4, 3, 0, 1, 3, 6, 7, 2, 5, 4, 6],
    "by": [0, 0, 0, 1, 0, 0, 1, 2, 0, 0, 0, 1, 2, 3, 0, 0],
    "relr": [7, 7, 0, 7, 7, 1, 3, 7, 7, 2, 5, 4, 6, 7, 7, 7],
    "rell": [7, 7, 6, 7, 7, 4, 3, 7, 7, 2, 5, 1, 0, 7, 7, 7],
    "addr": [0, 5, 4, 1, 5, 4, 4, 2, 5, 4, 4, 4, 4, 3, 5, 5],
    "addl": [3, 5, 4, 2, 5, 4, 4, 1, 5, 4, 4, 4, 4, 0, 5, 5],
    "data": [1, 0, 0, 1, 0, 0, 0, 1, 0, 0, 0, 0, 0, 1, 0, 0],
    "end2": [6, 3, 1, 0, 0, 1, 3, 6],
    "end1": [1, 1, 1, 0, 0, 1, 1, 1],
}
NEGATED = [0, 1, 2, 3, 4, 5, 6, 10, 11]

KINDS = {"e": ("ev%d", "pev", "ae%d", "rev", "rea"), "w": ("qt%d", "pw%d", "aw%d", "rw", "rwa"),
         "q": ("fq%d", "lq%d", "af%d", "rq", "rqa"), "s": ("fs%d", "ls%d", "af%d", "rsc", "rsa")}
HANDS = {"e": [0, 1], "w": [0], "q": [0], "s": [1]}


def names_of(kind, rnd):
    return [n % rnd if "%" in n else n for n in KINDS[kind]]


def partner_of(T, rank, rnd):
    return T.cores[rank ^ (1 << rnd)]


def engines_in(mask):
    return bin(mask).count("1")


def pieces(topo, src, dst, kind):
    n = PLACE[KINDS[kind][0] % 0][2]
    if topo.may_write(src, dst):
        return [(dst, topo.mask(src, dst), 0, n)]
    near = [c for c in topo.cores_of(src) if topo.may_write(c, dst) and topo.die(c) == topo.die(src)]
    hands = [near[0], near[-1]]
    leaving = topo.mask(near[0], dst)
    masks = [leaving, topo.mask(src, near[-1]) & ~leaving]
    if len(HANDS[kind]) == 1:
        masks = [topo.mask(src, c) for c in hands]
    step = n // len(HANDS[kind])
    return [(hands[h], masks[h], step * i, step * i + step) for i, h in enumerate(HANDS[kind])]


def run_of(T, name, a, b):
    return T[name][:, a:b].bitcast(dt.uint8) if SCRATCH[name][2] == Q4 else T[name][:, a:b]


def send(g, T, topo, src, writes):
    if len(writes) == 1:
        to, land, name, sem, mask, a, b = writes[0]
        rid, pid = topo.addr(to, src)
        g.remote_dma(run_of(T, land, a, b), run_of(T, name, a, b), T.sem[sem], T.sem["sent"], pid, rid, mask)
        return
    transfers = []
    for to, land, name, sem, mask, a, b in writes:
        rid, pid = topo.addr(to, src)
        transfers.append(RemoteDMATransfer(dst_ids=[DstId(rid=rid, pnc=pid)], dma_engine_mask=mask, remote_sem=T.sem[sem],
                                           src=run_of(T, name, a, b), dst=run_of(T, land, a, b)))
    g.remote_dma_fused(transfers, local_sem=T.sem["sent"])


def relay_program(g, core, T, topo):
    total = 0
    for rank, src in enumerate(T.cores):
        for rnd in range(NR):
            dst = partner_of(T, rank, rnd)
            for kind in "ewqs" if rnd == 0 else "wqs":
                for to, mask, a, b in pieces(topo, src, dst, kind):
                    if to == core:
                        _, land, sem, here, came = names_of(kind, rnd)
                        g.wait_ge(T.sem[came], engines_in(mask))
                        send(g, T, topo, core, [(dst, land, here, sem, topo.mask(core, dst), a, b)])
                        total += engines_in(topo.mask(core, dst))
    if total:
        g.wait_ge(T.sem["sent"], total)


def V(name, a=0, b=None, s=1):
    return (name, a, PLACE[name][2] if b is None else b, s)


def IND(win, off):
    return ("ind", win, off)


def count(v):
    return 16 * count(v[2]) if v[0] == "ind" else len(range(*v[1:]))


CYCLE, WAKE, LOAD, BYTE, TWO, PASSES = 1.04, 110.0, 1200.0, 0.65, 2.4, 3
HOP = {"e": 2300.0, "w": 1000.0, "qs": 2000.0}


def length(eng, kind, form, writes, reads):
    if kind != "c":
        return 0.0 if kind == "arrive" else 100.0
    n = count(reads[1] if form == "scatter" else writes[0])
    full = [v for v in writes + reads if isinstance(v, tuple) and count(v) == n]
    if eng == "t":
        return 0.63 * (n + 16)
    if eng == "g":
        return 130 + 2 * CYCLE * n
    if form == "pack":
        return 12 + 0.88 * n
    if form == "scatter":
        return 50 + 3.8 * CYCLE * n
    if any(v[0] == "ind" for v in full):
        return (65 if eng == "a" else 50) + 1.56 * CYCLE * n
    if eng == "a":
        return 65 + CYCLE * n
    if form == "two":
        return CYCLE * max(64, n if any(v[0] == "ps" for v in full) else 2 * n)
    return CYCLE * max(64, n / 2 if all(PLACE[v[0]][3] in (BF, U16) for v in full) else n)


def octal(digits):
    n = sum(d << 3 * i for i, d in enumerate(digits))
    return n - (1 << 24) if n >= 1 << 23 else n


def rank_program(g, core, T, topo):
    rank = T.rank_of(core)
    if rank is None:
        relay_program(g, core, T, topo)
        return
    ops, queued = [], [0]
    queues = {"v": g.vector, "a": g.scalar, "t": g.tensor, "g": g, "s": g.sync}

    def ap(v):
        if not isinstance(v, tuple):
            return v
        if v[0] == "ind":
            return ap(v[1]).indirect(ap(v[2]))
        name, a, b, s = v
        buf, at = PLACE[name][:2]
        return T[buf][:, at + a:at + b] if s == 1 else T[buf][:, at + a:at + b:s]

    def regions(vs):
        out = []
        for v in vs:
            if isinstance(v, tuple):
                out += [v[1], v[2]] if v[0] == "ind" else [v]
        return out

    def add(eng, fn, writes, reads, kind="c", sem=None, form=None, lag=0.0):
        w, r = regions(writes), regions(reads)
        banks = [("ps", v[1] // 512 * 512, v[1] // 512 * 512 + 512, 1) for v in w + r if v[0] == "ps"]
        ops.append({"eng": eng, "fn": fn, "w": [v for v in w if v[0] != "ps"] + banks, "r": [v for v in r if v[0] != "ps"],
                    "kind": kind, "sem": sem, "len": length(eng, kind, form, writes, reads), "lag": lag})

    def cp(out, in_):
        add("v", lambda: g.vector.tensor_copy(ap(out), ap(in_)), [out], [in_])

    def scat(win, off, in_):
        add("v", lambda: g.vector.tensor_copy(ap(IND(win, off)), ap(in_)), [win], [off, in_], form="scatter")

    def tt(out, a, b, op):
        add("v", lambda: g.vector.tensor_tensor(ap(out), ap(a), ap(b), op), [out], [a, b], form="two")

    def ts(out, a, s1, op0, s2=None, op1=None):
        if op1 is None:
            add("v", lambda: g.vector.tensor_scalar(ap(out), ap(a), ap(s1), None, op0), [out], [a, s1])
        else:
            add("v", lambda: g.vector.tensor_scalar(ap(out), ap(a), ap(s1), ap(s2), op0, op1), [out], [a, s1, s2])

    def scan(out, d0, d1, init, op0, op1):
        add("v", lambda: g.vector.tensor_tensor_scan(ap(out), ap(d0), ap(d1), ap(init), op0, op1), [out], [d0, d1, init])

    def tr(out, in_):
        add("v", lambda: g.vector.transpose(ap(out), ap(in_)), [out], [in_])

    def ms(out, val):
        add("v", lambda: g.vector.memset(ap(out), val), [out], [])

    def quant(q, sc, in_, after=()):
        add("v", lambda: g.vector.quantize_mx(ap(q), ap(sc), ap(in_)), [q, sc], [in_] + list(after), form="pack")

    def act(out, in_, scale=None, bias=None, func=ACT.Identity):
        if bias is not None:
            add("a", lambda: g.scalar.activation(ap(out), ap(in_), func, bias=ap(bias), scale=1.0 if scale is None else ap(scale)),
                [out], [in_, bias, scale])
        elif scale is None:
            add("a", lambda: g.scalar.activation(ap(out), ap(in_), ACT.Copy), [out], [in_])
        else:
            add("a", lambda: g.scalar.activation(ap(out), ap(in_), ACT.Copy, scale=scale), [out], [in_])

    def mm(out, lq, ls, rq, rs):
        add("t", lambda: g.tensor.matmul_mx(ap(out), ap(lq), ap(ls), ap(rq), ap(rs), True, True), [out], [lq, ls, rq, rs])

    def iota(out, pattern, base=0, cm=0):
        small = PLACE[out[0]][3] != I32
        add("g", lambda: g.iota(ap(out), pattern, base, cm, allow_small_or_imprecise_dtypes=small), [out], [])

    def load(eng, out, src, as_codes=False, after=()):
        queued[0] = (0 if after else queued[0]) + count(out) * (4 if as_codes else 2)
        add(eng, lambda: queues[eng].dma_start(ap(out).bitcast(dt.uint8) if as_codes else ap(out), src), [out], list(after), kind="dma",
            lag=LOAD + BYTE * queued[0])

    def store(eng, dst, src_ap, reads):
        add(eng, lambda: queues[eng].dma_start(dst, src_ap), [], reads, kind="out", lag=LOAD)

    sent = [0]

    def remote(rnd, kinds, name=None):
        dst, writes = partner_of(T, rank, rnd), []
        for kind in kinds:
            src, land, sem, there, came = names_of(kind, rnd)
            for to, mask, a, b in pieces(topo, core, dst, kind):
                sent[0] += engines_in(mask)
                writes.append((to, land if to == dst else there, name or src, sem if to == dst else came, mask, a, b))
        add("g", lambda: send(g, T, topo, core, writes), [], [V(w[2]) for w in writes], kind="remote")

    def arrival(rnd, kinds):
        src = partner_of(T, rank, rnd)
        n = sum(engines_in(topo.mask(src if to == core else to, core)) for k in kinds for to, _, _, _ in pieces(topo, src, core, k))
        hops = 1 if topo.may_write(src, core) else TWO
        add(None, None, [V(names_of(k, rnd)[1]) for k in kinds], [], kind="arrive", sem=(names_of(kinds[0], rnd)[2], n),
            lag=hops * HOP[kinds])

    cols = {}

    def col(name):
        i = cols.setdefault(name, len(cols))
        return V("col", i, i + 1)

    def tab(name):
        i = list(TABLES).index(name)
        return V("tab", i, i + 1)

    def lst(name, a=0, n=None):
        at, all_ = LISTS[name]
        return V("lst", at + a, at + a + (all_ - a if n is None else n))

    def weave(*parts):
        chains = []
        for part in parts:
            at = len(ops)
            part()
            chains.append(ops[at:])
            del ops[at:]
        for i in range(max(len(c) for c in chains)):
            ops.extend(c[i] for c in chains if i < len(c))

    left = [rank & (1 << rnd) == 0 for rnd in range(NR)]
    ROW_EI, ROW_IN, ROW_8, ROW_16, ROW_POS, ROW_32 = [V("rows", a, b) for a, b in [(0, 16), (16, 20), (20, 24), (24, 28), (32, 48), (48, 50)]]
    FIELDS = {"r": (0, 15), "pair": (1, 7), "s": (0, 7), "r8": (3, 1), "c": (0, 31), "hi": (2, 3), "lo": (0, 3),
              "b0": (0, 1), "b1": (1, 1), "b2": (2, 1)}
    for name in FIELDS:
        col(name)

    def fields(a, b):
        for i, (sh, m) in list(enumerate(FIELDS.values()))[a:b]:
            ts(V("coli", i, i + 1), V("pidx"), sh, A.logical_shift_right, m, A.bitwise_and)
        cp(V("col", a, b), V("coli", a, b))

    load("s", V("pin"), T.p[:])
    load("a", V("hin"), T.h[:])
    load("a", V("ut"), T.u[:])
    for a, b in PARTS:
        load("s", V("x0", 4 * a, 4 * b), T.x[:, 4 * a:4 * b])

    iota(V("pidx"), [[1, 1]], 0, 1)
    iota(V("c16"), [[16, 28]])
    iota(V("irl", 0, 128), [[1, 128]])
    for a in (128, 256):
        act(V("irl", a, a + 128), V("irl", 0, 128), bias=float(a))
    ms(V("k16"), 1.0)
    ms(V("wl", 24, 32), 0.0)
    fields(0, 10)
    ms(V("k16", 0, NP, 16), 0.0)
    ms(V("cc"), 0.0)
    ms(V("fsn", NP, 288), 0.0)
    cp(lst("up"), V("c16", 0, 8))
    ts(col("16c"), col("c"), 16.0, A.mult)

    def block_rows():
        iota(ROW_EI, [[8, 4], [0, 4]])
        ts(lst("ei"), ROW_EI, col("s"), A.add)
        if not all(left):
            iota(V("blk"), [[0, 2], [8, 2], [0, 8]])
            ms(V("ones"), 1.0)
            act(V("blk"), V("blk"), bias=col("16c"))
        iota(V("kk"), [[0, 4], [1, 8], [0, 8]])

    if not left[0]:
        block_rows()
    iota(V("j16"), [[0, 14], [1, 16]])
    iota(V("t9"), [[0, 25], [1, SEG]], -1)
    ts(V("dm"), V("j16"), col("r"), A.is_equal)

    def pair_lists():
        j, e = V("tmp", 0, 14), V("tmp", 16, 30)
        ts(j, V("c16", 0, 14), col("r"), A.add)
        ts(V("cq"), j, -4.0, A.add, 1.0 / SEG, A.mult)
        tt(e, j, V("cq"), A.subtract)
        ts(j, e, 2.0, A.mult, -2.0, A.add)
        ts(lst("pl", 0, 14), j, C - 2.0, A.min)
        ts(lst("pl", 14, 14), j, C - 2.0, A.min, 1.0, A.add)

    def right_mask_consts():
        act(col("4r8-128"), col("r8"), 4.0 * FAR, -128.0 * FAR)
        act(V("far"), V("t9", 1, SEG), -FAR, col("4r8-128"))
        act(V("maskr", 0, NP, SEG), V("t9", 0, NP, SEG), BIG)

    def left_mask():
        ts(V("maskl"), V("t9", 0, NP), col("pair"), A.not_equal, BIG, A.mult)
        act(V("maskl", 0, NP, SEG), V("t9", 0, NP, SEG), BIG)

    def inverse():
        tt(V("wr"), V("wt"), V("blk"), A.subtract)
        tt(V("nm"), IND(V("wr"), lst("ei")), V("kk"), A.not_equal)
        scan(V("iv"), V("nm"), V("ones"), 0.0, A.mult, A.add)

    def left_change(ev, ed):
        ts(ev, V("wt"), col("16c"), A.subtract, 0.0625, A.mult)
        tt(V(ed[0], 0, 32, 2), V(ev[0], 1, 32, 2), V(ev[0], 0, 32, 2), A.subtract)
        tt(V(ed[0], 1, 32, 2), V(ev[0], 0, 32, 2), V(ev[0], 1, 32, 2), A.subtract)

    def right_change(iv, ev, ed):
        act(V("pb"), iv, -0.5, 131.75)
        act(V("v8"), iv, 0.125)
        act(V("e1"), V("pb"), -0.25, 527.0 / 16)
        if ev:
            act(ev, iv, 0.0625)
        tt(ed, V("e1"), V("v8"), A.subtract)

    def right_mask():
        for t in range(1, SEG):
            out = V("maskr", t, NP, SEG)
            act(out, V("pb", 0, count(out)), FAR, V("far", t - 1, t), ACT.Square)

    def score_lists():
        for a in (NP, 0):
            tt(V("ext", a, a + NP), IND(V("hw"), lst("pl", a // 16, 14)), V("dm"), A.mult)
        for a in (NP, 0):
            scan(V("exs", a, a + NP), V("k16"), V("ext", a, a + NP), 0.0, A.mult, A.add)
        cp(V("lab"), V("exs", 15, 2 * NP, 16))

    def product(x, i, last):
        a, b = (HALVES if last else PARTS)[i]
        bank = 2048 + 512 * i
        quant(V("xq", a, b), V("xsc", a, b), V(x, 4 * a, 4 * b))
        mm(V("ps", bank, bank + b - a), V("vq" if last else "uq2"), V("vs" if last else "us2"), V("xq", a, b), V("xsc", a, b))

    def fetch(i, last, eng="a"):
        a, b = (HALVES if last else PARTS)[i]
        bank = 2048 + 512 * i
        (act if eng == "a" else cp)(V("yo" if last else "s", a, b), V("ps", bank, bank + b - a))

    def tables():
        for i in range(3):
            act(col("w%d" % i), col("b%d" % i), 8.0 ** -(1 << i) - 1.0, 1.0)
        for i, t in enumerate(TABLES.values()):
            lo, hi = octal(t[:8]), octal(t[-8:])
            act(V("tabn", i, i + 1), col("r8"), float(hi - lo), float(lo))
        ts(col("w"), col("w0"), col("w1"), A.mult, col("w2"), A.mult)
        ts(col("half"), col("w"), -0.5, A.mult, 0.5, A.add)
        n = len(TABLES)
        ts(V("tabi", 0, n), V("tabn", 0, n), col("w"), A.mult, col("half"), A.subtract)
        ts(V("taba", 0, n), V("tabi", 0, n), 7, A.bitwise_and)
        cp(V("tab", 0, n), V("taba", 0, n))

    def lead_lists():
        for out, by in [(lst("u", 0, 4), "link"), (lst("u", 4, 4), "direct"), (lst("v", 0, 4), "to"), (lst("v", 4, 4), "to")]:
            ts(out, ROW_IN, tab(by), A.add, col("8r8"), A.add)
        ts(lst("u", 8), ROW_8, col("lo"), A.add)
        ts(lst("v", 8), ROW_8, col("hi"), A.add, 4.0, A.add)

    def meet_lists():
        for name, src, scale, bias in [
                ("rank", col("lo"), 4.0, 3.0), ("turn", col("lo"), 4.0, col("hi")), ("topr", tab("by"), 4.0, 3.0),
                ("topl", tab("by"), -4.0, 15.0), ("cell", tab("data"), -48.0, 51.0), ("end", tab("end2"), 2.0, tab("end1")),
                ("addr", tab("addr"), 4.0, col("cell")), ("addl", tab("addl"), 4.0, col("cell")), ("pos", col("b2"), 64.0, col("end")),
                ("mv", col("r8"), 16.0, col("pos")), ("399+r", col("r"), 1.0, 399.0), ("160+r", col("r"), 1.0, float(TS)),
                ("-16c", col("c"), -16.0, -400.0), ("dex0", col("c"), 16.0, -1000.0), ("dex1", col("c"), 16.0, -992.0)]:
            act(col(name), src, scale, bias)
        for name, row, scale, bias in [
                ("pg", ROW_8, 1.0, tab("count")), ("rank", ROW_16, 1.0, col("rank")), ("turn", ROW_16, 1.0, col("turn")),
                ("relr", ROW_8, 1.0, tab("relr")), ("rell", ROW_8, 1.0, tab("rell")),
                ("addr", ROW_16, tab("data"), col("addr")), ("addl", ROW_16, tab("data"), col("addl")),
                ("topr", ROW_16, 1.0, col("topr")), ("topl", ROW_16, 1.0, col("topl")),
                ("pos", ROW_POS, 1.0, col("pos")), ("mv", ROW_32, 1.0, col("mv")), ("tot", ROW_16[:2] + (26, 1), 1.0, 15.0)]:
            act(("lsf",) + lst(name)[1:], row, scale, bias)
        for a, b in [("pg", "addl"), ("topr", "tot")]:
            at, end = lst(a)[1], lst(b)[2]
            cp(V("lst", at, end), V("lsf", at, end))
        act(V("k160"), V("c16", 0, 24), bias=col("160+r"))
        act(V("base", 0, 1), col("399+r"))

    def meet_rows():
        iota(V("ag", 32, 40), [[0, 8]])
        ms(V("fone"), 0.0)
        ms(V("fone", 64 + 7, 128, 8), 2.0)
        iota(V("cg"), [[0, 4], [-1, 2], [0, 8]], 1)
        for i in range(16):
            if (i in NEGATED) != (i < 8):
                iota(V("cg", i, 64, 16), [[0, 4]], int(i in NEGATED))
        iota(V("kp"), [[0, 128]], 1)
        iota(V("kp", 0, 128, 4), [[0, 32]])
        for at, reset in [(64, 64), (144, -64)]:
            iota(V("ps2", at, at + 16), [[0, 2], [reset, 2], [0, 4]])
        iota(V("k4"), [[0, 64]], 1)
        iota(V("k4", 0, 64, 4), [[0, 16]])
        iota(V("kbig"), [[0, 64]])
        iota(V("kbig", 0, 64, 4), [[0, 16]], 64)
        iota(V("k2"), [[0, 4], [1, 8]])
        iota(V("six"), [[0, 24]], 16)
        iota(V("ew", 0, TS), [[0, TS]], C - 1)

    def unpack_consts():
        iota(V("e0"), [[0, 512]], 16)
        for b in range(4):
            out = V("et", 512 * b, 512 * b + 512)
            add("g", lambda out=out, b=b: g.affine_select(ap(out), ap(V("e0")), [[-4, 128], [-1, 4]], A.is_equal, 0.0, b, 4),
                [out], [V("e0")])

    def spread_u():
        quant(V("uq"), V("us"), V("ut"))
        add("v", lambda: g.vector.tensor_copy(T.uq2[:].bitcast(dt.uint32), T.uq[:].bitcast(dt.uint32).indirect(ap(lst("up")))),
            [V("uq2")], [V("uq"), lst("up")])
        act(V("us2"), IND(V("us"), lst("up")))

    cp(V("h16"), V("hin"))
    cp(V("w16"), V("pin"))
    cp(V("wl", 0, 24), V("pin"))
    act(V("hrl"), IND(V("irl"), V("h16")))
    act(V("hw"), IND(V("hrl"), V("w16")))
    tr(V("wt"), V("wl"))
    if left[0]:
        weave(lambda: left_change(V("ev0"), V("ed")), pair_lists)
        remote(0, "e")
        tr(V("cc", 0, 288, SEG), V("ed"))
    else:
        weave(inverse, pair_lists)
        act(V("ev0"), V("iv", 7, 256, 8), 0.0625)
        remote(0, "e")
        right_mask_consts()
        tr(V("vl"), V("iv", 7, 256, 8))
        right_change(V("vl"), None, V("cc", 0, 288, SEG))
    arrival(0, "e")
    spread_u()
    tables()
    weave(score_lists, lambda: [product("x0", i, False) for i in range(2)])
    (left_mask if left[0] else right_mask)()
    fetch(0, False)
    fetch(1, False, "v")
    iota(ROW_IN, [[4, 2], [16, 2]])
    iota(ROW_8, [[8, 4]])
    iota(ROW_16, [[16, 4]])
    iota(ROW_POS, [[16, 4], [0, 4]])
    iota(ROW_32, [[32, 2]])
    if left[0]:
        block_rows()
    act(col("8r8"), col("r8"), 8.0)

    def scaled(eng, out, src, by):
        if eng == "a":
            act(out, src, by)
        else:
            ts(out, src, by, A.mult)

    for rnd in range(NR):
        last = rnd + 1 == NR
        q = V("qt%d" % rnd)
        def scores(a, b):
            return IND(V("s"), V("lab", a // 16, b // 16))

        for a, b in ((0, 128), (128, NP)):
            tt(V("sb", a, b), scores(NP + a, NP + b), V("maskl" if left[rnd] else "maskr", a, b), A.add)
        for a, b in ((0, 128), (128, NP)):
            tt(V("fl", a, b), scores(a, b), V("sb", a, b), A.is_lt)
        for a, b in ((0, 14 * SEG), (14 * SEG, NP)):
            scan(V("fsn", a, b), V("fl", a, b), V("cc", a, b), 0.0, A.mult, A.add)
        if rnd == 0:
            tr(V("ft0"), V("fsn", SEG - 1, 288, SEG))
            remote(rnd, "w", "ft0")
            meet_rows()
            for t in range(4):
                ts(V("xh16", 24 * t, 24 * t + 24), V("hin"), 4.0, A.mult, float(t), A.add)
            if not all(left):
                act(V("nk"), V("kk"), -0.0625, 0.5)
                ms(V("k8"), 1.0)
                ms(V("k8", 0, 256, 8), 0.0)
            tt(q, V("ft0"), V("ev0"), A.add)
            lead_lists()
        else:
            tr(q, V("fsn", SEG - 1, 288, SEG))
            remote(rnd, "w")
        for i in range(8):
            act(V("xh", H * i, H * i + H), IND(V("xs" if rnd else "x0"), V("xh16", 12 * i, 12 * i + 12)))

        def own_half():
            tt(V("oa"), IND(q, lst("u")), V("fone"), A.add)
            tt(V("own"), IND(q, lst("v")), V("oa"), A.is_lt)

        def word_half():
            if left[rnd]:
                ts(V("ag", 0, 32), q, 16.0, A.mult, col("16c"), A.add)
                tt(V("adf"), V("ag", 0, 32), V("ag", 1, 33), A.subtract)
                cp(V("adf", 7, 32, 8), V("ag", 7, 32, 8))
                act(V("dex"), IND(V("adf"), lst("ei")))
            else:
                for a in (0, 128):
                    tt(V("nm", a, a + 128), IND(q, lst("ei", a // 16, 8)), V("nk", a, a + 128), A.is_equal)
                for bk in range(4):
                    act(V("dex", 64 * bk, 64 * bk + 64), V("nm", 64 * bk, 64 * bk + 64), 1000.0, col("dex%d" % (bk % 2)))

        if rnd == 0:
            weave(own_half, meet_lists)
            act(V("negk"), V("j16", 0, 32), -1.0, col("-16c"))
            act(V("cbig"), V("dm", 0, TS), 1000.0)
            word_half()
        else:
            weave(own_half, word_half)
        pw = V("pw%d" % rnd)
        arrival(rnd, "w")
        if rnd == 0:
            load("s", V("wq"), T.wc[:], as_codes=True, after=[pw])
            load("s", V("wsc"), T.ws[:], after=[pw])
            unpack_consts()
            tt(V("pq"), pw, V("pev"), A.add)
            pw = V("pq")
        tt(V("pu", 0, 128), IND(pw, lst("u", 0, 8)), V("own", 0, 128), A.add)
        tt(V("pu", 128, 192), IND(pw, lst("u", 8)), V("own", 128, 192), A.add)
        tt(V("lead", 0, 128), IND(pw, lst("v", 0, 8)), V("pu", 0, 128), A.is_lt)
        tt(V("lead", 128, 192), IND(pw, lst("v", 8)), V("pu", 128, 192), A.is_lt)
        scan(V("rr"), V("lead", 0, 64), V("lead", 64, 128), 0.0, A.mult, A.max)
        for at in (1, 13):
            act(V("kp", at, 128, 16), V("rr", 5, 64, 8), -1.0, 1.0)
        act(V("lm"), V("lead", 128, 192), 8.0, -7.0)
        act(V("nl"), IND(V("lead", 128, 192), lst("turn")), -4.0, 4.0)
        act(V("rl", 64, 128), IND(V("rr", 32, 64), lst("relr")))
        act(V("rl", 0, 64), IND(V("rr", 0, 32), lst("rell")), -4.0, 4.0)
        for hf in range(2):
            tt(V("pg", 64 * hf, 64 * hf + 64), IND(V("rr", 32 * hf, 32 * hf + 32), lst("pg")), V("cg"), A.not_equal)
        for hf in range(2):
            scan(V("ps2", 80 * hf, 80 * hf + 64), V("kp", 64 * hf, 64 * hf + 64), V("pg", 64 * hf, 64 * hf + 64), 0.0, A.mult, A.add)
        act(V("d1", 64, 128), IND(V("ps2", 80, 160), lst("addr")))
        act(V("d1", 0, 64), IND(V("ps2", 0, 80), lst("addl")))
        tt(V("tn", 0, 64), IND(V("ps2", 0, 64), lst("rank")), V("lm"), A.add)
        tt(V("tn", 64, 128), IND(V("ps2", 80, 144), lst("rank")), V("nl"), A.max)
        scan(V("tb", 0, 64), V("k4"), V("tn", 0, 64), 0.0, A.mult, A.max)
        scan(V("tb", 64, 128), V("kbig"), V("tn", 64, 128), 0.0, A.add, A.min)
        tt(V("fin", 64, 128), IND(V("tb", 0, 64), lst("topr")), V("rl", 64, 128), A.mult)
        tt(V("fin", 0, 64), IND(V("tb", 64, 128), lst("topl")), V("rl", 0, 64), A.max)
        scan(V("fs", 64, 128), V("fin", 64, 128), V("d1", 64, 128), 0.0, A.max, A.add)
        scan(V("fs", 0, 64), V("fin", 0, 64), V("d1", 0, 64), 64.0, A.min, A.add)

        def match(hf):
            a, b = 128 * hf, 128 * hf + 128
            at = IND(V("fs"), lst("pos", 8 * hf, 8))
            if left[rnd]:
                tt(V("nm", a, b), at, V("kk", a, b), A.not_equal)
            else:
                tt(V("t11", a, b), at, V("dex", a, b), A.add)

        def new_word(hf):
            a, b = 128 * hf, 128 * hf + 128
            if left[rnd]:
                scan(V("nw", a, b), V("nm", a, b), V("dex", a, b), 0.0, A.mult, A.add)
            else:
                scan(V("nw", a, b), V("k8", a, b), V("t11", a, b), 0.0, A.mult, A.max)

        match(0)
        match(1)
        tt(V("mv"), IND(V("fs"), lst("mv")), V("k2"), A.not_equal)
        new_word(0)
        new_word(1)
        scan(V("pp"), V("k16", 0, 32), V("mv"), 0.0, A.mult, A.add)
        tt(V("uu"), V("mv"), V("negk"), A.mult)
        tr(V("wl"), V("nw", 7, 256, 8))
        act(V("tp", 32, 64), IND(V("pp"), lst("tot")))
        tt(V("tp", 0, 32), V("pp"), V("uu"), A.add)
        cp(V("w16"), V("wl", 0, 24))
        act(V("wt"), V("nw", 7, 256, 8))
        if last:
            load("s", V("vt"), T.v[:], after=[V("wt")])
            for gr in range(8):
                a, y = gr // 2, gr % 2
                store("s", T.op[gr:gr + 1, :], T.wf[32 * a:32 * a + 24, PLACE["wt"][1] + 16 * y:PLACE["wt"][1] + 16 * y + 16], [V("wt")])
        for lo, hi in HALVES:
            for b in range(4):
                act(V("z", 4 * lo + b, 4 * hi, 4), IND(V("xh", C * b, C * b + C), V("w16", lo // 16, hi // 16)))
        tr(V("tpt"), V("tp"))
        scan(V("base", 1, 24), V("tpt", 32, 55), V("six", 0, 23), col("399+r"), A.add, A.add)
        tt(V("sl"), V("base"), V("tpt", 0, 24), A.add)
        cp(V("sl16"), V("sl"))
        scat(V("ew"), V("sl16"), V("irl"))

        def layer(hf):
            lo, hi = HALVES[hf]
            quant(V("zq", lo, hi), V("zs", lo, hi), V("z", 4 * lo, 4 * hi))
            for b in range(4):
                bank = 512 * (2 * b + hf)
                mm(V("ps", bank, bank + H), V("wq", 128 * b, 128 * b + 128), V("wsc", 128 * b, 128 * b + 128), V("zq", lo, hi), V("zs", lo, hi))

        layer(0)
        scan(V("esn"), V("cbig"), V("ew", 0, TS), 0.0, A.add, A.min)
        ts(V("z32", 0, 4 * H), V("z", 0, 4 * H), 32.0, A.mult)
        cp(V("e16"), V("esn", 15, TS, 16))
        for b in range(4):
            act(V("z32", 4 * H + b, 4 * C, 4), V("z", 4 * H + b, 4 * C, 4), 32.0)
        layer(1)
        for b, hf in [(0, 0), (1, 0), (0, 1), (1, 1), (2, 0), (2, 1), (3, 0), (3, 1)]:
            (lo, hi), bank, at = HALVES[hf], 512 * (2 * b + hf), YW * b + TS
            tt(V("ym", at + lo, at + hi), V("ps", bank, bank + H), V("z32", 4 * lo + b, 4 * hi, 4), A.add)
        for eng, b, lo, hi in [("a", 0, 0, 10), ("a", 1, 0, 10), ("a", 2, 0, 10), ("v", 3, 0, 6), ("a", 3, 6, 10)]:
            scaled(eng, V("f", 64 * lo + b, 64 * hi, 4), IND(V("ym", YW * b + TS, YW * b + YW), V("e16", lo, hi)), 0.03125)
        quant(V("fq%d" % rnd), V("fs%d" % rnd), V("f"))
        remote(rnd, "q")
        remote(rnd, "s")
        if not last:
            act(V("hw"), IND(V("hrl"), V("w16")))
            iota(V("ew", 0, TS), [[0, TS]], C - 1)
        act(V("f16"), V("f"), 16.0)

        def slots():
            ts(V("i1"), V("sl"), float(TS), A.is_ge, 1000.0, A.mult)
            tt(V("i2"), V("i1"), V("sl"), A.add)
            tt(V("i3"), V("i2"), V("k160"), A.min)
            cp(V("idx"), V("i3"))

        if rnd == 0:
            if left[0] and not all(left):
                right_mask_consts()
            if any(left) and not left[0]:
                left_mask()
        if last:
            weave(slots, lambda: quant(V("vq"), V("vs"), V("vt")))
        elif left[rnd + 1]:
            weave(slots, lambda: left_change(V("ev"), V("ed")))
            tr(V("cc", SEG - 1, 288, SEG), V("ev"))
            tr(V("cc", 0, 288, SEG), V("ed"))
            score_lists()
        else:
            weave(slots, inverse)
            tr(V("vl"), V("iv", 7, 256, 8))
            right_change(V("vl"), V("cc", SEG - 1, 288, SEG), V("cc", 0, 288, SEG))
            weave(score_lists, right_mask)
        if rnd == 0:
            for b in range(4):
                quant(V("eq", 128 * b, 128 * b + 128), V("es", 128 * b, 128 * b + 128), V("et", 512 * b, 512 * b + 512), [V("fs0")])
        arrival(rnd, "qs")
        for b in (0, 3, 1, 2):
            mm(V("ps", 512 * b, 512 * b + TS), V("eq", 128 * b, 128 * b + 128), V("es", 128 * b, 128 * b + 128),
               V("lq%d" % rnd), V("ls%d" % rnd))
        for b in (0, 3, 1, 2):
            tt(V("ym", YW * b, YW * b + TS), V("ps", 512 * b, 512 * b + TS), V("f16", b, 4 * TS, 4), A.add)
        parts = HALVES if last else PARTS
        for i, (a, b) in enumerate(parts):
            for pl in (0, 1, 3, 2):
                scaled(PICKS[i][pl], V("xs", 4 * a + pl, 4 * b, 4), IND(V("ym", YW * pl, YW * pl + YW), V("idx", a // 16, b // 16)), 0.03125)
            product("xs", i, last)
            if last:
                store("s", T.oc[:, 4 * a:4 * b], T.xq[:, a:b].bitcast(dt.uint8), [V("xq", a, b)])
        for i, (a, b) in enumerate(parts):
            fetch(i, last, "v" if last else "av"[i])
            if last:
                store("as"[i % 2], T.y[:, a:b], T.yo[:, a:b], [V("yo", a, b)])

    for k in range(4):
        store("a", T.osc[4 * k:4 * k + 4, :], T.xsc[32 * k:32 * k + 4, :], [V("xsc")])

    emit(g, T, ops, queues, sent[0])


def touching(ops):
    cache = {}

    def cols(v):
        if v not in cache:
            cache[v] = sum(1 << i for i in range(v[1], v[2], v[3]))
        return cache[v]

    hist, out = {}, []
    for i, op in enumerate(ops):
        deps = set()
        for v in op["w"]:
            deps |= {j for j, m, wr in hist.get(v[0], []) if m & cols(v)}
        for v in op["r"]:
            deps |= {j for j, m, wr in hist.get(v[0], []) if wr and m & cols(v)}
        for v in op["w"]:
            hist[v[0]] = [(j, m & ~cols(v), wr) for j, m, wr in hist.get(v[0], []) if m & ~cols(v)] + [(i, cols(v), True)]
        for v in op["r"]:
            hist.setdefault(v[0], []).append((i, cols(v), False))
        deps.discard(i)
        out.append(deps)
    return out


def arrange(ops):
    deps, kept = touching(ops), {}
    remote = own = None
    issued = {}
    for i, op in enumerate(ops):
        if op["kind"] == "arrive":
            deps[i].add(remote)
        if op["kind"] == "remote":
            remote = i
        if op["eng"] == "g":
            kept[i], own = own, i
        if op["kind"] == "dma":
            issued[i] = max(issued, default=None)
    for i, j in kept.items():
        deps[i] |= {j} - {None}
    after = [[] for _ in ops]
    for i, d in enumerate(deps):
        for j in d:
            after[j].append(i)

    def place(order, before, forward):
        busy, span = {}, {}
        for i in order:
            op = ops[i]
            t = max([span[j][1] + (0.0 if j == kept.get(i) or i == kept.get(j) else WAKE) for j in before[i]], default=0.0)
            t += 0.0 if forward else op["lag"]
            if forward and issued.get(i) in span:
                t = max(t, span[issued[i]][0])
            taken = busy.setdefault(op["eng"], [])
            at = 0
            for a, b in taken if op["eng"] else []:
                if t + op["len"] <= a:
                    break
                t, at = max(t, b), at + 1
            taken.insert(at, (t, t + op["len"]))
            span[i] = (t, t + op["len"] + (op["lag"] if forward else 0.0))
        return span

    order, best = list(range(len(ops))), None
    for _ in range(PASSES):
        span = place(order, deps, True)
        end = max(b for _, b in span.values())
        if best is None or end < best[0]:
            best = (end, sorted(span, key=lambda i: (span[i][0], order.index(i))))
        back = place(sorted(span, key=lambda i: (-span[i][1], -span[i][0], -i)), after, False)
        order = sorted(back, key=lambda i: (-back[i][1], -back[i][0], i))
        first = [i for i in issued if not deps[i]]
        order = first + [i for i in order if i not in first]
    return [ops[i] for i in best[1]]


def emit(g, T, ops, queues, sent):
    ops = arrange(ops)
    known = {e: set() for e in queues}
    at_issue, waits = [], []
    for op, deps in zip(ops, touching(ops)):
        mine = []
        if op["eng"] is not None:
            kn = known[op["eng"]]
            for j in sorted(deps, reverse=True):
                if j not in kn:
                    mine.append(j)
                    kn.add(j)
                    kn |= at_issue[j]
            at_issue.append(set(kn))
        else:
            at_issue.append(set())
        waits.append(mine[::-1])
    needed = {j for w in waits for j in w}
    signal, used = {}, {e: [] for e in POOL}
    outs = 0
    for i, op in enumerate(ops):
        if op["kind"] == "arrive":
            signal[i] = op["sem"]
            continue
        queue = queues[op["eng"]]
        pool = "dma" if op["kind"] == "dma" else op["eng"]
        if i in needed:
            n = len(used[pool])
            if n >= POOL[pool] and used[pool][n - POOL[pool]] not in at_issue[i]:
                waits[i] = waits[i] + [used[pool][n - POOL[pool]]]
            step = 16 if pool == "dma" else 1
            signal[i] = ("%s%d" % (pool, n % POOL[pool]), step * (n // POOL[pool] + 1))
            used[pool].append(i)
        for j in waits[i]:
            queue.wait_ge(T.sem[signal[j][0]], signal[j][1])
        ins = op["fn"]()
        if op["kind"] == "out":
            ins.then_inc(T.sem["outs"], 16)
            outs += 16
        elif i in needed:
            ins.then_inc(T.sem[signal[i][0]], 16 if pool == "dma" else 1)
    g.wait_ge(T.sem["sent"], sent)
    g.sync.wait_ge(T.sem["outs"], outs)
